import numpy as np
import ml_dtypes


def mxq(x, axis, fmt="e4m3"):
    dtype, down = {"e4m3": (ml_dtypes.float8_e4m3fn, 7), "e5m2": (ml_dtypes.float8_e5m2, 14)}[fmt]
    v = np.moveaxis(np.asarray(x, np.float32).astype(ml_dtypes.bfloat16).astype(np.float64), axis, -1)
    blocks = v.reshape(v.shape[:-1] + (-1, 32))
    amax = np.abs(blocks).max(-1, keepdims=True)
    byte = np.maximum(np.where(amax > 0, np.frexp(amax)[1] - 1 + 127, 0) - down, 1)
    scale = np.exp2(byte - 127.0)
    codes = (blocks / scale).astype(np.float32).astype(dtype).astype(np.float64)
    return np.moveaxis((codes * scale).reshape(v.shape), -1, axis)


WIDE = False


def mx_kscale(k):
    if not WIDE:
        return np.ones(k)
    levels = np.array([24, -24, 12, -12, 0])
    if k % 512:
        return np.exp2(np.random.permutation(np.resize(levels, k // 32))).repeat(32)
    a = np.empty((k // 512, 16))
    for p in range(k // 512):
        a[p, :8] = np.random.permutation(np.resize(levels, 8))
        for g in range(8):
            far = levels[np.abs(levels - a[p, g]) >= 10]
            a[p, g + 8] = far[np.random.randint(len(far))]
    return np.exp2(a.ravel()).repeat(32)


def f64(x):
    return np.asarray(x).astype(np.float64)


def striped(idx):
    return np.tile(idx.reshape(-1, 16).T, (8, 1)).astype(np.uint16)


def unstriped(offs):
    return offs[:16].T.reshape(-1).astype(np.int64)


E2M1 = np.array([0.0, 0.5, 1.0, 1.5, 2.0, 3.0, 4.0, 6.0, -0.0, -0.5, -1.0, -1.5, -2.0, -3.0, -4.0, -6.0])


def pack_weight(w, fmt):
    k, n = w.shape
    w = f64(np.asarray(w, np.float32).astype(ml_dtypes.bfloat16)).reshape(k // 32, 32, n)
    amax = np.abs(w).max(1)
    if fmt == "e4m3":
        byte = np.frexp(amax)[1] - 1 + 127 - 7
    else:
        mant, ex = np.frexp(amax / 6.0)
        byte = np.where(mant > 0.5, ex, ex - 1) + 127
    byte = np.clip(np.where(amax > 0, byte, 1), 1, 254)
    scaled = (w * np.exp2(127.0 - byte)[:, None, :]).reshape(k, n).astype(np.float32)
    by_word = np.ascontiguousarray(scaled.reshape(k // 512, 128, 4, n).transpose(0, 1, 3, 2))
    if fmt == "e4m3":
        words = by_word.astype(ml_dtypes.float8_e4m3fn).view(np.uint8)
    else:
        c = by_word.astype(ml_dtypes.float4_e2m1fn).view(np.uint8) & 0xF
        words = (c[..., 0::2] | (c[..., 1::2] << 4)).reshape(k // 512, 128, 2 * n)
    return np.ascontiguousarray(words), np.ascontiguousarray(byte.astype(np.uint8).reshape(k // 512, 16, n))


def unpack_weight(words, scales, fmt):
    g, _, n = scales.shape
    words = np.ascontiguousarray(words).reshape(g, 128, n, -1)
    if fmt == "e4m3":
        vals = words.view(ml_dtypes.float8_e4m3fn).astype(np.float64)
    else:
        nib = np.empty((g, 128, n, 4), np.uint8)
        nib[..., 0::2] = words & 0xF
        nib[..., 1::2] = words >> 4
        vals = E2M1[nib]
    vals = vals * np.repeat(np.exp2(scales.astype(np.float64) - 127.0), 8, axis=1)[..., None]
    return vals.transpose(0, 1, 3, 2).reshape(g * 512, n)


def pack_table4(v):
    words, scales = pack_weight(v, "e2m1")
    g, t = words.shape[0] // 2, v.shape[1]
    return np.ascontiguousarray(words.reshape(g, 2, 128, t, 2).transpose(0, 2, 3, 1, 4).reshape(g, 128, t, 4)), scales


def unpack_table4(words, scales):
    g, _, t, _ = words.shape
    return unpack_weight(words.reshape(g, 128, t, 2, 2).transpose(0, 3, 1, 2, 4).reshape(2 * g, 128, 2 * t), scales, "e2m1")


def sigm(f):
    return 1.0 / (1.0 + np.exp(-np.maximum(f, -700.0)))


K, L, R, N, T, J = 512, 1024, 512, 512, 2048, 1024


def setup_inputs():
    n = np.random.standard_normal
    s = mx_kscale(K)[:, None]
    s2 = mx_kscale(L)[:, None]
    u = mx_kscale(R)[:, None]
    p_tab = pack_weight(n((K, T)) * s, "e4m3")
    p_tab2 = pack_table4(n((L, T)) * s2)
    p_nr = pack_weight(n((R, N)) / np.sqrt(R) / u, "e2m1")
    p_ni = pack_weight(n((R, N)) / np.sqrt(R) / u, "e2m1")
    return {
        "tab_words": p_tab[0],
        "tab_scales": p_tab[1],
        "tab2_words": p_tab2[0],
        "tab2_scales": p_tab2[1],
        "wer": (n((K, R)) / np.sqrt(K) / s * u.T).astype(np.float32),
        "wei": (n((K, R)) / np.sqrt(K) / s * u.T).astype(np.float32),
        "wrr": (n((L, R)) / np.sqrt(L) / s2).astype(np.float32),
        "wri": (n((L, R)) / np.sqrt(L) / s2).astype(np.float32),
        "nr_words": p_nr[0],
        "nr_scales": p_nr[1],
        "ni_words": p_ni[0],
        "ni_scales": p_ni[1],
        "offs": striped(np.random.permutation(T)[:J]),
        "offs2": striped(np.random.permutation(T)[:J]),
    }


def reference(tab_words, tab_scales, tab2_words, tab2_scales, wer, wei, wrr, wri, nr_words, nr_scales, ni_words, ni_scales, offs, offs2):
    idx = unstriped(offs)
    idx2 = unstriped(offs2)
    tab_ = unpack_weight(tab_words, tab_scales, "e4m3")[:, idx]
    tab2_ = unpack_table4(tab2_words, tab2_scales)[:, idx2]
    wer_ = mxq(f64(wer), 0, "e4m3")
    aer = wer_.T @ tab_
    wei_ = mxq(f64(wei), 0, "e4m3")
    aei = wei_.T @ tab_
    wrr_ = mxq(f64(wrr), 0, "e4m3")
    arr = wrr_.T @ tab2_
    wri_ = mxq(f64(wri), 0, "e4m3")
    ari = wri_.T @ tab2_
    hr = aer * arr - aei * ari
    hi = aer * ari + aei * arr
    hr_ = mxq(hr, 0, "e4m3")
    hi_ = mxq(hi, 0, "e4m3")
    nr_ = unpack_weight(nr_words, nr_scales, "e2m1")
    ni_ = unpack_weight(ni_words, ni_scales, "e2m1")
    y = nr_.T @ hr_ + ni_.T @ hi_
    return sigm(y)

@@ -1,0 +1,189 @@
+from contextlib import ExitStack
+
+import concourse.mybir as mybir
+
+K, L, R, N, T, J = 512, 1024, 512, 512, 2048, 1024
+FLOPS = 2 * J * (2 * K * R + 2 * L * R + 2 * R * N)
+
+F32 = mybir.dt.float32
+BF16 = mybir.dt.bfloat16
+I32 = mybir.dt.int32
+U32 = mybir.dt.uint32
+U16 = mybir.dt.uint16
+U8 = mybir.dt.uint8
+FP8X4 = mybir.dt.float8_e4m3fn_x4
+FP4X4 = mybir.dt.float4_e2m1fn_x4
+MULT = mybir.AluOpType.mult
+ADD = mybir.AluOpType.add
+SIGMOID = mybir.ActivationFunctionType.Sigmoid
+
+P = 128
+PACK = 4
+CHUNK = 128
+CHUNKS = J // CHUNK
+HALF = J // 2
+
+
+def tile_list_ckg_sig_kernel(
+    tc, tab_words, tab_scales, tab2_words, tab2_scales, wer, wei, wrr, wri,
+    nr_words, nr_scales, ni_words, ni_scales, offs, offs2, out
+):
+    nc = tc.nc
+    with ExitStack() as ctx:
+        keep = ctx.enter_context(tc.tile_pool(name="keep", bufs=1))
+        ring = ctx.enter_context(tc.tile_pool(name="ring", bufs=3))
+        psum = ctx.enter_context(tc.psum_pool(name="psum", bufs=1))
+
+        ent_list = keep.tile([P, J // 16], U16, name="ent_list")
+        rel_list = keep.tile([P, J // 16], U16, name="rel_list")
+        ent_words = keep.tile([P, T], I32, name="ent_words", align_bytes=64)
+        rel_words = keep.tile([P, T], I32, name="rel_words", align_bytes=64)
+        ent_scales = keep.tile([P, T // 4], I32, name="ent_scales", align_bytes=64)
+        rel_scales = keep.tile([P, 2, T // 4], I32, name="rel_scales", align_bytes=64)
+        cand_words = keep.tile([P, 2, 2 * N], U8, name="cand_words", align_bytes=64)
+        cand_scales = keep.tile([P, 2, N // 4], I32, name="cand_scales", align_bytes=64)
+
+        nc.vector.memset(rel_scales[:], 0)
+        nc.vector.memset(ent_scales[:], 0)
+        nc.vector.memset(cand_scales[:], 0)
+
+        passes = {
+            "c0": wrr[0:512, :], "c1": wrr[512:1024, :], "d0": wri[0:512, :], "d1": wri[512:1024, :],
+            "a": wer, "b": wei,
+        }
+        raw = {name: keep.tile([P, PACK, R], F32, name="raw_" + name) for name in passes}
+
+        def load_weight(name, parts=1):
+            rows = passes[name].rearrange("(p j) c -> p j c", j=PACK)
+            w = R // parts
+            for h in range(parts):
+                nc.sync.dma_start(raw[name][:, :, h * w : (h + 1) * w], rows[:, :, h * w : (h + 1) * w])
+
+        nc.sync.dma_start(rel_list[:], offs2)
+        nc.sync.dma_start(rel_words[:], tab2_words[0].rearrange("p t i -> p (t i)").bitcast(I32))
+        for q in range(4):
+            nc.sync.dma_start(
+                rel_scales[32 * q : 32 * q + 4], tab2_scales[:, 4 * q : 4 * q + 4, :].bitcast(I32).rearrange("a q t -> q a t")
+            )
+        load_weight("c0")
+        nc.sync.dma_start(ent_list[:], offs)
+        nc.sync.dma_start(ent_words[:], tab_words[0].rearrange("p t i -> p (t i)").bitcast(I32))
+        load_weight("c1")
+        for q in range(4):
+            nc.sync.dma_start(ent_scales[32 * q : 32 * q + 4, :], tab_scales[0, 4 * q : 4 * q + 4, :].bitcast(I32))
+        load_weight("d0")
+        load_weight("d1")
+        load_weight("a")
+        load_weight("b", 2)
+        for s, (words, scales) in enumerate(((nr_words, nr_scales), (ni_words, ni_scales))):
+            nc.sync.dma_start(cand_words[:, s, :].bitcast(I32), words[0].bitcast(I32))
+            for q in range(4):
+                nc.sync.dma_start(cand_scales[32 * q : 32 * q + 4, s, :], scales[0, 4 * q : 4 * q + 4, :].bitcast(I32))
+
+        ent_codes = keep.tile([P, J], U32, name="ent_codes", align_bytes=64)
+        ent_sc = keep.tile([P, J], U8, name="ent_sc", align_bytes=64)
+        rel_pairs = keep.tile([P, J], U32, name="rel_pairs", align_bytes=64)
+        rel_codes = keep.tile([P, 2, 2 * J], U8, name="rel_codes", align_bytes=64)
+        rel_sc = [keep.tile([P, J], U8, name="rel_sc%d" % a, align_bytes=64) for a in range(2)]
+
+        def gather_rel(h):
+            cols = slice(h * HALF, (h + 1) * HALF)
+            lst = rel_list[:, h * HALF // 16 : (h + 1) * HALF // 16]
+            nc.vector.tensor_copy(rel_pairs[:, cols], rel_words[:].bitcast(U32).indirect(lst))
+            for a in range(2):
+                nc.vector.tensor_copy(rel_sc[a][:, cols], rel_scales[:, a, :].bitcast(U8).indirect(lst))
+            nc.vector.tensor_copy(
+                rel_codes[:, :, 2 * h * HALF : 2 * (h + 1) * HALF].bitcast(U16),
+                rel_pairs[:, cols].bitcast(U16).rearrange("p (j d) -> p d j", d=2),
+            )
+
+        def gather_ent(h):
+            cols = slice(h * HALF, (h + 1) * HALF)
+            lst = ent_list[:, h * HALF // 16 : (h + 1) * HALF // 16]
+            nc.vector.tensor_copy(ent_codes[:, cols], ent_words[:].bitcast(U32).indirect(lst))
+            nc.vector.tensor_copy(ent_sc[:, cols], ent_scales[:].bitcast(U8).indirect(lst))
+
+        w_codes = {name: keep.tile([P, R], U32, name="codes_" + name, align_bytes=64) for name in passes}
+        w_scales = {name: keep.tile([P, R], U8, name="scales_" + name, align_bytes=64) for name in passes}
+
+        def quantize_weight(name, on_vector=0):
+            grouped = ring.tile([P, PACK * R], BF16, name="grouped", align_bytes=64)
+            dst = grouped[:].rearrange("p (t m j) -> p m j t", t=PACK, j=PACK)
+            src = raw[name][:].rearrange("p j (m t) -> p m j t", t=PACK)
+            if on_vector:
+                nc.vector.tensor_copy(dst[:, :on_vector], src[:, :on_vector])
+            nc.scalar.copy(dst[:, on_vector:], src[:, on_vector:])
+            nc.vector.quantize_mx(out=w_codes[name][:].bitcast(FP8X4), scales=w_scales[name][:], in_=grouped[:])
+
+        gather_rel(0)
+        quantize_weight("c0")
+        quantize_weight("c1")
+        gather_ent(0)
+        quantize_weight("d0")
+        quantize_weight("d1")
+        quantize_weight("a", 64)
+        quantize_weight("b", 64)
+        gather_rel(1)
+        gather_ent(1)
+
+        def project(tag, bufs, names, moving):
+            acc = psum.tile([P, PACK, CHUNK], F32, name=tag, tag=tag, bufs=bufs)
+            for t in range(PACK):
+                m = slice(t * P, (t + 1) * P)
+                for g, name in enumerate(names):
+                    codes, scales = moving[g]
+                    nc.tensor.matmul_mx(
+                        out=acc[:, t, :], lhsT=w_codes[name][:, m].bitcast(FP8X4), lhsT_scale=w_scales[name][:, m],
+                        rhs=codes, rhs_scale=scales, start=(g == 0), stop=(g == len(names) - 1),
+                    )
+            return acc[:].rearrange("p t n -> p n t")
+
+        def complex_product(i):
+            cols = slice(i * CHUNK, (i + 1) * CHUNK)
+            rel = [
+                (rel_codes[:, a, 2 * i * CHUNK : 2 * (i + 1) * CHUNK].bitcast(FP4X4), rel_sc[a][:, cols])
+                for a in range(2)
+            ]
+            ent = [(ent_codes[:, cols].bitcast(FP8X4), ent_sc[:, cols])]
+            rel_sb = ring.tile([P, 2, CHUNK, PACK], F32, name="rel_sb")
+            nc.scalar.copy(rel_sb[:, 0], project("rel_acc", 3, ("c0", "c1"), rel))
+            nc.scalar.copy(rel_sb[:, 1], project("rel_acc", 3, ("d0", "d1"), rel))
+            terms = ring.tile([P, 4, CHUNK, PACK], F32, name="terms")
+            aer = project("aer_acc", 2, ("a",), ent)
+            nc.vector.tensor_tensor(terms[:, 0], aer, rel_sb[:, 0], MULT)
+            nc.vector.tensor_tensor(terms[:, 1], aer, rel_sb[:, 1], MULT)
+            aei = project("aei_acc", 2, ("b",), ent)
+            nc.vector.scalar_tensor_tensor(terms[:, 2], aei, -1.0, rel_sb[:, 1], MULT, MULT)
+            nc.vector.tensor_tensor(terms[:, 3], aei, rel_sb[:, 0], MULT)
+            return terms
+
+        def score(i, terms):
+            h = keep.tile([P, 2 * CHUNK * PACK], BF16, name="h", align_bytes=64)
+            flat = terms[:].rearrange("p s n t -> p (s n t)")
+            adder = nc.vector if i == CHUNKS - 1 else nc.gpsimd
+            adder.tensor_tensor(h[:], flat[:, : 2 * CHUNK * PACK], flat[:, 2 * CHUNK * PACK :], ADD)
+            h_codes = ring.tile([P, 2 * CHUNK], U32, name="h_codes", align_bytes=64)
+            h_scales = ring.tile([P, 2 * CHUNK], U8, name="h_scales", align_bytes=64)
+            nc.vector.quantize_mx(out=h_codes[:].bitcast(FP8X4), scales=h_scales[:], in_=h[:])
+            y = psum.tile([P, N // P, CHUNK], F32, name="y")
+            for u in range(N // P):
+                for s in range(2):
+                    nc.tensor.matmul_mx(
+                        out=y[:, u, :],
+                        lhsT=cand_words[:, s, 2 * u * P : 2 * (u + 1) * P].bitcast(FP4X4),
+                        lhsT_scale=cand_scales[:, s, :].bitcast(U8)[:, u * P : (u + 1) * P],
+                        rhs=h_codes[:, s * CHUNK : (s + 1) * CHUNK].bitcast(FP8X4),
+                        rhs_scale=h_scales[:, s * CHUNK : (s + 1) * CHUNK],
+                        start=(s == 0), stop=(s == 1),
+                    )
+            result = ring.tile([P, N // P, CHUNK], F32, name="result")
+            nc.scalar.activation(result[:], y[:], SIGMOID)
+            nc.sync.dma_start(out[:, i * CHUNK : (i + 1) * CHUNK].rearrange("(u p) j -> p u j", p=P), result[:])
+
+        pending = None
+        for i in range(CHUNKS):
+            terms = complex_product(i)
+            if pending is not None:
+                score(*pending)
+            pending = (i, terms)
+        score(*pending)

@@ -36,72 +36,62 @@ def tile_list_ckg_sig_kernel(
 
         ent_list = keep.tile([P, J // 16], U16, name="ent_list")
         rel_list = keep.tile([P, J // 16], U16, name="rel_list")
-        ent_words = keep.tile([P, T], I32, name="ent_words", align_bytes=64)
-        rel_words = keep.tile([P, T], I32, name="rel_words", align_bytes=64)
-        ent_scales = keep.tile([P, T // 4], I32, name="ent_scales", align_bytes=64)
-        rel_scales = keep.tile([P, 2, T // 4], I32, name="rel_scales", align_bytes=64)
-        cand_words = keep.tile([P, 2, 2 * N], U8, name="cand_words", align_bytes=64)
-        cand_scales = keep.tile([P, 2, N // 4], I32, name="cand_scales", align_bytes=64)
+        ent_scales = keep.tile([P, T // 4], I32, name="ent_scales", tag="slot_ent", align_bytes=64)
+        rel_scales = keep.tile([P, T // 4], I32, name="rel_scales", tag="slot_rel", align_bytes=64)
+        rel_sc = [keep.tile([P, J // 4], I32, name="rel_sc%d" % a, align_bytes=64) for a in range(2)]
 
         nc.vector.memset(rel_scales[:], 0)
         nc.vector.memset(ent_scales[:], 0)
-        nc.vector.memset(cand_scales[:], 0)
+        nc.vector.memset(rel_sc[1][:], 0)
 
         passes = {
             "c0": wrr[0:512, :], "c1": wrr[512:1024, :], "d0": wri[0:512, :], "d1": wri[512:1024, :],
             "a": wer, "b": wei,
         }
-        raw = {name: keep.tile([P, PACK, R], F32, name="raw_" + name) for name in passes}
+        raw = {}
+        slot = {"c0": "slot_c0", "c1": "slot_c1", "a": "slot_rel", "b": "slot_ent", "d0": "slot_c1", "d1": "slot_rel"}
 
         def load_weight(name, parts=1):
             rows = passes[name].rearrange("(p j) c -> p j c", j=PACK)
             w = R // parts
+            raw[name] = keep.tile([P, PACK, R], F32, name="raw_" + name, tag=slot[name], align_bytes=64)
             for h in range(parts):
                 nc.sync.dma_start(raw[name][:, :, h * w : (h + 1) * w], rows[:, :, h * w : (h + 1) * w])
-
-        nc.sync.dma_start(rel_list[:], offs2)
-        nc.sync.dma_start(rel_words[:], tab2_words[0].rearrange("p t i -> p (t i)").bitcast(I32))
-        for q in range(4):
-            nc.sync.dma_start(
-                rel_scales[32 * q : 32 * q + 4], tab2_scales[:, 4 * q : 4 * q + 4, :].bitcast(I32).rearrange("a q t -> q a t")
-            )
-        load_weight("c0")
-        nc.sync.dma_start(ent_list[:], offs)
-        nc.sync.dma_start(ent_words[:], tab_words[0].rearrange("p t i -> p (t i)").bitcast(I32))
-        load_weight("c1")
-        for q in range(4):
-            nc.sync.dma_start(ent_scales[32 * q : 32 * q + 4, :], tab_scales[0, 4 * q : 4 * q + 4, :].bitcast(I32))
-        load_weight("d0")
-        load_weight("d1")
-        load_weight("a")
-        load_weight("b", 2)
-        for s, (words, scales) in enumerate(((nr_words, nr_scales), (ni_words, ni_scales))):
-            nc.sync.dma_start(cand_words[:, s, :].bitcast(I32), words[0].bitcast(I32))
-            for q in range(4):
-                nc.sync.dma_start(cand_scales[32 * q : 32 * q + 4, s, :], scales[0, 4 * q : 4 * q + 4, :].bitcast(I32))
 
         ent_codes = keep.tile([P, J], U32, name="ent_codes", align_bytes=64)
         ent_sc = keep.tile([P, J], U8, name="ent_sc", align_bytes=64)
         rel_pairs = keep.tile([P, J], U32, name="rel_pairs", align_bytes=64)
         rel_codes = keep.tile([P, 2, 2 * J], U8, name="rel_codes", align_bytes=64)
-        rel_sc = [keep.tile([P, J], U8, name="rel_sc%d" % a, align_bytes=64) for a in range(2)]
+
+        rel_words = keep.tile([P, T], I32, name="rel_words", align_bytes=64)
+        nc.sync.dma_start(rel_list[:], offs2)
+        for q in range(4):
+            nc.sync.dma_start(rel_scales[32 * q : 32 * q + 8, :], tab2_scales[:, 4 * q : 4 * q + 4, :].bitcast(I32))
+        load_weight("c0")
+        nc.sync.dma_start(ent_list[:], offs)
+        nc.sync.dma_start(rel_words[:], tab2_words[0].rearrange("p t i -> p (t i)").bitcast(I32))
+        for q in range(4):
+            nc.sync.dma_start(ent_scales[32 * q : 32 * q + 4, :], tab_scales[0, 4 * q : 4 * q + 4, :].bitcast(I32))
+        load_weight("c1")
+        nc.vector.tensor_copy(rel_sc[0][:].bitcast(U8), rel_scales[:].bitcast(U8).indirect(rel_list[:]))
+        for q in range(4):
+            nc.sync.dma_start(rel_sc[1][32 * q : 32 * q + 4, :], rel_sc[0][32 * q + 4 : 32 * q + 8, :])
+        load_weight("a")
+        nc.vector.tensor_copy(ent_sc[:], ent_scales[:].bitcast(U8).indirect(ent_list[:]))
 
         def gather_rel(h):
             cols = slice(h * HALF, (h + 1) * HALF)
             lst = rel_list[:, h * HALF // 16 : (h + 1) * HALF // 16]
             nc.vector.tensor_copy(rel_pairs[:, cols], rel_words[:].bitcast(U32).indirect(lst))
-            for a in range(2):
-                nc.vector.tensor_copy(rel_sc[a][:, cols], rel_scales[:, a, :].bitcast(U8).indirect(lst))
             nc.vector.tensor_copy(
                 rel_codes[:, :, 2 * h * HALF : 2 * (h + 1) * HALF].bitcast(U16),
                 rel_pairs[:, cols].bitcast(U16).rearrange("p (j d) -> p d j", d=2),
             )
 
-        def gather_ent(h):
+        def gather_ent(h, ent_words):
             cols = slice(h * HALF, (h + 1) * HALF)
             lst = ent_list[:, h * HALF // 16 : (h + 1) * HALF // 16]
             nc.vector.tensor_copy(ent_codes[:, cols], ent_words[:].bitcast(U32).indirect(lst))
-            nc.vector.tensor_copy(ent_sc[:, cols], ent_scales[:].bitcast(U8).indirect(lst))
 
         w_codes = {name: keep.tile([P, R], U32, name="codes_" + name, align_bytes=64) for name in passes}
         w_scales = {name: keep.tile([P, R], U8, name="scales_" + name, align_bytes=64) for name in passes}
@@ -110,21 +100,33 @@ def tile_list_ckg_sig_kernel(
             grouped = ring.tile([P, PACK * R], BF16, name="grouped", align_bytes=64)
             dst = grouped[:].rearrange("p (t m j) -> p m j t", t=PACK, j=PACK)
             src = raw[name][:].rearrange("p j (m t) -> p m j t", t=PACK)
+            on_scalar = P - on_vector
+            nc.scalar.copy(dst[:, :on_scalar], src[:, :on_scalar])
             if on_vector:
-                nc.vector.tensor_copy(dst[:, :on_vector], src[:, :on_vector])
-            nc.scalar.copy(dst[:, on_vector:], src[:, on_vector:])
+                nc.vector.tensor_copy(dst[:, on_scalar:], src[:, on_scalar:])
             nc.vector.quantize_mx(out=w_codes[name][:].bitcast(FP8X4), scales=w_scales[name][:], in_=grouped[:])
 
-        gather_rel(0)
         quantize_weight("c0")
-        quantize_weight("c1")
-        gather_ent(0)
-        quantize_weight("d0")
-        quantize_weight("d1")
-        quantize_weight("a", 64)
-        quantize_weight("b", 64)
+        ent_words = keep.tile([P, T], I32, name="ent_words", tag="slot_c0", align_bytes=64)
+        nc.sync.dma_start(ent_words[:], tab_words[0].rearrange("p t i -> p (t i)").bitcast(I32))
+        load_weight("b", 2)
+        gather_rel(0)
         gather_rel(1)
-        gather_ent(1)
+        quantize_weight("c1")
+        load_weight("d0", 2)
+        quantize_weight("a")
+        load_weight("d1", 2)
+        gather_ent(0, ent_words)
+        gather_ent(1, ent_words)
+        cand = keep.tile([P, 2, 3 * N // 4], I32, name="cand", tag="slot_c0", align_bytes=64)
+        nc.gpsimd.memset(cand[:, :, N // 2 :], 0)
+        for s, (words, scales) in enumerate(((nr_words, nr_scales), (ni_words, ni_scales))):
+            nc.sync.dma_start(cand[:, s, : N // 2], words[0].bitcast(I32))
+            for q in range(4):
+                nc.sync.dma_start(cand[32 * q : 32 * q + 4, s, N // 2 :], scales[0, 4 * q : 4 * q + 4, :].bitcast(I32))
+        quantize_weight("b", 64)
+        quantize_weight("d0", 64)
+        quantize_weight("d1", 64)
 
         def project(tag, bufs, names, moving):
             acc = psum.tile([P, PACK, CHUNK], F32, name=tag, tag=tag, bufs=bufs)
@@ -138,52 +140,90 @@ def tile_list_ckg_sig_kernel(
                     )
             return acc[:].rearrange("p t n -> p n t")
 
+        ent_first = keep.tile([P, 2, CHUNK, PACK], F32, name="ent_first", tag="slot_c1", align_bytes=64)
+        ent_next = keep.tile([P, 2, 2, CHUNK, PACK], F32, name="ent_next", tag="slot_rel", align_bytes=64)
+
         def complex_product(i):
             cols = slice(i * CHUNK, (i + 1) * CHUNK)
             rel = [
-                (rel_codes[:, a, 2 * i * CHUNK : 2 * (i + 1) * CHUNK].bitcast(FP4X4), rel_sc[a][:, cols])
+                (rel_codes[:, a, 2 * i * CHUNK : 2 * (i + 1) * CHUNK].bitcast(FP4X4), rel_sc[a][:].bitcast(U8)[:, cols])
                 for a in range(2)
             ]
             ent = [(ent_codes[:, cols].bitcast(FP8X4), ent_sc[:, cols])]
-            rel_sb = ring.tile([P, 2, CHUNK, PACK], F32, name="rel_sb")
-            nc.scalar.copy(rel_sb[:, 0], project("rel_acc", 3, ("c0", "c1"), rel))
-            nc.scalar.copy(rel_sb[:, 1], project("rel_acc", 3, ("d0", "d1"), rel))
-            terms = ring.tile([P, 4, CHUNK, PACK], F32, name="terms")
-            aer = project("aer_acc", 2, ("a",), ent)
-            nc.vector.tensor_tensor(terms[:, 0], aer, rel_sb[:, 0], MULT)
-            nc.vector.tensor_tensor(terms[:, 1], aer, rel_sb[:, 1], MULT)
-            aei = project("aei_acc", 2, ("b",), ent)
-            nc.vector.scalar_tensor_tensor(terms[:, 2], aei, -1.0, rel_sb[:, 1], MULT, MULT)
-            nc.vector.tensor_tensor(terms[:, 3], aei, rel_sb[:, 0], MULT)
-            return terms
+            if i == 0:
+                ent_sb = ent_first[:]
+            elif i < 3:
+                ent_sb = ent_next[:, i - 1]
+            else:
+                ent_sb = ring.tile([P, 2, CHUNK, PACK], F32, name="ent_sb")[:]
+            aer, aei = ent_sb[:, 0], ent_sb[:, 1]
+            terms = keep.tile([P, 4, CHUNK, PACK], F32, name="terms%d" % i)
+            nc.scalar.copy(aer, project("ent_acc", 2, ("a",), ent))
+            nc.scalar.copy(aei, project("ent_acc", 2, ("b",), ent))
+            arr = project("arr_acc", 2, ("c0", "c1"), rel)
+            ari = project("ari_acc", 2, ("d0", "d1"), rel)
+            if i < 2:
+                nc.vector.tensor_tensor(terms[:, 0], arr, aer, MULT)
+                nc.vector.tensor_tensor(terms[:, 1], arr, aei, MULT)
+            else:
+                nc.vector.tensor_tensor(terms[:, 0:2], arr.unsqueeze(1).to_broadcast([P, 2, CHUNK, PACK]), ent_sb, MULT)
+            nc.vector.scalar_tensor_tensor(terms[:, 2], ari, -1.0, aei, MULT, MULT)
+            nc.vector.tensor_tensor(terms[:, 3], ari, aer, MULT)
+            return terms[:].rearrange("p (g s) n t -> p g s (n t)", g=2)
 
-        def score(i, terms):
-            h = keep.tile([P, 2 * CHUNK * PACK], BF16, name="h", align_bytes=64)
-            flat = terms[:].rearrange("p s n t -> p (s n t)")
-            adder = nc.vector if i == CHUNKS - 1 else nc.gpsimd
-            adder.tensor_tensor(h[:], flat[:, : 2 * CHUNK * PACK], flat[:, 2 * CHUNK * PACK :], ADD)
-            h_codes = ring.tile([P, 2 * CHUNK], U32, name="h_codes", align_bytes=64)
-            h_scales = ring.tile([P, 2 * CHUNK], U8, name="h_scales", align_bytes=64)
-            nc.vector.quantize_mx(out=h_codes[:].bitcast(FP8X4), scales=h_scales[:], in_=h[:])
-            y = psum.tile([P, N // P, CHUNK], F32, name="y")
+        WIDE = CHUNK * PACK
+
+        def quantize_h(h, tokens, name):
+            h_codes = keep.tile([P, tokens], U32, name="codes_" + name, align_bytes=64)
+            h_scales = keep.tile([P, tokens], U8, name="scales_" + name, align_bytes=64)
+            nc.vector.quantize_mx(out=h_codes[:].bitcast(FP8X4), scales=h_scales[:], in_=h)
+            return h_codes, h_scales
+
+        def score(y, u, operands):
+            for s, (codes, scales) in enumerate(operands):
+                nc.tensor.matmul_mx(
+                    out=y,
+                    lhsT=cand[:, s, :].bitcast(U8)[:, 2 * u * P : 2 * (u + 1) * P].bitcast(FP4X4),
+                    lhsT_scale=cand[:, s, :].bitcast(U8)[:, 2 * N + u * P : 2 * N + (u + 1) * P],
+                    rhs=codes.bitcast(FP8X4), rhs_scale=scales, start=(s == 0), stop=(s == 1),
+                )
+
+        def score_chunk(i, operands):
+            y = psum.tile([P, N // P, CHUNK], F32, name="y", tag="y", bufs=2)
             for u in range(N // P):
-                for s in range(2):
-                    nc.tensor.matmul_mx(
-                        out=y[:, u, :],
-                        lhsT=cand_words[:, s, 2 * u * P : 2 * (u + 1) * P].bitcast(FP4X4),
-                        lhsT_scale=cand_scales[:, s, :].bitcast(U8)[:, u * P : (u + 1) * P],
-                        rhs=h_codes[:, s * CHUNK : (s + 1) * CHUNK].bitcast(FP8X4),
-                        rhs_scale=h_scales[:, s * CHUNK : (s + 1) * CHUNK],
-                        start=(s == 0), stop=(s == 1),
-                    )
-            result = ring.tile([P, N // P, CHUNK], F32, name="result")
+                score(y[:, u, :], u, operands)
+            result = ring.tile([P, N // P, CHUNK], F32, name="result", tag="result")
             nc.scalar.activation(result[:], y[:], SIGMOID)
             nc.sync.dma_start(out[:, i * CHUNK : (i + 1) * CHUNK].rearrange("(u p) j -> p u j", p=P), result[:])
 
-        pending = None
-        for i in range(CHUNKS):
-            terms = complex_product(i)
-            if pending is not None:
-                score(*pending)
-            pending = (i, terms)
-        score(*pending)
+        terms = [complex_product(0)]
+        h_half = keep.tile([P, 2, 4, WIDE], BF16, name="h_half", tag="h", align_bytes=64)
+        for i in range(4):
+            nc.gpsimd.tensor_tensor(h_half[:, :, i, :], terms[i][:, 0], terms[i][:, 1], ADD)
+            terms.append(complex_product(i + 1))
+        codes, scales = quantize_h(h_half[:].rearrange("p s i w -> p (s i w)"), 2 * HALF, "half")
+        for u in range(N // P):
+            y = psum.tile([P, HALF], F32, name="y_half", tag="y", bufs=2)
+            score(y[:], u, [(codes[:, s * HALF : (s + 1) * HALF], scales[:, s * HALF : (s + 1) * HALF]) for s in range(2)])
+            result = ring.tile([P, HALF], F32, name="result_half", tag="result")
+            nc.scalar.activation(result[:], y[:], SIGMOID)
+            nc.sync.dma_start(out[u * P : (u + 1) * P, :HALF], result[:])
+
+        h_pair = keep.tile([P, 2, 2, WIDE], BF16, name="h_pair", tag="h", align_bytes=64)
+        for e in range(2):
+            nc.gpsimd.tensor_tensor(h_pair[:, e], terms[4 + e][:, 0], terms[4 + e][:, 1], ADD)
+            terms.append(complex_product(5 + e))
+        terms.append(complex_product(7))
+        codes, scales = quantize_h(h_pair[:].rearrange("p e s w -> p (e s w)"), 4 * CHUNK, "pair")
+        for e in range(2):
+            cols = [slice((2 * e + s) * CHUNK, (2 * e + s + 1) * CHUNK) for s in range(2)]
+            score_chunk(4 + e, [(codes[:, c], scales[:, c]) for c in cols])
+
+        h_last = keep.tile([P, 2, 2, WIDE], BF16, name="h_last", align_bytes=64)
+        nc.vector.tensor_tensor(h_last[:, 0], terms[6][:, 0], terms[6][:, 1], ADD)
+        nc.vector.tensor_tensor(h_last[:, 1, 0], terms[7][:, 0, 0], terms[7][:, 1, 0], ADD)
+        codes, scales = quantize_h(h_last[:, 0].rearrange("p s w -> p (s w)"), 2 * CHUNK, "six")
+        score_chunk(6, [(codes[:, s * CHUNK : (s + 1) * CHUNK], scales[:, s * CHUNK : (s + 1) * CHUNK]) for s in range(2)])
+        nc.vector.tensor_tensor(h_last[:, 1, 1], terms[7][:, 0, 1], terms[7][:, 1, 1], ADD)
+        made = [quantize_h(h_last[:, 1, s], CHUNK, "seven%d" % s) for s in range(2)]
+        score_chunk(7, [(codes[:], scales[:]) for codes, scales in made])

@@ -19,9 +19,16 @@ SIGMOID = mybir.ActivationFunctionType.Sigmoid
 
 P = 128
 PACK = 4
+K_PASS = P * PACK
+QUADS = 4
+GROUP = 16
 CHUNK = 128
-CHUNKS = J // CHUNK
+WIDE = CHUNK * PACK
 HALF = J // 2
+HALF_CHUNKS = HALF // CHUNK
+SHARED = P // 2
+BANKS = 2
+EARLY = 2
 
 
 def tile_list_ckg_sig_kernel(
@@ -34,8 +41,8 @@ def tile_list_ckg_sig_kernel(
         ring = ctx.enter_context(tc.tile_pool(name="ring", bufs=3))
         psum = ctx.enter_context(tc.psum_pool(name="psum", bufs=1))
 
-        ent_list = keep.tile([P, J // 16], U16, name="ent_list")
-        rel_list = keep.tile([P, J // 16], U16, name="rel_list")
+        ent_list = keep.tile([P, J // GROUP], U16, name="ent_list")
+        rel_list = keep.tile([P, J // GROUP], U16, name="rel_list")
         ent_scales = keep.tile([P, T // 4], I32, name="ent_scales", tag="slot_ent", align_bytes=64)
         rel_scales = keep.tile([P, T // 4], I32, name="rel_scales", tag="slot_rel", align_bytes=64)
         rel_sc = [keep.tile([P, J // 4], I32, name="rel_sc%d" % a, align_bytes=64) for a in range(2)]
@@ -45,61 +52,57 @@ def tile_list_ckg_sig_kernel(
         nc.vector.memset(rel_sc[1][:], 0)
 
         passes = {
-            "c0": wrr[0:512, :], "c1": wrr[512:1024, :], "d0": wri[0:512, :], "d1": wri[512:1024, :],
+            "c0": wrr[:K_PASS, :], "c1": wrr[K_PASS:, :], "d0": wri[:K_PASS, :], "d1": wri[K_PASS:, :],
             "a": wer, "b": wei,
         }
-        raw = {}
         slot = {"c0": "slot_c0", "c1": "slot_c1", "a": "slot_rel", "b": "slot_ent", "d0": "slot_c1", "d1": "slot_rel"}
+        raw = {}
 
         def load_weight(name, parts=1):
-            rows = passes[name].rearrange("(p j) c -> p j c", j=PACK)
-            w = R // parts
+            rows = passes[name].rearrange("(p e) r -> p e r", e=PACK)
+            width = R // parts
             raw[name] = keep.tile([P, PACK, R], F32, name="raw_" + name, tag=slot[name], align_bytes=64)
-            for h in range(parts):
-                nc.sync.dma_start(raw[name][:, :, h * w : (h + 1) * w], rows[:, :, h * w : (h + 1) * w])
+            for part in range(parts):
+                span = slice(part * width, (part + 1) * width)
+                nc.sync.dma_start(raw[name][:, :, span], rows[:, :, span])
 
         ent_codes = keep.tile([P, J], U32, name="ent_codes", align_bytes=64)
         ent_sc = keep.tile([P, J], U8, name="ent_sc", align_bytes=64)
         rel_pairs = keep.tile([P, J], U32, name="rel_pairs", align_bytes=64)
         rel_codes = keep.tile([P, 2, 2 * J], U8, name="rel_codes", align_bytes=64)
-
         rel_words = keep.tile([P, T], I32, name="rel_words", align_bytes=64)
+
         nc.sync.dma_start(rel_list[:], offs2)
-        for q in range(4):
-            nc.sync.dma_start(rel_scales[32 * q : 32 * q + 8, :], tab2_scales[:, 4 * q : 4 * q + 4, :].bitcast(I32))
+        for q in range(QUADS):
+            nc.scalar.dma_start(rel_scales[32 * q : 32 * q + 8, :], tab2_scales[:, 4 * q : 4 * q + 4, :].bitcast(I32))
         load_weight("c0")
         nc.sync.dma_start(ent_list[:], offs)
         nc.sync.dma_start(rel_words[:], tab2_words[0].rearrange("p t i -> p (t i)").bitcast(I32))
-        for q in range(4):
-            nc.sync.dma_start(ent_scales[32 * q : 32 * q + 4, :], tab_scales[0, 4 * q : 4 * q + 4, :].bitcast(I32))
+        for q in range(QUADS):
+            nc.scalar.dma_start(ent_scales[32 * q : 32 * q + 4, :], tab_scales[0, 4 * q : 4 * q + 4, :].bitcast(I32))
         load_weight("c1")
         nc.vector.tensor_copy(rel_sc[0][:].bitcast(U8), rel_scales[:].bitcast(U8).indirect(rel_list[:]))
-        for q in range(4):
+        for q in range(QUADS):
             nc.sync.dma_start(rel_sc[1][32 * q : 32 * q + 4, :], rel_sc[0][32 * q + 4 : 32 * q + 8, :])
         load_weight("a")
         nc.vector.tensor_copy(ent_sc[:], ent_scales[:].bitcast(U8).indirect(ent_list[:]))
 
-        def gather_rel(h):
-            cols = slice(h * HALF, (h + 1) * HALF)
-            lst = rel_list[:, h * HALF // 16 : (h + 1) * HALF // 16]
-            nc.vector.tensor_copy(rel_pairs[:, cols], rel_words[:].bitcast(U32).indirect(lst))
+        def gather_rel(half):
+            cols = slice(half * HALF, (half + 1) * HALF)
+            entries = rel_list[:, half * HALF // GROUP : (half + 1) * HALF // GROUP]
+            nc.vector.tensor_copy(rel_pairs[:, cols], rel_words[:].bitcast(U32).indirect(entries))
             nc.vector.tensor_copy(
-                rel_codes[:, :, 2 * h * HALF : 2 * (h + 1) * HALF].bitcast(U16),
-                rel_pairs[:, cols].bitcast(U16).rearrange("p (j d) -> p d j", d=2),
+                rel_codes[:, :, 2 * half * HALF : 2 * (half + 1) * HALF].bitcast(U16),
+                rel_pairs[:, cols].bitcast(U16).rearrange("p (j a) -> p a j", a=2),
             )
-
-        def gather_ent(h, ent_words):
-            cols = slice(h * HALF, (h + 1) * HALF)
-            lst = ent_list[:, h * HALF // 16 : (h + 1) * HALF // 16]
-            nc.vector.tensor_copy(ent_codes[:, cols], ent_words[:].bitcast(U32).indirect(lst))
 
         w_codes = {name: keep.tile([P, R], U32, name="codes_" + name, align_bytes=64) for name in passes}
         w_scales = {name: keep.tile([P, R], U8, name="scales_" + name, align_bytes=64) for name in passes}
 
         def quantize_weight(name, on_vector=0):
             grouped = ring.tile([P, PACK * R], BF16, name="grouped", align_bytes=64)
-            dst = grouped[:].rearrange("p (t m j) -> p m j t", t=PACK, j=PACK)
-            src = raw[name][:].rearrange("p j (m t) -> p m j t", t=PACK)
+            dst = grouped[:].rearrange("p (t m e) -> p m e t", t=PACK, e=PACK)
+            src = raw[name][:].rearrange("p e (m t) -> p m e t", t=PACK)
             on_scalar = P - on_vector
             nc.scalar.copy(dst[:, :on_scalar], src[:, :on_scalar])
             if on_vector:
@@ -116,114 +119,119 @@ def tile_list_ckg_sig_kernel(
         load_weight("d0", 2)
         quantize_weight("a")
         load_weight("d1", 2)
-        gather_ent(0, ent_words)
-        gather_ent(1, ent_words)
+        for half in range(2):
+            entries = ent_list[:, half * HALF // GROUP : (half + 1) * HALF // GROUP]
+            nc.vector.tensor_copy(
+                ent_codes[:, half * HALF : (half + 1) * HALF], ent_words[:].bitcast(U32).indirect(entries)
+            )
         cand = keep.tile([P, 2, 3 * N // 4], I32, name="cand", tag="slot_c0", align_bytes=64)
         nc.gpsimd.memset(cand[:, :, N // 2 :], 0)
-        for s, (words, scales) in enumerate(((nr_words, nr_scales), (ni_words, ni_scales))):
-            nc.sync.dma_start(cand[:, s, : N // 2], words[0].bitcast(I32))
-            for q in range(4):
-                nc.sync.dma_start(cand[32 * q : 32 * q + 4, s, N // 2 :], scales[0, 4 * q : 4 * q + 4, :].bitcast(I32))
-        quantize_weight("b", 64)
-        quantize_weight("d0", 64)
-        quantize_weight("d1", 64)
+        for s, (cand_words, cand_scales) in enumerate(((nr_words, nr_scales), (ni_words, ni_scales))):
+            nc.sync.dma_start(cand[:, s, : N // 2], cand_words[0].bitcast(I32))
+            for q in range(QUADS):
+                nc.sync.dma_start(
+                    cand[32 * q : 32 * q + 4, s, N // 2 :], cand_scales[0, 4 * q : 4 * q + 4, :].bitcast(I32)
+                )
+        for name in ("b", "d0", "d1"):
+            quantize_weight(name, SHARED)
 
-        def project(tag, bufs, names, moving):
-            acc = psum.tile([P, PACK, CHUNK], F32, name=tag, tag=tag, bufs=bufs)
+        def project(tag, names, moving):
+            acc = psum.tile([P, PACK, CHUNK], F32, name=tag, tag=tag, bufs=BANKS)
             for t in range(PACK):
                 m = slice(t * P, (t + 1) * P)
                 for g, name in enumerate(names):
-                    codes, scales = moving[g]
+                    table_codes, table_scales = moving[g]
                     nc.tensor.matmul_mx(
                         out=acc[:, t, :], lhsT=w_codes[name][:, m].bitcast(FP8X4), lhsT_scale=w_scales[name][:, m],
-                        rhs=codes, rhs_scale=scales, start=(g == 0), stop=(g == len(names) - 1),
+                        rhs=table_codes, rhs_scale=table_scales, start=(g == 0), stop=(g == len(names) - 1),
                     )
             return acc[:].rearrange("p t n -> p n t")
 
         ent_first = keep.tile([P, 2, CHUNK, PACK], F32, name="ent_first", tag="slot_c1", align_bytes=64)
         ent_next = keep.tile([P, 2, 2, CHUNK, PACK], F32, name="ent_next", tag="slot_rel", align_bytes=64)
+        held = [ent_first[:], ent_next[:, 0], ent_next[:, 1]]
 
-        def complex_product(i):
+        def complex_terms(i):
             cols = slice(i * CHUNK, (i + 1) * CHUNK)
             rel = [
                 (rel_codes[:, a, 2 * i * CHUNK : 2 * (i + 1) * CHUNK].bitcast(FP4X4), rel_sc[a][:].bitcast(U8)[:, cols])
                 for a in range(2)
             ]
             ent = [(ent_codes[:, cols].bitcast(FP8X4), ent_sc[:, cols])]
-            if i == 0:
-                ent_sb = ent_first[:]
-            elif i < 3:
-                ent_sb = ent_next[:, i - 1]
-            else:
-                ent_sb = ring.tile([P, 2, CHUNK, PACK], F32, name="ent_sb")[:]
+            ent_sb = held[i] if i < len(held) else ring.tile([P, 2, CHUNK, PACK], F32, name="ent_sb")[:]
             aer, aei = ent_sb[:, 0], ent_sb[:, 1]
-            terms = keep.tile([P, 4, CHUNK, PACK], F32, name="terms%d" % i)
-            nc.scalar.copy(aer, project("ent_acc", 2, ("a",), ent))
-            nc.scalar.copy(aei, project("ent_acc", 2, ("b",), ent))
-            arr = project("arr_acc", 2, ("c0", "c1"), rel)
-            ari = project("ari_acc", 2, ("d0", "d1"), rel)
-            if i < 2:
-                nc.vector.tensor_tensor(terms[:, 0], arr, aer, MULT)
-                nc.vector.tensor_tensor(terms[:, 1], arr, aei, MULT)
+            products = keep.tile([P, 4, CHUNK, PACK], F32, name="terms%d" % i)
+            nc.scalar.copy(aer, project("ent_acc", ("a",), ent))
+            nc.scalar.copy(aei, project("ent_acc", ("b",), ent))
+            arr = project("arr_acc", ("c0", "c1"), rel)
+            ari = project("ari_acc", ("d0", "d1"), rel)
+            if i < EARLY:
+                nc.vector.tensor_tensor(products[:, 0], arr, aer, MULT)
+                nc.vector.tensor_tensor(products[:, 1], arr, aei, MULT)
             else:
-                nc.vector.tensor_tensor(terms[:, 0:2], arr.unsqueeze(1).to_broadcast([P, 2, CHUNK, PACK]), ent_sb, MULT)
-            nc.vector.scalar_tensor_tensor(terms[:, 2], ari, -1.0, aei, MULT, MULT)
-            nc.vector.tensor_tensor(terms[:, 3], ari, aer, MULT)
-            return terms[:].rearrange("p (g s) n t -> p g s (n t)", g=2)
+                arr_twice = arr.unsqueeze(1).to_broadcast([P, 2, CHUNK, PACK])
+                nc.vector.tensor_tensor(products[:, 0:2], arr_twice, ent_sb, MULT)
+            nc.vector.scalar_tensor_tensor(products[:, 2], ari, -1.0, aei, MULT, MULT)
+            nc.vector.tensor_tensor(products[:, 3], ari, aer, MULT)
+            return products[:].rearrange("p (g s) n t -> p g s (n t)", g=2)
 
-        WIDE = CHUNK * PACK
-
-        def quantize_h(h, tokens, name):
-            h_codes = keep.tile([P, tokens], U32, name="codes_" + name, align_bytes=64)
-            h_scales = keep.tile([P, tokens], U8, name="scales_" + name, align_bytes=64)
+        def quantize_h(h, columns, name):
+            h_codes = keep.tile([P, columns], U32, name="codes_" + name, align_bytes=64)
+            h_scales = keep.tile([P, columns], U8, name="scales_" + name, align_bytes=64)
             nc.vector.quantize_mx(out=h_codes[:].bitcast(FP8X4), scales=h_scales[:], in_=h)
             return h_codes, h_scales
 
+        def hr_hi(quantized, first, tokens):
+            h_codes, h_scales = quantized
+            spans = [slice(first + s * tokens, first + (s + 1) * tokens) for s in range(2)]
+            return [(h_codes[:, span], h_scales[:, span]) for span in spans]
+
         def score(y, u, operands):
-            for s, (codes, scales) in enumerate(operands):
+            for s, (h_codes, h_scales) in enumerate(operands):
                 nc.tensor.matmul_mx(
                     out=y,
                     lhsT=cand[:, s, :].bitcast(U8)[:, 2 * u * P : 2 * (u + 1) * P].bitcast(FP4X4),
                     lhsT_scale=cand[:, s, :].bitcast(U8)[:, 2 * N + u * P : 2 * N + (u + 1) * P],
-                    rhs=codes.bitcast(FP8X4), rhs_scale=scales, start=(s == 0), stop=(s == 1),
+                    rhs=h_codes.bitcast(FP8X4), rhs_scale=h_scales, start=(s == 0), stop=(s == 1),
                 )
 
         def score_chunk(i, operands):
-            y = psum.tile([P, N // P, CHUNK], F32, name="y", tag="y", bufs=2)
+            y = psum.tile([P, N // P, CHUNK], F32, name="y", tag="y", bufs=BANKS)
             for u in range(N // P):
                 score(y[:, u, :], u, operands)
             result = ring.tile([P, N // P, CHUNK], F32, name="result", tag="result")
             nc.scalar.activation(result[:], y[:], SIGMOID)
             nc.sync.dma_start(out[:, i * CHUNK : (i + 1) * CHUNK].rearrange("(u p) j -> p u j", p=P), result[:])
 
-        terms = [complex_product(0)]
-        h_half = keep.tile([P, 2, 4, WIDE], BF16, name="h_half", tag="h", align_bytes=64)
-        for i in range(4):
+        terms = [complex_terms(0)]
+        h_half = keep.tile([P, 2, HALF_CHUNKS, WIDE], BF16, name="h_half", tag="h", align_bytes=64)
+        for i in range(HALF_CHUNKS):
             nc.gpsimd.tensor_tensor(h_half[:, :, i, :], terms[i][:, 0], terms[i][:, 1], ADD)
-            terms.append(complex_product(i + 1))
-        codes, scales = quantize_h(h_half[:].rearrange("p s i w -> p (s i w)"), 2 * HALF, "half")
+            terms.append(complex_terms(i + 1))
+        operands = hr_hi(quantize_h(h_half[:].rearrange("p s i w -> p (s i w)"), 2 * HALF, "half"), 0, HALF)
         for u in range(N // P):
-            y = psum.tile([P, HALF], F32, name="y_half", tag="y", bufs=2)
-            score(y[:], u, [(codes[:, s * HALF : (s + 1) * HALF], scales[:, s * HALF : (s + 1) * HALF]) for s in range(2)])
-            result = ring.tile([P, HALF], F32, name="result_half", tag="result")
-            nc.scalar.activation(result[:], y[:], SIGMOID)
-            nc.sync.dma_start(out[u * P : (u + 1) * P, :HALF], result[:])
+            y_half = psum.tile([P, HALF], F32, name="y_half", tag="y", bufs=BANKS)
+            score(y_half[:], u, operands)
+            result_half = ring.tile([P, HALF], F32, name="result_half", tag="result")
+            nc.scalar.activation(result_half[:], y_half[:], SIGMOID)
+            nc.sync.dma_start(out[u * P : (u + 1) * P, :HALF], result_half[:])
 
         h_pair = keep.tile([P, 2, 2, WIDE], BF16, name="h_pair", tag="h", align_bytes=64)
         for e in range(2):
-            nc.gpsimd.tensor_tensor(h_pair[:, e], terms[4 + e][:, 0], terms[4 + e][:, 1], ADD)
-            terms.append(complex_product(5 + e))
-        terms.append(complex_product(7))
-        codes, scales = quantize_h(h_pair[:].rearrange("p e s w -> p (e s w)"), 4 * CHUNK, "pair")
+            i = HALF_CHUNKS + e
+            nc.gpsimd.tensor_tensor(h_pair[:, e], terms[i][:, 0], terms[i][:, 1], ADD)
+            terms.append(complex_terms(i + 1))
+        before_last, last = HALF_CHUNKS + 2, HALF_CHUNKS + 3
+        terms.append(complex_terms(last))
+        pair = quantize_h(h_pair[:].rearrange("p e s w -> p (e s w)"), 4 * CHUNK, "pair")
         for e in range(2):
-            cols = [slice((2 * e + s) * CHUNK, (2 * e + s + 1) * CHUNK) for s in range(2)]
-            score_chunk(4 + e, [(codes[:, c], scales[:, c]) for c in cols])
+            score_chunk(HALF_CHUNKS + e, hr_hi(pair, 2 * e * CHUNK, CHUNK))
 
         h_last = keep.tile([P, 2, 2, WIDE], BF16, name="h_last", align_bytes=64)
-        nc.vector.tensor_tensor(h_last[:, 0], terms[6][:, 0], terms[6][:, 1], ADD)
-        nc.vector.tensor_tensor(h_last[:, 1, 0], terms[7][:, 0, 0], terms[7][:, 1, 0], ADD)
-        codes, scales = quantize_h(h_last[:, 0].rearrange("p s w -> p (s w)"), 2 * CHUNK, "six")
-        score_chunk(6, [(codes[:, s * CHUNK : (s + 1) * CHUNK], scales[:, s * CHUNK : (s + 1) * CHUNK]) for s in range(2)])
-        nc.vector.tensor_tensor(h_last[:, 1, 1], terms[7][:, 0, 1], terms[7][:, 1, 1], ADD)
-        made = [quantize_h(h_last[:, 1, s], CHUNK, "seven%d" % s) for s in range(2)]
-        score_chunk(7, [(codes[:], scales[:]) for codes, scales in made])
+        nc.vector.tensor_tensor(h_last[:, 0], terms[before_last][:, 0], terms[before_last][:, 1], ADD)
+        nc.vector.tensor_tensor(h_last[:, 1, 0], terms[last][:, 0, 0], terms[last][:, 1, 0], ADD)
+        single = quantize_h(h_last[:, 0].rearrange("p s w -> p (s w)"), 2 * CHUNK, "six")
+        score_chunk(before_last, hr_hi(single, 0, CHUNK))
+        nc.vector.tensor_tensor(h_last[:, 1, 1], terms[last][:, 0, 1], terms[last][:, 1, 1], ADD)
+        apart = [quantize_h(h_last[:, 1, s], CHUNK, "seven%d" % s) for s in range(2)]
+        score_chunk(last, [(h_codes[:], h_scales[:]) for h_codes, h_scales in apart])

@@ -38,105 +38,127 @@ def tile_list_ckg_sig_kernel(
     nc = tc.nc
     with ExitStack() as ctx:
         keep = ctx.enter_context(tc.tile_pool(name="keep", bufs=1))
+        loads = ctx.enter_context(tc.tile_pool(name="loads", bufs=1))
         ring = ctx.enter_context(tc.tile_pool(name="ring", bufs=3))
         psum = ctx.enter_context(tc.psum_pool(name="psum", bufs=1))
 
         ent_list = keep.tile([P, J // GROUP], U16, name="ent_list")
         rel_list = keep.tile([P, J // GROUP], U16, name="rel_list")
-        ent_scales = keep.tile([P, T // 4], I32, name="ent_scales", tag="slot_ent", align_bytes=64)
-        rel_scales = keep.tile([P, T // 4], I32, name="rel_scales", tag="slot_rel", align_bytes=64)
-        rel_sc = [keep.tile([P, J // 4], I32, name="rel_sc%d" % a, align_bytes=64) for a in range(2)]
+        ent_scales = keep.tile([P, T // 4], I32, name="ent_scales", align_bytes=64)
+        rel_sc1 = keep.tile([P, J // 4], I32, name="rel_sc1", align_bytes=64)
 
-        nc.vector.memset(rel_scales[:], 0)
+        SLOT = 4 * T
+        BANK_BYTES = 2048
+        zeros = loads.tile([P, 5 * T], I32, name="zeros", offset=SLOT, align_bytes=64)
+        rel_held = loads.tile([P, 3 * T // 4], I32, name="rel_held", offset=7 * SLOT - T // 2, align_bytes=64)
+        rel_scales = rel_held[:, : T // 4]
         nc.vector.memset(ent_scales[:], 0)
-        nc.vector.memset(rel_sc[1][:], 0)
+        nc.gpsimd.memset(zeros[:, : J // 4], 0)
+        nc.gpsimd.memset(rel_scales, 0)
+        nc.vector.tensor_copy(rel_sc1[:], zeros[:, : J // 4])
 
+        ent_words = loads.tile([P, T], I32, name="ent_words", offset=2 * SLOT, align_bytes=64)
+        rel_words = loads.tile([P, T], I32, name="rel_words", offset=SLOT, align_bytes=64)
         passes = {
-            "c0": wrr[:K_PASS, :], "c1": wrr[K_PASS:, :], "d0": wri[:K_PASS, :], "d1": wri[K_PASS:, :],
             "a": wer, "b": wei,
+            "c0": wrr[:K_PASS, :], "c1": wrr[K_PASS:, :], "d0": wri[:K_PASS, :], "d1": wri[K_PASS:, :],
         }
-        slot = {"c0": "slot_c0", "c1": "slot_c1", "a": "slot_rel", "b": "slot_ent", "d0": "slot_c1", "d1": "slot_rel"}
         raw = {}
+        slot = {"a": 0, "b": 3, "c0": 4, "c1": 5, "d0": 6, "d1": 7}
 
-        def load_weight(name, parts=1):
+        def load_weight(name, parts=1, only=None):
             rows = passes[name].rearrange("(p e) r -> p e r", e=PACK)
             width = R // parts
-            raw[name] = keep.tile([P, PACK, R], F32, name="raw_" + name, tag=slot[name], align_bytes=64)
-            for part in range(parts):
-                span = slice(part * width, (part + 1) * width)
-                nc.sync.dma_start(raw[name][:, :, span], rows[:, :, span])
+            raw.setdefault(name, [])
+            for part in range(parts) if only is None else [only]:
+                piece = loads.tile(
+                    [P, PACK, width], F32, name="raw_%s_%d" % (name, part), align_bytes=64,
+                    offset=slot[name] * SLOT + part * SLOT // parts,
+                )
+                nc.sync.dma_start(piece[:], rows[:, :, part * width : (part + 1) * width])
+                raw[name].append(piece)
 
-        ent_codes = keep.tile([P, J], U32, name="ent_codes", align_bytes=64)
-        ent_sc = keep.tile([P, J], U8, name="ent_sc", align_bytes=64)
-        rel_pairs = keep.tile([P, J], U32, name="rel_pairs", align_bytes=64)
-        rel_codes = keep.tile([P, 2, 2 * J], U8, name="rel_codes", align_bytes=64)
-        rel_words = keep.tile([P, T], I32, name="rel_words", align_bytes=64)
+        late = 11 * SLOT
+        ent_codes = [
+            keep.tile([P, HALF], U32, name="ent_codes0", align_bytes=64),
+            keep.tile([P, HALF], U32, name="ent_codes1", align_bytes=64),
+        ]
+        rel_pairs = [
+            keep.tile([P, HALF], U32, name="rel_pairs0", align_bytes=64),
+            loads.tile([P, HALF], U32, name="rel_pairs1", offset=late + 4 * HALF, align_bytes=64),
+        ]
+        rel_codes = [keep.tile([P, 2, 2 * HALF], U8, name="rel_codes%d" % e, align_bytes=64) for e in range(2)]
 
-        nc.sync.dma_start(rel_list[:], offs2)
-        for q in range(QUADS):
-            nc.scalar.dma_start(rel_scales[32 * q : 32 * q + 8, :], tab2_scales[:, 4 * q : 4 * q + 4, :].bitcast(I32))
-        load_weight("c0")
-        nc.sync.dma_start(ent_list[:], offs)
-        nc.sync.dma_start(rel_words[:], tab2_words[0].rearrange("p t i -> p (t i)").bitcast(I32))
-        for q in range(QUADS):
-            nc.scalar.dma_start(ent_scales[32 * q : 32 * q + 4, :], tab_scales[0, 4 * q : 4 * q + 4, :].bitcast(I32))
-        load_weight("c1")
-        nc.vector.tensor_copy(rel_sc[0][:].bitcast(U8), rel_scales[:].bitcast(U8).indirect(rel_list[:]))
-        for q in range(QUADS):
-            nc.sync.dma_start(rel_sc[1][32 * q : 32 * q + 4, :], rel_sc[0][32 * q + 4 : 32 * q + 8, :])
-        load_weight("a")
-        nc.vector.tensor_copy(ent_sc[:], ent_scales[:].bitcast(U8).indirect(ent_list[:]))
+        def gather_entities(e):
+            entries = ent_list[:, e * HALF // GROUP : (e + 1) * HALF // GROUP]
+            nc.vector.tensor_copy(ent_codes[e][:], ent_words[:].bitcast(U32).indirect(entries))
 
-        def gather_rel(half):
-            cols = slice(half * HALF, (half + 1) * HALF)
-            entries = rel_list[:, half * HALF // GROUP : (half + 1) * HALF // GROUP]
-            nc.vector.tensor_copy(rel_pairs[:, cols], rel_words[:].bitcast(U32).indirect(entries))
+        def gather_relations(e):
+            entries = rel_list[:, e * HALF // GROUP : (e + 1) * HALF // GROUP]
+            nc.vector.tensor_copy(rel_pairs[e][:], rel_words[:].bitcast(U32).indirect(entries))
+
+        def part_relations(e):
             nc.vector.tensor_copy(
-                rel_codes[:, :, 2 * half * HALF : 2 * (half + 1) * HALF].bitcast(U16),
-                rel_pairs[:, cols].bitcast(U16).rearrange("p (j a) -> p a j", a=2),
+                rel_codes[e][:].bitcast(U16), rel_pairs[e][:].bitcast(U16).rearrange("p (j a) -> p a j", a=2)
             )
 
-        w_codes = {name: keep.tile([P, R], U32, name="codes_" + name, align_bytes=64) for name in passes}
+        ent_sc = keep.tile([P, J], U8, name="ent_sc", align_bytes=64)
+        w_codes = {name: keep.tile([P, R], U32, name="codes_" + name, align_bytes=64) for name in passes if name != "b"}
+        w_codes["b"] = loads.tile([P, R], U32, name="codes_b", offset=4 * SLOT + SLOT // 2, align_bytes=64)
         w_scales = {name: keep.tile([P, R], U8, name="scales_" + name, align_bytes=64) for name in passes}
 
-        def quantize_weight(name, on_vector=0):
-            grouped = ring.tile([P, PACK * R], BF16, name="grouped", align_bytes=64)
+        def on_gpsimd(dst, src):
+            for e in range(PACK):
+                nc.gpsimd.tensor_scalar(dst[:, :, e, :], src[:, :, e, :], 1.0, 0.0, MULT, ADD)
+
+        on_scalar, on_vector = nc.scalar.copy, nc.vector.tensor_copy
+
+        placed = {"a": 9 * SLOT + SLOT // 2, "d1": 10 * SLOT + SLOT // 2, "c1": late}
+
+        def interleave(name, engines):
+            if name in placed:
+                grouped = loads.tile([P, PACK * R], BF16, name="grouped_" + name, offset=placed[name], align_bytes=64)
+            else:
+                grouped = ring.tile([P, PACK * R], BF16, name="grouped", align_bytes=64)
             dst = grouped[:].rearrange("p (t m e) -> p m e t", t=PACK, e=PACK)
-            src = raw[name][:].rearrange("p e (m t) -> p m e t", t=PACK)
-            on_scalar = P - on_vector
-            nc.scalar.copy(dst[:, :on_scalar], src[:, :on_scalar])
-            if on_vector:
-                nc.vector.tensor_copy(dst[:, on_scalar:], src[:, on_scalar:])
+            share = P // len(engines)
+            for part, copy in enumerate(engines):
+                src = raw[name][part][:].rearrange("p e (m t) -> p m e t", t=PACK)
+                copy(dst[:, part * share : (part + 1) * share], src)
+            return grouped
+
+        def quantize(name, grouped):
             nc.vector.quantize_mx(out=w_codes[name][:].bitcast(FP8X4), scales=w_scales[name][:], in_=grouped[:])
 
-        quantize_weight("c0")
-        ent_words = keep.tile([P, T], I32, name="ent_words", tag="slot_c0", align_bytes=64)
-        nc.sync.dma_start(ent_words[:], tab_words[0].rearrange("p t i -> p (t i)").bitcast(I32))
-        load_weight("b", 2)
-        gather_rel(0)
-        gather_rel(1)
-        quantize_weight("c1")
-        load_weight("d0", 2)
-        quantize_weight("a")
-        load_weight("d1", 2)
-        for half in range(2):
-            entries = ent_list[:, half * HALF // GROUP : (half + 1) * HALF // GROUP]
-            nc.vector.tensor_copy(
-                ent_codes[:, half * HALF : (half + 1) * HALF], ent_words[:].bitcast(U32).indirect(entries)
-            )
-        cand = keep.tile([P, 2, 3 * N // 4], I32, name="cand", tag="slot_c0", align_bytes=64)
-        nc.gpsimd.memset(cand[:, :, N // 2 :], 0)
-        for s, (cand_words, cand_scales) in enumerate(((nr_words, nr_scales), (ni_words, ni_scales))):
-            nc.sync.dma_start(cand[:, s, : N // 2], cand_words[0].bitcast(I32))
-            for q in range(QUADS):
-                nc.sync.dma_start(
-                    cand[32 * q : 32 * q + 4, s, N // 2 :], cand_scales[0, 4 * q : 4 * q + 4, :].bitcast(I32)
-                )
-        for name in ("b", "d0", "d1"):
-            quantize_weight(name, SHARED)
+        def quantize_weight(name, engines):
+            quantize(name, interleave(name, engines))
 
-        def project(tag, names, moving):
-            acc = psum.tile([P, PACK, CHUNK], F32, name=tag, tag=tag, bufs=BANKS)
+        nc.sync.dma_start(ent_list[:], offs)
+        nc.sync.dma_start(rel_list[:], offs2)
+        load_weight("a")
+        for q in range(QUADS):
+            nc.sync.dma_start(ent_scales[32 * q : 32 * q + 4, :], tab_scales[0, 4 * q : 4 * q + 4, :].bitcast(I32))
+        nc.sync.dma_start(ent_words[:], tab_words[0].rearrange("p t i -> p (t i)").bitcast(I32))
+        load_weight("b")
+        for q in range(QUADS):
+            nc.sync.dma_start(rel_held[32 * q : 32 * q + 8, : T // 4], tab2_scales[:, 4 * q : 4 * q + 4, :].bitcast(I32))
+        nc.sync.dma_start(rel_words[:], tab2_words[0].rearrange("p t i -> p (t i)").bitcast(I32))
+        load_weight("c0", 2)
+        load_weight("c1", 2)
+        nc.vector.tensor_copy(ent_sc[:], ent_scales[:].bitcast(U8).indirect(ent_list[:]))
+        gather_entities(0)
+        gather_entities(1)
+        quantize_weight("a", [on_scalar])
+        rel_sc0 = loads.tile([P, J // 4], I32, name="rel_sc0", offset=9 * SLOT + SLOT // 2, align_bytes=64)
+        rel_sc = [rel_sc0, rel_sc1]
+        nc.vector.tensor_copy(rel_sc0[:].bitcast(U8), rel_scales.bitcast(U8).indirect(rel_list[:]))
+        for q in range(QUADS):
+            nc.sync.dma_start(rel_sc1[32 * q : 32 * q + 4, :], rel_sc0[32 * q + 4 : 32 * q + 8, :])
+        load_weight("d0", 1)
+        load_weight("d1", 2)
+
+        def project(tag, names, moving, bank):
+            acc = psum.tile([P, PACK, CHUNK], F32, name=tag, offset=bank * BANK_BYTES)
             for t in range(PACK):
                 m = slice(t * P, (t + 1) * P)
                 for g, name in enumerate(names):
@@ -147,33 +169,72 @@ def tile_list_ckg_sig_kernel(
                     )
             return acc[:].rearrange("p t n -> p n t")
 
-        ent_first = keep.tile([P, 2, CHUNK, PACK], F32, name="ent_first", tag="slot_c1", align_bytes=64)
-        ent_next = keep.tile([P, 2, 2, CHUNK, PACK], F32, name="ent_next", tag="slot_rel", align_bytes=64)
-        held = [ent_first[:], ent_next[:, 0], ent_next[:, 1]]
+        half = SLOT // 2
+        first = [3 * SLOT, 3 * SLOT + half, 5 * SLOT]
+        place = first + [7 * SLOT, 7 * SLOT + half] + first
+        ent_sb = [
+            loads.tile([P, 2, CHUNK, PACK], F32, name="ent_sb%d" % i, offset=place[i], align_bytes=64) for i in range(8)
+        ]
+        with_arr = [
+            loads.tile([P, 2, CHUNK, PACK], F32, name="with_arr%d" % i, offset=10 * SLOT + (i - 1) * half)
+            if i == 2 else keep.tile([P, 2, CHUNK, PACK], F32, name="with_arr%d" % i)
+            for i in range(8)
+        ]
+        terms = {}
 
-        def complex_terms(i):
+        def entity_sum(i, s, bank):
             cols = slice(i * CHUNK, (i + 1) * CHUNK)
-            rel = [
-                (rel_codes[:, a, 2 * i * CHUNK : 2 * (i + 1) * CHUNK].bitcast(FP4X4), rel_sc[a][:].bitcast(U8)[:, cols])
+            within = slice(i % HALF_CHUNKS * CHUNK, (i % HALF_CHUNKS + 1) * CHUNK)
+            ent = [(ent_codes[i // HALF_CHUNKS][:, within].bitcast(FP8X4), ent_sc[:, cols])]
+            nc.scalar.copy(ent_sb[i][:, s], project("ent%d_%d" % (i, s), ("ab"[s],), ent, bank))
+
+        def relation(i):
+            cols = slice(i * CHUNK, (i + 1) * CHUNK)
+            within = slice(i % HALF_CHUNKS * 2 * CHUNK, (i % HALF_CHUNKS + 1) * 2 * CHUNK)
+            return [
+                (rel_codes[i // HALF_CHUNKS][:, a, within].bitcast(FP4X4), rel_sc[a][:].bitcast(U8)[:, cols])
                 for a in range(2)
             ]
-            ent = [(ent_codes[:, cols].bitcast(FP8X4), ent_sc[:, cols])]
-            ent_sb = held[i] if i < len(held) else ring.tile([P, 2, CHUNK, PACK], F32, name="ent_sb")[:]
-            aer, aei = ent_sb[:, 0], ent_sb[:, 1]
-            products = keep.tile([P, 4, CHUNK, PACK], F32, name="terms%d" % i)
-            nc.scalar.copy(aer, project("ent_acc", ("a",), ent))
-            nc.scalar.copy(aei, project("ent_acc", ("b",), ent))
-            arr = project("arr_acc", ("c0", "c1"), rel)
-            ari = project("ari_acc", ("d0", "d1"), rel)
-            if i < EARLY:
-                nc.vector.tensor_tensor(products[:, 0], arr, aer, MULT)
-                nc.vector.tensor_tensor(products[:, 1], arr, aei, MULT)
-            else:
-                arr_twice = arr.unsqueeze(1).to_broadcast([P, 2, CHUNK, PACK])
-                nc.vector.tensor_tensor(products[:, 0:2], arr_twice, ent_sb, MULT)
-            nc.vector.scalar_tensor_tensor(products[:, 2], ari, -1.0, aei, MULT, MULT)
-            nc.vector.tensor_tensor(products[:, 3], ari, aer, MULT)
-            return products[:].rearrange("p (g s) n t -> p g s (n t)", g=2)
+
+        def arr_terms(i):
+            arr = project("arr%d" % i, ("c0", "c1"), relation(i), 4 + i % 2)
+            nc.vector.tensor_tensor(
+                with_arr[i][:], arr.unsqueeze(1).to_broadcast([P, 2, CHUNK, PACK]), ent_sb[i][:], MULT
+            )
+
+        def ari_terms(i):
+            with_ari = ring.tile([P, 2, CHUNK, PACK], F32, name="with_ari", bufs=5)
+            ari = project("ari%d" % i, ("d0", "d1"), relation(i), 6 + i % 2)
+            nc.vector.scalar_tensor_tensor(with_ari[:, 0], ari, -1.0, ent_sb[i][:, 1], MULT, MULT)
+            nc.vector.tensor_tensor(with_ari[:, 1], ari, ent_sb[i][:, 0], MULT)
+            terms[i] = [x[:].rearrange("p s n t -> p s (n t)") for x in (with_arr[i], with_ari)]
+
+        gather_relations(0)
+        part_relations(0)
+        grouped_b = interleave("b", [on_scalar])
+        entity_sum(0, 0, 0)
+        entity_sum(1, 0, 1)
+        grouped_c0 = interleave("c0", [on_scalar, on_scalar])
+        cand = loads.tile([P, 2, N // 2], I32, name="cand", offset=4 * SLOT, align_bytes=64)
+        cand_sc = loads.tile([P, 2, N // 4], I32, name="cand_sc", offset=4 * SLOT + 4 * N, align_bytes=64)
+        nc.gpsimd.memset(cand_sc[:], 0)
+        for s, (cand_words, cand_scales) in enumerate(((nr_words, nr_scales), (ni_words, ni_scales))):
+            nc.sync.dma_start(cand[:, s, :], cand_words[0].bitcast(I32))
+            for q in range(QUADS):
+                nc.sync.dma_start(cand_sc[32 * q : 32 * q + 4, s, :], cand_scales[0, 4 * q : 4 * q + 4, :].bitcast(I32))
+
+        quantize("b", grouped_b)
+        quantize("c0", grouped_c0)
+        quantize_weight("c1", [on_scalar, on_vector])
+        gather_relations(1)
+        part_relations(1)
+        entity_sum(2, 0, 2)
+        for i in range(3):
+            entity_sum(i, 1, (3 + i) % 4)
+        arr_terms(0)
+        arr_terms(1)
+        quantize_weight("d0", [on_scalar])
+        quantize_weight("d1", [on_scalar,on_vector])
 
         def quantize_h(h, columns, name):
             h_codes = keep.tile([P, columns], U32, name="codes_" + name, align_bytes=64)
@@ -191,26 +252,37 @@ def tile_list_ckg_sig_kernel(
                 nc.tensor.matmul_mx(
                     out=y,
                     lhsT=cand[:, s, :].bitcast(U8)[:, 2 * u * P : 2 * (u + 1) * P].bitcast(FP4X4),
-                    lhsT_scale=cand[:, s, :].bitcast(U8)[:, 2 * N + u * P : 2 * N + (u + 1) * P],
+                    lhsT_scale=cand_sc[:, s, :].bitcast(U8)[:, u * P : (u + 1) * P],
                     rhs=h_codes.bitcast(FP8X4), rhs_scale=h_scales, start=(s == 0), stop=(s == 1),
                 )
 
         def score_chunk(i, operands):
-            y = psum.tile([P, N // P, CHUNK], F32, name="y", tag="y", bufs=BANKS)
+            y = psum.tile([P, N // P, CHUNK], F32, name="y%d" % i, offset=i % 4 * BANK_BYTES)
             for u in range(N // P):
                 score(y[:, u, :], u, operands)
             result = ring.tile([P, N // P, CHUNK], F32, name="result", tag="result")
             nc.scalar.activation(result[:], y[:], SIGMOID)
             nc.sync.dma_start(out[:, i * CHUNK : (i + 1) * CHUNK].rearrange("(u p) j -> p u j", p=P), result[:])
 
-        terms = [complex_terms(0)]
+        def both_sums(i):
+            for s in range(2):
+                entity_sum(i, s, 2 * ((i + 1) % 2) + s)
+
         h_half = keep.tile([P, 2, HALF_CHUNKS, WIDE], BF16, name="h_half", tag="h", align_bytes=64)
-        for i in range(HALF_CHUNKS):
-            nc.gpsimd.tensor_tensor(h_half[:, :, i, :], terms[i][:, 0], terms[i][:, 1], ADD)
-            terms.append(complex_terms(i + 1))
+        both_sums(3)
+        both_sums(4)
+        arr_terms(2)
+        for i in range(6):
+            if i >= 3:
+                arr_terms(i)
+            ari_terms(i)
+            if i < 3:
+                both_sums(5 + i)
+            if i < HALF_CHUNKS:
+                nc.gpsimd.tensor_tensor(h_half[:, :, i, :], terms[i][0], terms[i][1], ADD)
         operands = hr_hi(quantize_h(h_half[:].rearrange("p s i w -> p (s i w)"), 2 * HALF, "half"), 0, HALF)
         for u in range(N // P):
-            y_half = psum.tile([P, HALF], F32, name="y_half", tag="y", bufs=BANKS)
+            y_half = psum.tile([P, HALF], F32, name="y_half%d" % u, offset=u * BANK_BYTES)
             score(y_half[:], u, operands)
             result_half = ring.tile([P, HALF], F32, name="result_half", tag="result")
             nc.scalar.activation(result_half[:], y_half[:], SIGMOID)
@@ -218,20 +290,18 @@ def tile_list_ckg_sig_kernel(
 
         h_pair = keep.tile([P, 2, 2, WIDE], BF16, name="h_pair", tag="h", align_bytes=64)
         for e in range(2):
-            i = HALF_CHUNKS + e
-            nc.gpsimd.tensor_tensor(h_pair[:, e], terms[i][:, 0], terms[i][:, 1], ADD)
-            terms.append(complex_terms(i + 1))
-        before_last, last = HALF_CHUNKS + 2, HALF_CHUNKS + 3
-        terms.append(complex_terms(last))
+            nc.gpsimd.tensor_tensor(h_pair[:, e], terms[4 + e][0], terms[4 + e][1], ADD)
+            arr_terms(6 + e)
+            ari_terms(6 + e)
         pair = quantize_h(h_pair[:].rearrange("p e s w -> p (e s w)"), 4 * CHUNK, "pair")
         for e in range(2):
-            score_chunk(HALF_CHUNKS + e, hr_hi(pair, 2 * e * CHUNK, CHUNK))
+            score_chunk(4 + e, hr_hi(pair, 2 * e * CHUNK, CHUNK))
 
         h_last = keep.tile([P, 2, 2, WIDE], BF16, name="h_last", align_bytes=64)
-        nc.vector.tensor_tensor(h_last[:, 0], terms[before_last][:, 0], terms[before_last][:, 1], ADD)
-        nc.vector.tensor_tensor(h_last[:, 1, 0], terms[last][:, 0, 0], terms[last][:, 1, 0], ADD)
+        nc.vector.tensor_tensor(h_last[:, 0], terms[6][0], terms[6][1], ADD)
+        nc.vector.tensor_tensor(h_last[:, 1, 0], terms[7][0][:, 0], terms[7][1][:, 0], ADD)
         single = quantize_h(h_last[:, 0].rearrange("p s w -> p (s w)"), 2 * CHUNK, "six")
-        score_chunk(before_last, hr_hi(single, 0, CHUNK))
-        nc.vector.tensor_tensor(h_last[:, 1, 1], terms[last][:, 0, 1], terms[last][:, 1, 1], ADD)
+        score_chunk(6, hr_hi(single, 0, CHUNK))
+        nc.vector.tensor_tensor(h_last[:, 1, 1], terms[7][0][:, 1], terms[7][1][:, 1], ADD)
         apart = [quantize_h(h_last[:, 1, s], CHUNK, "seven%d" % s) for s in range(2)]
-        score_chunk(last, [(h_codes[:], h_scales[:]) for h_codes, h_scales in apart])
+        score_chunk(7, [(h_codes[:], h_scales[:]) for h_codes, h_scales in apart])

@@ -49,13 +49,19 @@ def tile_list_ckg_sig_kernel(
 
         SLOT = 4 * T
         BANK_BYTES = 2048
-        zeros = loads.tile([P, 5 * T], I32, name="zeros", offset=SLOT, align_bytes=64)
+        TURNED = (3, 5)
+        ones = loads.tile([P, 6 * T], F32, name="ones", offset=SLOT, align_bytes=64)
         rel_held = loads.tile([P, 3 * T // 4], I32, name="rel_held", offset=7 * SLOT - T // 2, align_bytes=64)
         rel_scales = rel_held[:, : T // 4]
-        nc.vector.memset(ent_scales[:], 0)
-        nc.gpsimd.memset(zeros[:, : J // 4], 0)
+        nc.gpsimd.memset(ent_scales[:], 0)
+        identity = keep.tile([P, P], F32, name="identity")
+        nc.gpsimd.memset(ones[:, :P], 1.0)
+        nc.gpsimd.affine_select(
+            out=identity[:], in_=ones[:, :P], pattern=[[-1, P]], compare_op=mybir.AluOpType.is_equal,
+            fill=0.0, base=0, channel_multiplier=1,
+        )
         nc.gpsimd.memset(rel_scales, 0)
-        nc.vector.tensor_copy(rel_sc1[:], zeros[:, : J // 4])
+        nc.vector.memset(rel_sc1[:], 0)
 
         ent_words = loads.tile([P, T], I32, name="ent_words", offset=2 * SLOT, align_bytes=64)
         rel_words = loads.tile([P, T], I32, name="rel_words", offset=SLOT, align_bytes=64)
@@ -103,8 +109,7 @@ def tile_list_ckg_sig_kernel(
             )
 
         ent_sc = keep.tile([P, J], U8, name="ent_sc", align_bytes=64)
-        w_codes = {name: keep.tile([P, R], U32, name="codes_" + name, align_bytes=64) for name in passes if name != "b"}
-        w_codes["b"] = loads.tile([P, R], U32, name="codes_b", offset=4 * SLOT + SLOT // 2, align_bytes=64)
+        w_codes = {name: keep.tile([P, R], U32, name="codes_" + name, align_bytes=64) for name in passes}
         w_scales = {name: keep.tile([P, R], U8, name="scales_" + name, align_bytes=64) for name in passes}
 
         def on_gpsimd(dst, src):
@@ -113,7 +118,7 @@ def tile_list_ckg_sig_kernel(
 
         on_scalar, on_vector = nc.scalar.copy, nc.vector.tensor_copy
 
-        placed = {"a": 9 * SLOT + SLOT // 2, "d1": 10 * SLOT + SLOT // 2, "c1": late}
+        placed = {"a": 9 * SLOT + SLOT // 2, "d1": 10 * SLOT, "c1": late}
 
         def interleave(name, engines):
             if name in placed:
@@ -123,8 +128,8 @@ def tile_list_ckg_sig_kernel(
             dst = grouped[:].rearrange("p (t m e) -> p m e t", t=PACK, e=PACK)
             share = P // len(engines)
             for part, copy in enumerate(engines):
-                src = raw[name][part][:].rearrange("p e (m t) -> p m e t", t=PACK)
-                copy(dst[:, part * share : (part + 1) * share], src)
+                src = raw[name][0][:].rearrange("p e (m t) -> p m e t", t=PACK)
+                copy(dst[:, part * share : (part + 1) * share], src[:, part * share : (part + 1) * share])
             return grouped
 
         def quantize(name, grouped):
@@ -143,8 +148,8 @@ def tile_list_ckg_sig_kernel(
         for q in range(QUADS):
             nc.sync.dma_start(rel_held[32 * q : 32 * q + 8, : T // 4], tab2_scales[:, 4 * q : 4 * q + 4, :].bitcast(I32))
         nc.sync.dma_start(rel_words[:], tab2_words[0].rearrange("p t i -> p (t i)").bitcast(I32))
-        load_weight("c0", 2)
-        load_weight("c1", 2)
+        load_weight("c0")
+        load_weight("c1")
         nc.vector.tensor_copy(ent_sc[:], ent_scales[:].bitcast(U8).indirect(ent_list[:]))
         gather_entities(0)
         gather_entities(1)
@@ -155,9 +160,19 @@ def tile_list_ckg_sig_kernel(
         for q in range(QUADS):
             nc.sync.dma_start(rel_sc1[32 * q : 32 * q + 4, :], rel_sc0[32 * q + 4 : 32 * q + 8, :])
         load_weight("d0", 1)
-        load_weight("d1", 2)
+        load_weight("d1")
 
-        def project(tag, names, moving, bank):
+        def project(tag, names, moving, bank, turned=False):
+            if turned:
+                wide = psum.tile([P, R], F32, name=tag, offset=bank * BANK_BYTES)
+                for g, name in enumerate(names):
+                    table_codes, table_scales = moving[g]
+                    nc.tensor.matmul_mx(
+                        out=wide[:], lhsT=table_codes, lhsT_scale=table_scales,
+                        rhs=w_codes[name][:].bitcast(FP8X4), rhs_scale=w_scales[name][:],
+                        start=(g == 0), stop=(g == len(names) - 1),
+                    )
+                return wide[:].rearrange("p (n t) -> p n t", t=PACK)
             acc = psum.tile([P, PACK, CHUNK], F32, name=tag, offset=bank * BANK_BYTES)
             for t in range(PACK):
                 m = slice(t * P, (t + 1) * P)
@@ -170,14 +185,26 @@ def tile_list_ckg_sig_kernel(
             return acc[:].rearrange("p t n -> p n t")
 
         half = SLOT // 2
-        first = [3 * SLOT, 3 * SLOT + half, 5 * SLOT]
-        place = first + [7 * SLOT, 7 * SLOT + half] + first
-        ent_sb = [
-            loads.tile([P, 2, CHUNK, PACK], F32, name="ent_sb%d" % i, offset=place[i], align_bytes=64) for i in range(8)
+        quarter = SLOT // 4
+        place = [7 * SLOT, 7 * SLOT + half, 8 * SLOT, 8 * SLOT + half, 9 * SLOT, 0]
+        apart_sb = [
+            [
+                loads.tile([P, CHUNK, PACK], F32, name="ent%d_%d" % (i, s), offset=(3 + 2 * s) * SLOT + i * quarter)
+                for s in range(2)
+            ]
+            for i in range(EARLY)
         ]
+        ent_sb = {
+            i: loads.tile([P, 2, CHUNK, PACK], F32, name="ent_sb%d" % i, offset=place[i - EARLY])
+            for i in range(EARLY, 8)
+        }
+
+        def entity(i, s):
+            return apart_sb[i][s][:] if i < EARLY else ent_sb[i][:, s]
+
         with_arr = [
             loads.tile([P, 2, CHUNK, PACK], F32, name="with_arr%d" % i, offset=10 * SLOT + (i - 1) * half)
-            if i == 2 else keep.tile([P, 2, CHUNK, PACK], F32, name="with_arr%d" % i)
+            if i == 1 else keep.tile([P, 2, CHUNK, PACK], F32, name="with_arr%d" % i)
             for i in range(8)
         ]
         terms = {}
@@ -186,7 +213,7 @@ def tile_list_ckg_sig_kernel(
             cols = slice(i * CHUNK, (i + 1) * CHUNK)
             within = slice(i % HALF_CHUNKS * CHUNK, (i % HALF_CHUNKS + 1) * CHUNK)
             ent = [(ent_codes[i // HALF_CHUNKS][:, within].bitcast(FP8X4), ent_sc[:, cols])]
-            nc.scalar.copy(ent_sb[i][:, s], project("ent%d_%d" % (i, s), ("ab"[s],), ent, bank))
+            nc.scalar.copy(entity(i, s), project("ent%d_%d" % (i, s), ("ab"[s],), ent, bank, i in TURNED))
 
         def relation(i):
             cols = slice(i * CHUNK, (i + 1) * CHUNK)
@@ -196,25 +223,36 @@ def tile_list_ckg_sig_kernel(
                 for a in range(2)
             ]
 
+        sums = {}
+
+        def arr_sum(i):
+            sums["arr", i] = project("arr%d" % i, ("c0", "c1"), relation(i), 4 + i % 2, i in TURNED)
+
+        def ari_sum(i):
+            sums["ari", i] = project("ari%d" % i, ("d0", "d1"), relation(i), 6 + i % 2, i in TURNED)
+
         def arr_terms(i):
-            arr = project("arr%d" % i, ("c0", "c1"), relation(i), 4 + i % 2)
-            nc.vector.tensor_tensor(
-                with_arr[i][:], arr.unsqueeze(1).to_broadcast([P, 2, CHUNK, PACK]), ent_sb[i][:], MULT
-            )
+            arr = sums["arr", i]
+            if i < EARLY:
+                for s in range(2):
+                    nc.vector.tensor_tensor(with_arr[i][:, s], arr, entity(i, s), MULT)
+            else:
+                arr_twice = arr.unsqueeze(1).to_broadcast([P, 2, CHUNK, PACK])
+                nc.vector.tensor_tensor(with_arr[i][:], arr_twice, ent_sb[i][:], MULT)
 
         def ari_terms(i):
             with_ari = ring.tile([P, 2, CHUNK, PACK], F32, name="with_ari", bufs=5)
-            ari = project("ari%d" % i, ("d0", "d1"), relation(i), 6 + i % 2)
-            nc.vector.scalar_tensor_tensor(with_ari[:, 0], ari, -1.0, ent_sb[i][:, 1], MULT, MULT)
-            nc.vector.tensor_tensor(with_ari[:, 1], ari, ent_sb[i][:, 0], MULT)
+            ari = sums["ari", i]
+            nc.vector.scalar_tensor_tensor(with_ari[:, 0], ari, -1.0, entity(i, 1), MULT, MULT)
+            nc.vector.tensor_tensor(with_ari[:, 1], ari, entity(i, 0), MULT)
             terms[i] = [x[:].rearrange("p s n t -> p s (n t)") for x in (with_arr[i], with_ari)]
 
         gather_relations(0)
         part_relations(0)
-        grouped_b = interleave("b", [on_scalar])
+        quantize_weight("b", [on_scalar])
         entity_sum(0, 0, 0)
         entity_sum(1, 0, 1)
-        grouped_c0 = interleave("c0", [on_scalar, on_scalar])
+        grouped_c0 = interleave("c0", [on_scalar])
         cand = loads.tile([P, 2, N // 2], I32, name="cand", offset=4 * SLOT, align_bytes=64)
         cand_sc = loads.tile([P, 2, N // 4], I32, name="cand_sc", offset=4 * SLOT + 4 * N, align_bytes=64)
         nc.gpsimd.memset(cand_sc[:], 0)
@@ -223,16 +261,16 @@ def tile_list_ckg_sig_kernel(
             for q in range(QUADS):
                 nc.sync.dma_start(cand_sc[32 * q : 32 * q + 4, s, :], cand_scales[0, 4 * q : 4 * q + 4, :].bitcast(I32))
 
-        quantize("b", grouped_b)
         quantize("c0", grouped_c0)
         quantize_weight("c1", [on_scalar, on_vector])
         gather_relations(1)
         part_relations(1)
-        entity_sum(2, 0, 2)
-        for i in range(3):
-            entity_sum(i, 1, (3 + i) % 4)
+        entity_sum(0, 1, 2)
+        entity_sum(1, 1, 3)
+        arr_sum(0)
+        arr_sum(1)
         arr_terms(0)
-        arr_terms(1)
+        arr_sum(2)
         quantize_weight("d0", [on_scalar])
         quantize_weight("d1", [on_scalar,on_vector])
 
@@ -257,48 +295,75 @@ def tile_list_ckg_sig_kernel(
                 )
 
         def score_chunk(i, operands):
-            y = psum.tile([P, N // P, CHUNK], F32, name="y%d" % i, offset=i % 4 * BANK_BYTES)
+            y = psum.tile([P, N // P, CHUNK], F32, name="y%d" % i, offset=(i + 2) % 4 * BANK_BYTES)
             for u in range(N // P):
                 score(y[:, u, :], u, operands)
-            result = ring.tile([P, N // P, CHUNK], F32, name="result", tag="result")
+            result = ring.tile([P, N // P, CHUNK], F32, name="result", tag="result", bufs=8)
             nc.scalar.activation(result[:], y[:], SIGMOID)
             nc.sync.dma_start(out[:, i * CHUNK : (i + 1) * CHUNK].rearrange("(u p) j -> p u j", p=P), result[:])
 
+        def add_turned(i, banks):
+            totals = []
+            for s in range(2):
+                total = psum.tile([P, PACK, CHUNK], F32, name="sum%d_%d" % (i, s), offset=banks[s] * BANK_BYTES)
+                for t in range(PACK):
+                    for g in range(2):
+                        nc.tensor.matmul(
+                            total[:, t, :], terms[i][g][:, s, t * P : (t + 1) * P], identity[:],
+                            start=(g == 0), stop=(g == 1), is_transpose=True,
+                        )
+                totals.append(total)
+            return totals
+
+        def round_sums(h, totals):
+            for s, total in enumerate(totals):
+                nc.scalar.copy(h[:, s].rearrange("p (n t) -> p n t", t=PACK), total[:].rearrange("p t n -> p n t"))
+
         def both_sums(i):
             for s in range(2):
-                entity_sum(i, s, 2 * ((i + 1) % 2) + s)
+                entity_sum(i, s, 2 * (i % 2) + s)
 
         h_half = keep.tile([P, 2, HALF_CHUNKS, WIDE], BF16, name="h_half", tag="h", align_bytes=64)
-        both_sums(3)
-        both_sums(4)
-        arr_terms(2)
-        for i in range(6):
-            if i >= 3:
+        ari_sum(0)
+        ari_sum(1)
+        both_sums(2)
+        arr_terms(1)
+        arr_sum(3)
+
+        def products(i):
+            if i >= EARLY:
                 arr_terms(i)
+                if i + 2 < 8:
+                    arr_sum(i + 2)
             ari_terms(i)
+            if i + 2 < 8:
+                ari_sum(i + 2)
+
+        for i in range(5):
+            products(i)
+            both_sums(3 + i)
             if i < 3:
-                both_sums(5 + i)
-            if i < HALF_CHUNKS:
                 nc.gpsimd.tensor_tensor(h_half[:, :, i, :], terms[i][0], terms[i][1], ADD)
+            if i == 3:
+                round_sums(h_half[:, :, i, :], add_turned(i, (2, 3)))
         operands = hr_hi(quantize_h(h_half[:].rearrange("p s i w -> p (s i w)"), 2 * HALF, "half"), 0, HALF)
+        h_pair = keep.tile([P, 2, 2, WIDE], BF16, name="h_pair", tag="h", align_bytes=64)
+        nc.gpsimd.tensor_tensor(h_pair[:, 0], terms[4][0], terms[4][1], ADD)
+        products(5)
+        round_sums(h_pair[:, 1], add_turned(5, (0, 1)))
         for u in range(N // P):
-            y_half = psum.tile([P, HALF], F32, name="y_half%d" % u, offset=u * BANK_BYTES)
+            y_half = psum.tile([P, HALF], F32, name="y_half%d" % u, offset=(u + 2) % 4 * BANK_BYTES)
             score(y_half[:], u, operands)
-            result_half = ring.tile([P, HALF], F32, name="result_half", tag="result")
+            result_half = ring.tile([P, HALF], F32, name="result_half", tag="result", bufs=8)
             nc.scalar.activation(result_half[:], y_half[:], SIGMOID)
             nc.sync.dma_start(out[u * P : (u + 1) * P, :HALF], result_half[:])
-
-        h_pair = keep.tile([P, 2, 2, WIDE], BF16, name="h_pair", tag="h", align_bytes=64)
-        for e in range(2):
-            nc.gpsimd.tensor_tensor(h_pair[:, e], terms[4 + e][0], terms[4 + e][1], ADD)
-            arr_terms(6 + e)
-            ari_terms(6 + e)
+        products(6)
+        h_last = keep.tile([P, 2, 2, WIDE], BF16, name="h_last", align_bytes=64)
+        nc.gpsimd.tensor_tensor(h_last[:, 0], terms[6][0], terms[6][1], ADD)
+        products(7)
         pair = quantize_h(h_pair[:].rearrange("p e s w -> p (e s w)"), 4 * CHUNK, "pair")
         for e in range(2):
             score_chunk(4 + e, hr_hi(pair, 2 * e * CHUNK, CHUNK))
-
-        h_last = keep.tile([P, 2, 2, WIDE], BF16, name="h_last", align_bytes=64)
-        nc.vector.tensor_tensor(h_last[:, 0], terms[6][0], terms[6][1], ADD)
         nc.vector.tensor_tensor(h_last[:, 1, 0], terms[7][0][:, 0], terms[7][1][:, 0], ADD)
         single = quantize_h(h_last[:, 0].rearrange("p s w -> p (s w)"), 2 * CHUNK, "six")
         score_chunk(6, hr_hi(single, 0, CHUNK))

@@ -28,7 +28,7 @@ HALF = J // 2
 HALF_CHUNKS = HALF // CHUNK
 SHARED = P // 2
 BANKS = 2
-EARLY = 2
+EARLY = 4
 
 
 def tile_list_ckg_sig_kernel(
@@ -45,32 +45,35 @@ def tile_list_ckg_sig_kernel(
         ent_list = keep.tile([P, J // GROUP], U16, name="ent_list")
         rel_list = keep.tile([P, J // GROUP], U16, name="rel_list")
         ent_scales = keep.tile([P, T // 4], I32, name="ent_scales", align_bytes=64)
-        rel_sc1 = keep.tile([P, J // 4], I32, name="rel_sc1", align_bytes=64)
 
         SLOT = 4 * T
         BANK_BYTES = 2048
-        TURNED = (3, 5)
-        ones = loads.tile([P, 6 * T], F32, name="ones", offset=SLOT, align_bytes=64)
-        rel_held = loads.tile([P, 3 * T // 4], I32, name="rel_held", offset=7 * SLOT - T // 2, align_bytes=64)
-        rel_scales = rel_held[:, : T // 4]
-        nc.gpsimd.memset(ent_scales[:], 0)
+        TURNED = (3, 6)
+        ones = loads.tile([P, 7 * T + J // 4], F32, name="ones", offset=0, align_bytes=64)
+        LIP = 16
+        MID = 7 * SLOT + J
+        GAP = 3 * SLOT // 4
+        rel_held = loads.tile([P, GAP // 4 + 2 * LIP], I32, name="rel_held", offset=MID - 4 * LIP, align_bytes=64)
+        rel_scales = rel_held[:, LIP : LIP + T // 4]
+        nc.vector.memset(ent_scales[:], 0)
         identity = keep.tile([P, P], F32, name="identity")
         nc.gpsimd.memset(ones[:, :P], 1.0)
         nc.gpsimd.affine_select(
             out=identity[:], in_=ones[:, :P], pattern=[[-1, P]], compare_op=mybir.AluOpType.is_equal,
             fill=0.0, base=0, channel_multiplier=1,
         )
-        nc.gpsimd.memset(rel_scales, 0)
-        nc.vector.memset(rel_sc1[:], 0)
+        nc.gpsimd.memset(rel_held[:, LIP : LIP + T // 4 + N // 2], 0)
+        zeros = loads.tile([P, 5 * T], I32, name="zeros", offset=SLOT, align_bytes=64)
+        nc.gpsimd.memset(zeros[:, : J // 4], 0)
 
-        ent_words = loads.tile([P, T], I32, name="ent_words", offset=2 * SLOT, align_bytes=64)
-        rel_words = loads.tile([P, T], I32, name="rel_words", offset=SLOT, align_bytes=64)
+        ent_words = loads.tile([P, T], I32, name="ent_words", offset=2 * SLOT + J, align_bytes=64)
+        rel_words = loads.tile([P, T], I32, name="rel_words", offset=SLOT + J, align_bytes=64)
         passes = {
             "a": wer, "b": wei,
             "c0": wrr[:K_PASS, :], "c1": wrr[K_PASS:, :], "d0": wri[:K_PASS, :], "d1": wri[K_PASS:, :],
         }
         raw = {}
-        slot = {"a": 0, "b": 3, "c0": 4, "c1": 5, "d0": 6, "d1": 7}
+        slot = {"a": 0, "b": 3 * SLOT + J, "c0": 4 * SLOT + J, "c1": 5 * SLOT + J, "d0": MID - SLOT, "d1": MID + GAP}
 
         def load_weight(name, parts=1, only=None):
             rows = passes[name].rearrange("(p e) r -> p e r", e=PACK)
@@ -79,7 +82,7 @@ def tile_list_ckg_sig_kernel(
             for part in range(parts) if only is None else [only]:
                 piece = loads.tile(
                     [P, PACK, width], F32, name="raw_%s_%d" % (name, part), align_bytes=64,
-                    offset=slot[name] * SLOT + part * SLOT // parts,
+                    offset=slot[name] + part * SLOT // parts,
                 )
                 nc.sync.dma_start(piece[:], rows[:, :, part * width : (part + 1) * width])
                 raw[name].append(piece)
@@ -87,13 +90,16 @@ def tile_list_ckg_sig_kernel(
         late = 11 * SLOT
         ent_codes = [
             keep.tile([P, HALF], U32, name="ent_codes0", align_bytes=64),
-            keep.tile([P, HALF], U32, name="ent_codes1", align_bytes=64),
+            loads.tile([P, HALF], U32, name="ent_codes1", offset=late + SLOT, align_bytes=64),
         ]
         rel_pairs = [
             keep.tile([P, HALF], U32, name="rel_pairs0", align_bytes=64),
-            loads.tile([P, HALF], U32, name="rel_pairs1", offset=late + 4 * HALF, align_bytes=64),
+            keep.tile([P, HALF], U32, name="rel_pairs1", align_bytes=64),
         ]
-        rel_codes = [keep.tile([P, 2, 2 * HALF], U8, name="rel_codes%d" % e, align_bytes=64) for e in range(2)]
+        rel_codes = [
+            keep.tile([P, 2, 2 * HALF], U8, name="rel_codes0", align_bytes=64),
+            loads.tile([P, 2, 2 * HALF], U8, name="rel_codes1", offset=late + SLOT // 2, align_bytes=64),
+        ]
 
         def gather_entities(e):
             entries = ent_list[:, e * HALF // GROUP : (e + 1) * HALF // GROUP]
@@ -118,18 +124,18 @@ def tile_list_ckg_sig_kernel(
 
         on_scalar, on_vector = nc.scalar.copy, nc.vector.tensor_copy
 
-        placed = {"a": 9 * SLOT + SLOT // 2, "d1": 10 * SLOT, "c1": late}
+        placed = {"a": late - SLOT // 2, "b": late + SLOT, "c0": late - SLOT // 2, "d1": late, "c1": late + SLOT // 2}
 
-        def interleave(name, engines):
+        def interleave(name, engines, first=P // 2):
             if name in placed:
                 grouped = loads.tile([P, PACK * R], BF16, name="grouped_" + name, offset=placed[name], align_bytes=64)
             else:
-                grouped = ring.tile([P, PACK * R], BF16, name="grouped", align_bytes=64)
+                grouped = ring.tile([P, PACK * R], BF16, name="grouped", align_bytes=64, bufs=1)
             dst = grouped[:].rearrange("p (t m e) -> p m e t", t=PACK, e=PACK)
-            share = P // len(engines)
-            for part, copy in enumerate(engines):
-                src = raw[name][0][:].rearrange("p e (m t) -> p m e t", t=PACK)
-                copy(dst[:, part * share : (part + 1) * share], src[:, part * share : (part + 1) * share])
+            src = raw[name][0][:].rearrange("p e (m t) -> p m e t", t=PACK)
+            shares = [slice(0, P)] if len(engines) == 1 else [slice(0, first), slice(first, P)]
+            for share, copy in zip(shares, engines):
+                copy(dst[:, share], src[:, share])
             return grouped
 
         def quantize(name, grouped):
@@ -140,27 +146,33 @@ def tile_list_ckg_sig_kernel(
 
         nc.sync.dma_start(ent_list[:], offs)
         nc.sync.dma_start(rel_list[:], offs2)
-        load_weight("a")
         for q in range(QUADS):
             nc.sync.dma_start(ent_scales[32 * q : 32 * q + 4, :], tab_scales[0, 4 * q : 4 * q + 4, :].bitcast(I32))
+        load_weight("a")
+        for q in range(QUADS):
+            nc.sync.dma_start(rel_held[32 * q : 32 * q + 8, LIP : LIP + T // 4], tab2_scales[:, 4 * q : 4 * q + 4, :].bitcast(I32))
         nc.sync.dma_start(ent_words[:], tab_words[0].rearrange("p t i -> p (t i)").bitcast(I32))
         load_weight("b")
-        for q in range(QUADS):
-            nc.sync.dma_start(rel_held[32 * q : 32 * q + 8, : T // 4], tab2_scales[:, 4 * q : 4 * q + 4, :].bitcast(I32))
         nc.sync.dma_start(rel_words[:], tab2_words[0].rearrange("p t i -> p (t i)").bitcast(I32))
         load_weight("c0")
         load_weight("c1")
         nc.vector.tensor_copy(ent_sc[:], ent_scales[:].bitcast(U8).indirect(ent_list[:]))
-        gather_entities(0)
-        gather_entities(1)
-        quantize_weight("a", [on_scalar])
-        rel_sc0 = loads.tile([P, J // 4], I32, name="rel_sc0", offset=9 * SLOT + SLOT // 2, align_bytes=64)
+        rel_sc0 = keep.tile([P, J // 4], I32, name="rel_sc0", align_bytes=64)
+        rel_sc1 = loads.tile([P, J // 4], I32, name="rel_sc1", offset=SLOT, align_bytes=64)
         rel_sc = [rel_sc0, rel_sc1]
         nc.vector.tensor_copy(rel_sc0[:].bitcast(U8), rel_scales.bitcast(U8).indirect(rel_list[:]))
+        quantize_weight("a", [on_scalar])
+        gather_entities(0)
         for q in range(QUADS):
             nc.sync.dma_start(rel_sc1[32 * q : 32 * q + 4, :], rel_sc0[32 * q + 4 : 32 * q + 8, :])
         load_weight("d0", 1)
         load_weight("d1")
+        cand_sc = loads.tile([P, 2, N // 4], I32, name="cand_sc", offset=MID + T, align_bytes=64)
+        cand = loads.tile([P, 2, N // 2], I32, name="cand", offset=MID + T + 2 * N, align_bytes=64)
+        for s, (cand_words, cand_scales) in enumerate(((nr_words, nr_scales), (ni_words, ni_scales))):
+            nc.sync.dma_start(cand[:, s, :], cand_words[0].bitcast(I32))
+            for q in range(QUADS):
+                nc.sync.dma_start(cand_sc[32 * q : 32 * q + 4, s, :], cand_scales[0, 4 * q : 4 * q + 4, :].bitcast(I32))
 
         def project(tag, names, moving, bank, turned=False):
             if turned:
@@ -174,22 +186,29 @@ def tile_list_ckg_sig_kernel(
                     )
                 return wide[:].rearrange("p (n t) -> p n t", t=PACK)
             acc = psum.tile([P, PACK, CHUNK], F32, name=tag, offset=bank * BANK_BYTES)
-            for t in range(PACK):
-                m = slice(t * P, (t + 1) * P)
-                for g, name in enumerate(names):
-                    table_codes, table_scales = moving[g]
+            for g, name in enumerate(names):
+                table_codes, table_scales = moving[g]
+                for t in range(PACK):
+                    m = slice(t * P, (t + 1) * P)
                     nc.tensor.matmul_mx(
                         out=acc[:, t, :], lhsT=w_codes[name][:, m].bitcast(FP8X4), lhsT_scale=w_scales[name][:, m],
-                        rhs=table_codes, rhs_scale=table_scales, start=(g == 0), stop=(g == len(names) - 1),
+                        rhs=table_codes, rhs_scale=table_scales,
+                        start=(g == 0 and t == 0), stop=(g == len(names) - 1 and t == PACK - 1),
                     )
             return acc[:].rearrange("p t n -> p n t")
 
         half = SLOT // 2
         quarter = SLOT // 4
-        place = [7 * SLOT, 7 * SLOT + half, 8 * SLOT, 8 * SLOT + half, 9 * SLOT, 0]
+        place = [slot["d1"], slot["d1"] + half, 9 * SLOT, 9 * SLOT + half]
+
+        def early_at(i, s):
+            if i == EARLY - 1:
+                return slot[("c0", "c1")[s]]
+            return slot[("b", "a")[s]] + i * quarter
+
         apart_sb = [
             [
-                loads.tile([P, CHUNK, PACK], F32, name="ent%d_%d" % (i, s), offset=(3 + 2 * s) * SLOT + i * quarter)
+                loads.tile([P, CHUNK, PACK], F32, name="ent%d_%d" % (i, s), offset=early_at(i, s))
                 for s in range(2)
             ]
             for i in range(EARLY)
@@ -202,11 +221,20 @@ def tile_list_ckg_sig_kernel(
         def entity(i, s):
             return apart_sb[i][s][:] if i < EARLY else ent_sb[i][:, s]
 
-        with_arr = [
-            loads.tile([P, 2, CHUNK, PACK], F32, name="with_arr%d" % i, offset=10 * SLOT + (i - 1) * half)
-            if i == 1 else keep.tile([P, 2, CHUNK, PACK], F32, name="with_arr%d" % i)
-            for i in range(8)
+        held = {4: slot["c0"], 6: slot["d0"] + half}
+        with_arr = {
+            i: loads.tile([P, 2, CHUNK, PACK], F32, name="with_arr%d" % i, offset=held[i])
+            if i in held else keep.tile([P, 2, CHUNK, PACK], F32, name="with_arr%d" % i)
+            for i in range(8) if i != EARLY - 1
+        }
+        straddling = [
+            keep.tile([P, CHUNK, PACK], F32, name="straddling0"),
+            loads.tile([P, CHUNK, PACK], F32, name="straddling1", offset=late),
         ]
+
+        def arr_term(i, s):
+            return straddling[s][:] if i == EARLY - 1 else with_arr[i][:, s]
+
         terms = {}
 
         def entity_sum(i, s, bank):
@@ -231,11 +259,11 @@ def tile_list_ckg_sig_kernel(
         def ari_sum(i):
             sums["ari", i] = project("ari%d" % i, ("d0", "d1"), relation(i), 6 + i % 2, i in TURNED)
 
-        def arr_terms(i):
+        def arr_terms(i, parts=(0, 1)):
             arr = sums["arr", i]
             if i < EARLY:
-                for s in range(2):
-                    nc.vector.tensor_tensor(with_arr[i][:, s], arr, entity(i, s), MULT)
+                for s in parts:
+                    nc.vector.tensor_tensor(arr_term(i, s), arr, entity(i, s), MULT)
             else:
                 arr_twice = arr.unsqueeze(1).to_broadcast([P, 2, CHUNK, PACK])
                 nc.vector.tensor_tensor(with_arr[i][:], arr_twice, ent_sb[i][:], MULT)
@@ -245,37 +273,41 @@ def tile_list_ckg_sig_kernel(
             ari = sums["ari", i]
             nc.vector.scalar_tensor_tensor(with_ari[:, 0], ari, -1.0, entity(i, 1), MULT, MULT)
             nc.vector.tensor_tensor(with_ari[:, 1], ari, entity(i, 0), MULT)
-            terms[i] = [x[:].rearrange("p s n t -> p s (n t)") for x in (with_arr[i], with_ari)]
+            if i in TURNED:
+                terms[i] = [[x.rearrange("p n t -> p (n t)") for x in (arr_term(i, s), with_ari[:, s])] for s in range(2)]
+            else:
+                terms[i] = [x[:].rearrange("p s n t -> p s (n t)") for x in (with_arr[i], with_ari)]
 
+        quantize("b", interleave("b", [on_scalar, on_vector], 3 * P // 8))
+        gather_entities(1)
+        for s in range(2):
+            for i in range(EARLY - 1):
+                entity_sum(i, s, (s * (EARLY - 1) + i) % 4)
         gather_relations(0)
-        part_relations(0)
-        quantize_weight("b", [on_scalar])
-        entity_sum(0, 0, 0)
-        entity_sum(1, 0, 1)
-        grouped_c0 = interleave("c0", [on_scalar])
-        cand = loads.tile([P, 2, N // 2], I32, name="cand", offset=4 * SLOT, align_bytes=64)
-        cand_sc = loads.tile([P, 2, N // 4], I32, name="cand_sc", offset=4 * SLOT + 4 * N, align_bytes=64)
-        nc.gpsimd.memset(cand_sc[:], 0)
-        for s, (cand_words, cand_scales) in enumerate(((nr_words, nr_scales), (ni_words, ni_scales))):
-            nc.sync.dma_start(cand[:, s, :], cand_words[0].bitcast(I32))
-            for q in range(QUADS):
-                nc.sync.dma_start(cand_sc[32 * q : 32 * q + 4, s, :], cand_scales[0, 4 * q : 4 * q + 4, :].bitcast(I32))
-
-        quantize("c0", grouped_c0)
-        quantize_weight("c1", [on_scalar, on_vector])
         gather_relations(1)
+        part_relations(0)
+        quantize("c0", interleave("c0", [on_scalar, on_vector], 3 * P // 4))
+        entity_sum(EARLY - 1, 0, 2)
+        quantize("c1", interleave("c1", [on_scalar, on_vector], 3 * P // 8))
+        entity_sum(EARLY - 1, 1, 3)
         part_relations(1)
-        entity_sum(0, 1, 2)
-        entity_sum(1, 1, 3)
         arr_sum(0)
         arr_sum(1)
         arr_terms(0)
         arr_sum(2)
+        arr_terms(1)
+        arr_sum(3)
         quantize_weight("d0", [on_scalar])
-        quantize_weight("d1", [on_scalar,on_vector])
+        arr_terms(2)
+        arr_sum(4)
+        arr_terms(3, (0,))
+        quantize_weight("d1", [on_scalar])
 
-        def quantize_h(h, columns, name):
-            h_codes = keep.tile([P, columns], U32, name="codes_" + name, align_bytes=64)
+        def quantize_h(h, columns, name, offset=None):
+            if offset is None:
+                h_codes = keep.tile([P, columns], U32, name="codes_" + name, align_bytes=64)
+            else:
+                h_codes = loads.tile([P, columns], U32, name="codes_" + name, offset=offset, align_bytes=64)
             h_scales = keep.tile([P, columns], U8, name="scales_" + name, align_bytes=64)
             nc.vector.quantize_mx(out=h_codes[:].bitcast(FP8X4), scales=h_scales[:], in_=h)
             return h_codes, h_scales
@@ -309,7 +341,7 @@ def tile_list_ckg_sig_kernel(
                 for t in range(PACK):
                     for g in range(2):
                         nc.tensor.matmul(
-                            total[:, t, :], terms[i][g][:, s, t * P : (t + 1) * P], identity[:],
+                            total[:, t, :], terms[i][s][g][:, t * P : (t + 1) * P], identity[:],
                             start=(g == 0), stop=(g == 1), is_transpose=True,
                         )
                 totals.append(total)
@@ -323,44 +355,50 @@ def tile_list_ckg_sig_kernel(
             for s in range(2):
                 entity_sum(i, s, 2 * (i % 2) + s)
 
-        h_half = keep.tile([P, 2, HALF_CHUNKS, WIDE], BF16, name="h_half", tag="h", align_bytes=64)
+        h_half = loads.tile([P, 2, HALF_CHUNKS, WIDE], BF16, name="h_half", offset=slot["d0"], align_bytes=64)
         ari_sum(0)
         ari_sum(1)
-        both_sums(2)
-        arr_terms(1)
-        arr_sum(3)
+        arr_terms(3, (1,))
+        arr_sum(5)
+        both_sums(4)
+        both_sums(5)
 
-        def products(i):
-            if i >= EARLY:
-                arr_terms(i)
-                if i + 2 < 8:
-                    arr_sum(i + 2)
+        def with_arr_part(i):
+            arr_terms(i)
+            if i + 2 < 8:
+                arr_sum(i + 2)
+
+        def with_ari_part(i):
             ari_terms(i)
             if i + 2 < 8:
                 ari_sum(i + 2)
 
-        for i in range(5):
-            products(i)
-            both_sums(3 + i)
-            if i < 3:
+        for i in range(6):
+            if i >= EARLY:
+                with_arr_part(i)
+            with_ari_part(i)
+            if i in TURNED:
+                round_sums(h_half[:, :, i, :], add_turned(i, (0, 1)))
+            elif i < HALF_CHUNKS:
                 nc.gpsimd.tensor_tensor(h_half[:, :, i, :], terms[i][0], terms[i][1], ADD)
-            if i == 3:
-                round_sums(h_half[:, :, i, :], add_turned(i, (2, 3)))
-        operands = hr_hi(quantize_h(h_half[:].rearrange("p s i w -> p (s i w)"), 2 * HALF, "half"), 0, HALF)
-        h_pair = keep.tile([P, 2, 2, WIDE], BF16, name="h_pair", tag="h", align_bytes=64)
-        nc.gpsimd.tensor_tensor(h_pair[:, 0], terms[4][0], terms[4][1], ADD)
-        products(5)
-        round_sums(h_pair[:, 1], add_turned(5, (0, 1)))
+            if i < 2:
+                both_sums(6 + i)
+        operands = hr_hi(quantize_h(h_half[:].rearrange("p s i w -> p (s i w)"), 2 * HALF, "half", place[1]), 0, HALF)
+        h_pair = loads.tile([P, 2, 2, WIDE], BF16, name="h_pair", offset=slot["d0"], align_bytes=64)
+        for e in range(2):
+            nc.gpsimd.tensor_tensor(h_pair[:, e], terms[4 + e][0], terms[4 + e][1], ADD)
         for u in range(N // P):
             y_half = psum.tile([P, HALF], F32, name="y_half%d" % u, offset=(u + 2) % 4 * BANK_BYTES)
             score(y_half[:], u, operands)
             result_half = ring.tile([P, HALF], F32, name="result_half", tag="result", bufs=8)
             nc.scalar.activation(result_half[:], y_half[:], SIGMOID)
             nc.sync.dma_start(out[u * P : (u + 1) * P, :HALF], result_half[:])
-        products(6)
+        with_arr_part(6)
+        with_ari_part(6)
         h_last = keep.tile([P, 2, 2, WIDE], BF16, name="h_last", align_bytes=64)
-        nc.gpsimd.tensor_tensor(h_last[:, 0], terms[6][0], terms[6][1], ADD)
-        products(7)
+        round_sums(h_last[:, 0], add_turned(6, (4, 6)))
+        with_arr_part(7)
+        with_ari_part(7)
         pair = quantize_h(h_pair[:].rearrange("p e s w -> p (e s w)"), 4 * CHUNK, "pair")
         for e in range(2):
             score_chunk(4 + e, hr_hi(pair, 2 * e * CHUNK, CHUNK))

@@ -48,7 +48,7 @@ def tile_list_ckg_sig_kernel(
 
         SLOT = 4 * T
         BANK_BYTES = 2048
-        TURNED = (3, 6)
+        TURNED = (1, 3, 6)
         ones = loads.tile([P, 7 * T + J // 4], F32, name="ones", offset=0, align_bytes=64)
         LIP = 16
         MID = 7 * SLOT + J
@@ -221,7 +221,7 @@ def tile_list_ckg_sig_kernel(
         def entity(i, s):
             return apart_sb[i][s][:] if i < EARLY else ent_sb[i][:, s]
 
-        held = {4: slot["c0"], 6: slot["d0"] + half}
+        held = {4: slot["c0"], 5: slot["d1"], 6: slot["d0"] + half, 7: slot["d0"] - half}
         with_arr = {
             i: loads.tile([P, 2, CHUNK, PACK], F32, name="with_arr%d" % i, offset=held[i])
             if i in held else keep.tile([P, 2, CHUNK, PACK], F32, name="with_arr%d" % i)
@@ -317,19 +317,24 @@ def tile_list_ckg_sig_kernel(
             spans = [slice(first + s * tokens, first + (s + 1) * tokens) for s in range(2)]
             return [(h_codes[:, span], h_scales[:, span]) for span in spans]
 
-        def score(y, u, operands):
-            for s, (h_codes, h_scales) in enumerate(operands):
-                nc.tensor.matmul_mx(
-                    out=y,
-                    lhsT=cand[:, s, :].bitcast(U8)[:, 2 * u * P : 2 * (u + 1) * P].bitcast(FP4X4),
-                    lhsT_scale=cand_sc[:, s, :].bitcast(U8)[:, u * P : (u + 1) * P],
-                    rhs=h_codes.bitcast(FP8X4), rhs_scale=h_scales, start=(s == 0), stop=(s == 1),
-                )
+        def score_pass(y, u, s, operand, start, stop):
+            h_codes, h_scales = operand
+            nc.tensor.matmul_mx(
+                out=y,
+                lhsT=cand[:, s, :].bitcast(U8)[:, 2 * u * P : 2 * (u + 1) * P].bitcast(FP4X4),
+                lhsT_scale=cand_sc[:, s, :].bitcast(U8)[:, u * P : (u + 1) * P],
+                rhs=h_codes.bitcast(FP8X4), rhs_scale=h_scales, start=start, stop=stop,
+            )
 
-        def score_chunk(i, operands):
-            y = psum.tile([P, N // P, CHUNK], F32, name="y%d" % i, offset=(i + 2) % 4 * BANK_BYTES)
-            for u in range(N // P):
-                score(y[:, u, :], u, operands)
+        def score(y, u, operands):
+            for s in range(2):
+                score_pass(y, u, s, operands[s], s == 0, s == 1)
+
+        def score_chunk(i, operands, bank):
+            y = psum.tile([P, N // P, CHUNK], F32, name="y%d" % i, offset=bank * BANK_BYTES)
+            for s in range(2):
+                for u in range(N // P):
+                    score_pass(y[:, u, :], u, s, operands[s], s == 0 and u == 0, s == 1 and u == N // P - 1)
             result = ring.tile([P, N // P, CHUNK], F32, name="result", tag="result", bufs=8)
             nc.scalar.activation(result[:], y[:], SIGMOID)
             nc.sync.dma_start(out[:, i * CHUNK : (i + 1) * CHUNK].rearrange("(u p) j -> p u j", p=P), result[:])
@@ -373,38 +378,47 @@ def tile_list_ckg_sig_kernel(
             if i + 2 < 8:
                 ari_sum(i + 2)
 
-        for i in range(6):
-            if i >= EARLY:
-                with_arr_part(i)
-            with_ari_part(i)
-            if i in TURNED:
-                round_sums(h_half[:, :, i, :], add_turned(i, (0, 1)))
-            elif i < HALF_CHUNKS:
-                nc.gpsimd.tensor_tensor(h_half[:, :, i, :], terms[i][0], terms[i][1], ADD)
-            if i < 2:
-                both_sums(6 + i)
+        def add_on_gpsimd(h, i):
+            nc.gpsimd.tensor_tensor(h, terms[i][0], terms[i][1], ADD)
+
+        with_ari_part(0)
+        add_on_gpsimd(h_half[:, :, 0, :], 0)
+        both_sums(6)
+        with_ari_part(1)
+        both_sums(7)
+        round_sums(h_half[:, :, 1, :], add_turned(1, (0, 1)))
+        with_ari_part(2)
+        add_on_gpsimd(h_half[:, :, 2, :], 2)
+        with_ari_part(3)
+        round_sums(h_half[:, :, 3, :], add_turned(3, (2, 3)))
+        with_arr_part(4)
+        with_ari_part(4)
+        h_four = loads.tile([P, 2, WIDE], BF16, name="h_four", offset=slot["d0"] - half, align_bytes=64)
+        add_on_gpsimd(h_four[:], 4)
+        with_arr_part(5)
+        with_ari_part(5)
         operands = hr_hi(quantize_h(h_half[:].rearrange("p s i w -> p (s i w)"), 2 * HALF, "half", place[1]), 0, HALF)
-        h_pair = loads.tile([P, 2, 2, WIDE], BF16, name="h_pair", offset=slot["d0"], align_bytes=64)
-        for e in range(2):
-            nc.gpsimd.tensor_tensor(h_pair[:, e], terms[4 + e][0], terms[4 + e][1], ADD)
+        h_five = loads.tile([P, 2, WIDE], BF16, name="h_five", offset=slot["d0"], align_bytes=64)
+        add_on_gpsimd(h_five[:], 5)
         for u in range(N // P):
-            y_half = psum.tile([P, HALF], F32, name="y_half%d" % u, offset=(u + 2) % 4 * BANK_BYTES)
+            y_half = psum.tile([P, HALF], F32, name="y_half%d" % u, offset=u * BANK_BYTES)
             score(y_half[:], u, operands)
             result_half = ring.tile([P, HALF], F32, name="result_half", tag="result", bufs=8)
             nc.scalar.activation(result_half[:], y_half[:], SIGMOID)
             nc.sync.dma_start(out[u * P : (u + 1) * P, :HALF], result_half[:])
         with_arr_part(6)
         with_ari_part(6)
-        h_last = keep.tile([P, 2, 2, WIDE], BF16, name="h_last", align_bytes=64)
-        round_sums(h_last[:, 0], add_turned(6, (4, 6)))
+        h_six = keep.tile([P, 2, WIDE], BF16, name="h_six", align_bytes=64)
+        round_sums(h_six[:], add_turned(6, (4, 6)))
+        for i, h in ((4, h_four), (5, h_five)):
+            single = quantize_h(h[:].rearrange("p s w -> p (s w)"), 2 * CHUNK, "single%d" % i, place[2] + (i - 4) * quarter)
+            score_chunk(i, hr_hi(single, 0, CHUNK), i - 4)
         with_arr_part(7)
         with_ari_part(7)
-        pair = quantize_h(h_pair[:].rearrange("p e s w -> p (e s w)"), 4 * CHUNK, "pair")
-        for e in range(2):
-            score_chunk(4 + e, hr_hi(pair, 2 * e * CHUNK, CHUNK))
-        nc.vector.tensor_tensor(h_last[:, 1, 0], terms[7][0][:, 0], terms[7][1][:, 0], ADD)
-        single = quantize_h(h_last[:, 0].rearrange("p s w -> p (s w)"), 2 * CHUNK, "six")
-        score_chunk(6, hr_hi(single, 0, CHUNK))
-        nc.vector.tensor_tensor(h_last[:, 1, 1], terms[7][0][:, 1], terms[7][1][:, 1], ADD)
-        apart = [quantize_h(h_last[:, 1, s], CHUNK, "seven%d" % s) for s in range(2)]
-        score_chunk(7, [(h_codes[:], h_scales[:]) for h_codes, h_scales in apart])
+        h_last = keep.tile([P, 2, WIDE], BF16, name="h_last", align_bytes=64)
+        nc.vector.tensor_tensor(h_last[:, 0], terms[7][0][:, 0], terms[7][1][:, 0], ADD)
+        single = quantize_h(h_six[:].rearrange("p s w -> p (s w)"), 2 * CHUNK, "six")
+        score_chunk(6, hr_hi(single, 0, CHUNK), 2)
+        nc.vector.tensor_tensor(h_last[:, 1], terms[7][0][:, 1], terms[7][1][:, 1], ADD)
+        apart = [quantize_h(h_last[:, s], CHUNK, "seven%d" % s) for s in range(2)]
+        score_chunk(7, [(h_codes[:], h_scales[:]) for h_codes, h_scales in apart], 3)

@@ -98,7 +98,7 @@ def tile_list_ckg_sig_kernel(
         ]
         rel_codes = [
             keep.tile([P, 2, 2 * HALF], U8, name="rel_codes0", align_bytes=64),
-            loads.tile([P, 2, 2 * HALF], U8, name="rel_codes1", offset=late + SLOT // 2, align_bytes=64),
+            loads.tile([P, 2, 2 * HALF], U8, name="rel_codes1", offset=10 * SLOT, align_bytes=64),
         ]
 
         def gather_entities(e):
@@ -124,7 +124,7 @@ def tile_list_ckg_sig_kernel(
 
         on_scalar, on_vector = nc.scalar.copy, nc.vector.tensor_copy
 
-        placed = {"a": late - SLOT // 2, "b": late + SLOT, "c0": late - SLOT // 2, "d1": late, "c1": late + SLOT // 2}
+        placed = {"a": late - SLOT // 2, "b": late + SLOT, "c0": late - SLOT // 2, "d1": late, "c1": 10 * SLOT}
 
         def interleave(name, engines, first=P // 2):
             if name in placed:
@@ -147,10 +147,11 @@ def tile_list_ckg_sig_kernel(
         nc.sync.dma_start(ent_list[:], offs)
         nc.sync.dma_start(rel_list[:], offs2)
         for q in range(QUADS):
-            nc.sync.dma_start(ent_scales[32 * q : 32 * q + 4, :], tab_scales[0, 4 * q : 4 * q + 4, :].bitcast(I32))
+            nc.sync.dma_start(ent_scales[32 * q + 8 : 32 * q + 12, :], tab_scales[0, 4 * q : 4 * q + 4, :].bitcast(I32))
         load_weight("a")
         for q in range(QUADS):
-            nc.sync.dma_start(rel_held[32 * q : 32 * q + 8, LIP : LIP + T // 4], tab2_scales[:, 4 * q : 4 * q + 4, :].bitcast(I32))
+            nc.sync.dma_start(rel_held[32 * q : 32 * q + 4, LIP : LIP + T // 4], tab2_scales[0, 4 * q : 4 * q + 4, :].bitcast(I32))
+        nc.sync.dma_start(rel_held[4:P:8, LIP : LIP + T // 4], tab2_scales[1].bitcast(I32))
         nc.sync.dma_start(ent_words[:], tab_words[0].rearrange("p t i -> p (t i)").bitcast(I32))
         load_weight("b")
         nc.sync.dma_start(rel_words[:], tab2_words[0].rearrange("p t i -> p (t i)").bitcast(I32))
@@ -164,7 +165,7 @@ def tile_list_ckg_sig_kernel(
         quantize_weight("a", [on_scalar])
         gather_entities(0)
         for q in range(QUADS):
-            nc.sync.dma_start(rel_sc1[32 * q : 32 * q + 4, :], rel_sc0[32 * q + 4 : 32 * q + 8, :])
+            nc.sync.dma_start(rel_sc1[q:P:32, :], rel_sc0[8 * q + 4 : P : 32, :])
         load_weight("d0", 1)
         load_weight("d1")
         cand_sc = loads.tile([P, 2, N // 4], I32, name="cand_sc", offset=MID + T, align_bytes=64)
@@ -222,10 +223,11 @@ def tile_list_ckg_sig_kernel(
             return apart_sb[i][s][:] if i < EARLY else ent_sb[i][:, s]
 
         held = {4: slot["c0"], 5: slot["d1"], 6: slot["d0"] + half, 7: slot["d0"] - half}
+        held[3] = late + quarter
         with_arr = {
             i: loads.tile([P, 2, CHUNK, PACK], F32, name="with_arr%d" % i, offset=held[i])
             if i in held else keep.tile([P, 2, CHUNK, PACK], F32, name="with_arr%d" % i)
-            for i in range(8) if i != EARLY - 1
+            for i in range(8) if i != 1
         }
         straddling = [
             keep.tile([P, CHUNK, PACK], F32, name="straddling0"),
@@ -233,14 +235,14 @@ def tile_list_ckg_sig_kernel(
         ]
 
         def arr_term(i, s):
-            return straddling[s][:] if i == EARLY - 1 else with_arr[i][:, s]
+            return straddling[s][:] if i == 1 else with_arr[i][:, s]
 
         terms = {}
 
         def entity_sum(i, s, bank):
             cols = slice(i * CHUNK, (i + 1) * CHUNK)
             within = slice(i % HALF_CHUNKS * CHUNK, (i % HALF_CHUNKS + 1) * CHUNK)
-            ent = [(ent_codes[i // HALF_CHUNKS][:, within].bitcast(FP8X4), ent_sc[:, cols])]
+            ent = [(ent_codes[i // HALF_CHUNKS][:, within].bitcast(FP8X4), ent_sc[8:, cols])]
             nc.scalar.copy(entity(i, s), project("ent%d_%d" % (i, s), ("ab"[s],), ent, bank, i in TURNED))
 
         def relation(i):
@@ -254,7 +256,7 @@ def tile_list_ckg_sig_kernel(
         sums = {}
 
         def arr_sum(i):
-            sums["arr", i] = project("arr%d" % i, ("c0", "c1"), relation(i), 4 + i % 2, i in TURNED)
+            sums["arr", i] = project("arr%d" % i, ("c0", "c1"), relation(i), (4, 4, 5, 6, 5, 4, 5, 4)[i], i in TURNED)
 
         def ari_sum(i):
             sums["ari", i] = project("ari%d" % i, ("d0", "d1"), relation(i), 6 + i % 2, i in TURNED)
@@ -292,16 +294,19 @@ def tile_list_ckg_sig_kernel(
         entity_sum(EARLY - 1, 1, 3)
         part_relations(1)
         arr_sum(0)
-        arr_sum(1)
-        arr_terms(0)
         arr_sum(2)
-        arr_terms(1)
         arr_sum(3)
-        quantize_weight("d0", [on_scalar])
+        arr_terms(0)
+        arr_sum(1)
         arr_terms(2)
         arr_sum(4)
-        arr_terms(3, (0,))
-        quantize_weight("d1", [on_scalar])
+        arr_terms(1, (0,))
+        quantize_weight("d0", [on_scalar])
+        arr_sb = loads.tile([P, CHUNK, PACK], F32, name="arr_sb", offset=slot["d0"] - quarter + 4 * LIP)
+        nc.scalar.copy(arr_sb[:], sums["arr", 3])
+        quantize("d1", interleave("d1", [on_scalar, on_vector], 5 * P // 8))
+        for s in range(2):
+            nc.gpsimd.tensor_tensor(arr_term(3, s), arr_sb[:], entity(3, s), MULT)
 
         def quantize_h(h, columns, name, offset=None):
             if offset is None:
@@ -363,7 +368,7 @@ def tile_list_ckg_sig_kernel(
         h_half = loads.tile([P, 2, HALF_CHUNKS, WIDE], BF16, name="h_half", offset=slot["d0"], align_bytes=64)
         ari_sum(0)
         ari_sum(1)
-        arr_terms(3, (1,))
+        arr_terms(1, (1,))
         arr_sum(5)
         both_sums(4)
         both_sums(5)
@@ -409,7 +414,7 @@ def tile_list_ckg_sig_kernel(
         with_arr_part(6)
         with_ari_part(6)
         h_six = keep.tile([P, 2, WIDE], BF16, name="h_six", align_bytes=64)
-        round_sums(h_six[:], add_turned(6, (4, 6)))
+        round_sums(h_six[:], add_turned(6, (5, 6)))
         for i, h in ((4, h_four), (5, h_five)):
             single = quantize_h(h[:].rearrange("p s w -> p (s w)"), 2 * CHUNK, "single%d" % i, place[2] + (i - 4) * quarter)
             score_chunk(i, hr_hi(single, 0, CHUNK), i - 4)

@@ -49,22 +49,22 @@ def tile_list_ckg_sig_kernel(
         SLOT = 4 * T
         BANK_BYTES = 2048
         TURNED = (1, 3, 6)
-        ones = loads.tile([P, 7 * T + J // 4], F32, name="ones", offset=0, align_bytes=64)
+        ones = loads.tile([P, 5 * T], F32, name="ones", offset=SLOT + J, align_bytes=64)
         LIP = 16
         MID = 7 * SLOT + J
-        GAP = 3 * SLOT // 4
+        GAP = SLOT
         rel_held = loads.tile([P, GAP // 4 + 2 * LIP], I32, name="rel_held", offset=MID - 4 * LIP, align_bytes=64)
         rel_scales = rel_held[:, LIP : LIP + T // 4]
         nc.vector.memset(ent_scales[:], 0)
+        zeros = loads.tile([P, LIP + J // 4], I32, name="zeros", offset=SLOT - 4 * LIP, align_bytes=64)
+        nc.vector.memset(zeros[:, LIP:], 0)
+        nc.vector.memset(rel_held[:, LIP : LIP + T // 4 + N // 2], 0)
         identity = keep.tile([P, P], F32, name="identity")
-        nc.gpsimd.memset(ones[:, :P], 1.0)
+        nc.vector.memset(ones[:, :P], 1.0)
         nc.gpsimd.affine_select(
             out=identity[:], in_=ones[:, :P], pattern=[[-1, P]], compare_op=mybir.AluOpType.is_equal,
             fill=0.0, base=0, channel_multiplier=1,
         )
-        nc.gpsimd.memset(rel_held[:, LIP : LIP + T // 4 + N // 2], 0)
-        zeros = loads.tile([P, 5 * T], I32, name="zeros", offset=SLOT, align_bytes=64)
-        nc.gpsimd.memset(zeros[:, : J // 4], 0)
 
         ent_words = loads.tile([P, T], I32, name="ent_words", offset=2 * SLOT + J, align_bytes=64)
         rel_words = loads.tile([P, T], I32, name="rel_words", offset=SLOT + J, align_bytes=64)
@@ -90,7 +90,7 @@ def tile_list_ckg_sig_kernel(
         late = 11 * SLOT
         ent_codes = [
             keep.tile([P, HALF], U32, name="ent_codes0", align_bytes=64),
-            loads.tile([P, HALF], U32, name="ent_codes1", offset=late + SLOT, align_bytes=64),
+            loads.tile([P, HALF], U32, name="ent_codes1", offset=slot["b"] + 3 * SLOT // 4, align_bytes=64),
         ]
         rel_pairs = [
             keep.tile([P, HALF], U32, name="rel_pairs0", align_bytes=64),
@@ -98,7 +98,7 @@ def tile_list_ckg_sig_kernel(
         ]
         rel_codes = [
             keep.tile([P, 2, 2 * HALF], U8, name="rel_codes0", align_bytes=64),
-            loads.tile([P, 2, 2 * HALF], U8, name="rel_codes1", offset=10 * SLOT, align_bytes=64),
+            loads.tile([P, 2, 2 * HALF], U8, name="rel_codes1", offset=slot["c1"] + SLOT // 2, align_bytes=64),
         ]
 
         def gather_entities(e):
@@ -124,7 +124,7 @@ def tile_list_ckg_sig_kernel(
 
         on_scalar, on_vector = nc.scalar.copy, nc.vector.tensor_copy
 
-        placed = {"a": late - SLOT // 2, "b": late + SLOT, "c0": late - SLOT // 2, "d1": late, "c1": 10 * SLOT}
+        placed = {"a": late - SLOT // 2, "b": late + SLOT, "c0": late - SLOT // 2, "d1": late, "c1": late + 3 * SLOT // 2}
 
         def interleave(name, engines, first=P // 2):
             if name in placed:
@@ -200,30 +200,22 @@ def tile_list_ckg_sig_kernel(
 
         half = SLOT // 2
         quarter = SLOT // 4
-        place = [slot["d1"], slot["d1"] + half, 9 * SLOT, 9 * SLOT + half]
-
-        def early_at(i, s):
-            if i == EARLY - 1:
-                return slot[("c0", "c1")[s]]
-            return slot[("b", "a")[s]] + i * quarter
-
-        apart_sb = [
-            [
-                loads.tile([P, CHUNK, PACK], F32, name="ent%d_%d" % (i, s), offset=early_at(i, s))
-                for s in range(2)
-            ]
-            for i in range(EARLY)
-        ]
+        under = slot["d1"] - 4 * LIP
+        ent_at = {(i, s): slot[("b", "a")[s]] + i * quarter for i in range(EARLY - 1) for s in range(2)}
+        ent_at.update({(3, 0): slot["c0"], (3, 1): slot["c1"]})
+        ent_at.update({(4, 1): under, (4, 0): under + quarter, (5, 0): under + half, (5, 1): under + half + quarter})
+        ent_at.update({(6, 0): 9 * SLOT + half, (6, 1): 9 * SLOT + half + quarter})
         ent_sb = {
-            i: loads.tile([P, 2, CHUNK, PACK], F32, name="ent_sb%d" % i, offset=place[i - EARLY])
-            for i in range(EARLY, 8)
+            (i, s): loads.tile([P, CHUNK, PACK], F32, name="ent%d_%d" % (i, s), offset=ent_at[i, s])
+            if (i, s) in ent_at else keep.tile([P, CHUNK, PACK], F32, name="ent%d_%d" % (i, s))
+            for i in range(8) for s in range(2)
         }
 
         def entity(i, s):
-            return apart_sb[i][s][:] if i < EARLY else ent_sb[i][:, s]
+            return ent_sb[i, s][:]
 
-        held = {4: slot["c0"], 5: slot["d1"], 6: slot["d0"] + half, 7: slot["d0"] - half}
-        held[3] = late + quarter
+        held = {4: ent_at[3, 1], 5: under - quarter, 6: ent_at[5, 1] + J, 7: ent_at[6, 1] + R}
+        held[3] = late
         with_arr = {
             i: loads.tile([P, 2, CHUNK, PACK], F32, name="with_arr%d" % i, offset=held[i])
             if i in held else keep.tile([P, 2, CHUNK, PACK], F32, name="with_arr%d" % i)
@@ -231,7 +223,7 @@ def tile_list_ckg_sig_kernel(
         }
         straddling = [
             keep.tile([P, CHUNK, PACK], F32, name="straddling0"),
-            loads.tile([P, CHUNK, PACK], F32, name="straddling1", offset=late),
+            loads.tile([P, CHUNK, PACK], F32, name="straddling1", offset=under + SLOT),
         ]
 
         def arr_term(i, s):
@@ -262,16 +254,14 @@ def tile_list_ckg_sig_kernel(
             sums["ari", i] = project("ari%d" % i, ("d0", "d1"), relation(i), 6 + i % 2, i in TURNED)
 
         def arr_terms(i, parts=(0, 1)):
-            arr = sums["arr", i]
-            if i < EARLY:
-                for s in parts:
-                    nc.vector.tensor_tensor(arr_term(i, s), arr, entity(i, s), MULT)
-            else:
-                arr_twice = arr.unsqueeze(1).to_broadcast([P, 2, CHUNK, PACK])
-                nc.vector.tensor_tensor(with_arr[i][:], arr_twice, ent_sb[i][:], MULT)
+            for s in parts:
+                nc.vector.tensor_tensor(arr_term(i, s), sums["arr", i], entity(i, s), MULT)
 
         def ari_terms(i):
-            with_ari = ring.tile([P, 2, CHUNK, PACK], F32, name="with_ari", bufs=5)
+            if i == 7:
+                with_ari = loads.tile([P, 2, CHUNK, PACK], F32, name="with_ari7", offset=slot["c0"] + half)
+            else:
+                with_ari = ring.tile([P, 2, CHUNK, PACK], F32, name="with_ari", bufs=5)
             ari = sums["ari", i]
             nc.vector.scalar_tensor_tensor(with_ari[:, 0], ari, -1.0, entity(i, 1), MULT, MULT)
             nc.vector.tensor_tensor(with_ari[:, 1], ari, entity(i, 0), MULT)
@@ -309,11 +299,11 @@ def tile_list_ckg_sig_kernel(
             nc.gpsimd.tensor_tensor(arr_term(3, s), arr_sb[:], entity(3, s), MULT)
 
         def quantize_h(h, columns, name, offset=None):
+            h_codes = keep.tile([P, columns], U32, name="codes_" + name, align_bytes=64)
             if offset is None:
-                h_codes = keep.tile([P, columns], U32, name="codes_" + name, align_bytes=64)
+                h_scales = keep.tile([P, columns], U8, name="scales_" + name, align_bytes=64)
             else:
-                h_codes = loads.tile([P, columns], U32, name="codes_" + name, offset=offset, align_bytes=64)
-            h_scales = keep.tile([P, columns], U8, name="scales_" + name, align_bytes=64)
+                h_scales = loads.tile([P, columns], U8, name="scales_" + name, offset=offset, align_bytes=64)
             nc.vector.quantize_mx(out=h_codes[:].bitcast(FP8X4), scales=h_scales[:], in_=h)
             return h_codes, h_scales
 
@@ -398,11 +388,11 @@ def tile_list_ckg_sig_kernel(
         round_sums(h_half[:, :, 3, :], add_turned(3, (2, 3)))
         with_arr_part(4)
         with_ari_part(4)
-        h_four = loads.tile([P, 2, WIDE], BF16, name="h_four", offset=slot["d0"] - half, align_bytes=64)
+        h_four = loads.tile([P, 2, WIDE], BF16, name="h_four", offset=slot["c0"] + half, align_bytes=64)
         add_on_gpsimd(h_four[:], 4)
         with_arr_part(5)
         with_ari_part(5)
-        operands = hr_hi(quantize_h(h_half[:].rearrange("p s i w -> p (s i w)"), 2 * HALF, "half", place[1]), 0, HALF)
+        operands = hr_hi(quantize_h(h_half[:].rearrange("p s i w -> p (s i w)"), 2 * HALF, "half", ent_at[5, 1]), 0, HALF)
         h_five = loads.tile([P, 2, WIDE], BF16, name="h_five", offset=slot["d0"], align_bytes=64)
         add_on_gpsimd(h_five[:], 5)
         for u in range(N // P):
@@ -415,10 +405,10 @@ def tile_list_ckg_sig_kernel(
         with_ari_part(6)
         h_six = keep.tile([P, 2, WIDE], BF16, name="h_six", align_bytes=64)
         round_sums(h_six[:], add_turned(6, (5, 6)))
-        for i, h in ((4, h_four), (5, h_five)):
-            single = quantize_h(h[:].rearrange("p s w -> p (s w)"), 2 * CHUNK, "single%d" % i, place[2] + (i - 4) * quarter)
-            score_chunk(i, hr_hi(single, 0, CHUNK), i - 4)
         with_arr_part(7)
+        for i, h in ((4, h_four), (5, h_five)):
+            single = quantize_h(h[:].rearrange("p s w -> p (s w)"), 2 * CHUNK, "single%d" % i, ent_at[6, 1] + (i - 4) * 2 * CHUNK)
+            score_chunk(i, hr_hi(single, 0, CHUNK), i - 4)
         with_ari_part(7)
         h_last = keep.tile([P, 2, WIDE], BF16, name="h_last", align_bytes=64)
         nc.vector.tensor_tensor(h_last[:, 0], terms[7][0][:, 0], terms[7][1][:, 0], ADD)

@@ -23,12 +23,38 @@ K_PASS = P * PACK
 QUADS = 4
 GROUP = 16
 CHUNK = 128
+CHUNKS = J // CHUNK
 WIDE = CHUNK * PACK
 HALF = J // 2
 HALF_CHUNKS = HALF // CHUNK
-SHARED = P // 2
-BANKS = 2
-EARLY = 4
+BANK_BYTES = 2048
+ENT_ROW = 8
+
+TURNED = (1, 3, 6)
+STRADDLING = 1
+ON_GPSIMD = 3
+ARR_ORDER = (0, 2, STRADDLING, 4, 5, 6, 7)
+ARR_BANK, ARI_BANK = 4, 6
+
+SCALAR_SHARE = {"er": P, "ei": 3 * P // 8, "rr0": 3 * P // 4, "rr1": 3 * P // 8, "ri0": P, "ri1": 5 * P // 8}
+
+SLOT = 4 * T
+HALF_SLOT = SLOT // 2
+QUARTER = SLOT // 4
+LIP = 64
+MOVED_AT = SLOT
+REL_WORDS_AT = MOVED_AT + J
+ENT_WORDS_AT = REL_WORDS_AT + SLOT
+WINDOW_AT = REL_WORDS_AT + 6 * SLOT
+RAW_AT = {
+    "er": 0, "ei": ENT_WORDS_AT + SLOT, "rr0": ENT_WORDS_AT + 2 * SLOT, "rr1": ENT_WORDS_AT + 3 * SLOT,
+    "ri0": WINDOW_AT - SLOT, "ri1": WINDOW_AT + SLOT,
+}
+SIXTH_AT = 9 * SLOT + HALF_SLOT
+GROUPED_AT = {
+    "er": 10 * SLOT + HALF_SLOT, "rr0": 10 * SLOT + HALF_SLOT, "ri1": 11 * SLOT, "ei": 12 * SLOT,
+    "rr1": 12 * SLOT + HALF_SLOT,
+}
 
 
 def tile_list_ckg_sig_kernel(
@@ -38,67 +64,48 @@ def tile_list_ckg_sig_kernel(
     nc = tc.nc
     with ExitStack() as ctx:
         keep = ctx.enter_context(tc.tile_pool(name="keep", bufs=1))
-        loads = ctx.enter_context(tc.tile_pool(name="loads", bufs=1))
-        ring = ctx.enter_context(tc.tile_pool(name="ring", bufs=3))
+        arena = ctx.enter_context(tc.tile_pool(name="arena", bufs=1))
+        ring = ctx.enter_context(tc.tile_pool(name="ring", bufs=1))
         psum = ctx.enter_context(tc.psum_pool(name="psum", bufs=1))
 
         ent_list = keep.tile([P, J // GROUP], U16, name="ent_list")
         rel_list = keep.tile([P, J // GROUP], U16, name="rel_list")
-        ent_scales = keep.tile([P, T // 4], I32, name="ent_scales", align_bytes=64)
 
-        SLOT = 4 * T
-        BANK_BYTES = 2048
-        TURNED = (1, 3, 6)
-        ones = loads.tile([P, 5 * T], F32, name="ones", offset=SLOT + J, align_bytes=64)
-        LIP = 16
-        MID = 7 * SLOT + J
-        GAP = SLOT
-        rel_held = loads.tile([P, GAP // 4 + 2 * LIP], I32, name="rel_held", offset=MID - 4 * LIP, align_bytes=64)
-        rel_scales = rel_held[:, LIP : LIP + T // 4]
-        nc.vector.memset(ent_scales[:], 0)
-        zeros = loads.tile([P, LIP + J // 4], I32, name="zeros", offset=SLOT - 4 * LIP, align_bytes=64)
-        nc.vector.memset(zeros[:, LIP:], 0)
-        nc.vector.memset(rel_held[:, LIP : LIP + T // 4 + N // 2], 0)
+        ent_window = keep.tile([P, T // 4], I32, name="ent_window", align_bytes=64)
+        nc.vector.memset(ent_window[:], 0)
+        moved_zeros = arena.tile([P, (LIP + J) // 4], I32, name="moved_zeros", offset=MOVED_AT - LIP, align_bytes=64)
+        nc.vector.memset(moved_zeros[:, LIP // 4 :], 0)
+        rel_held = arena.tile([P, (SLOT + 2 * LIP) // 4], I32, name="rel_held", offset=WINDOW_AT - LIP, align_bytes=64)
+        window_words = slice(LIP // 4, (LIP + T) // 4)
+        nc.vector.memset(rel_held[:, LIP // 4 : (LIP + T + 2 * N) // 4], 0)
         identity = keep.tile([P, P], F32, name="identity")
+        ones = arena.tile([P, 5 * T], F32, name="ones", offset=REL_WORDS_AT, align_bytes=64)
         nc.vector.memset(ones[:, :P], 1.0)
         nc.gpsimd.affine_select(
             out=identity[:], in_=ones[:, :P], pattern=[[-1, P]], compare_op=mybir.AluOpType.is_equal,
             fill=0.0, base=0, channel_multiplier=1,
         )
 
-        ent_words = loads.tile([P, T], I32, name="ent_words", offset=2 * SLOT + J, align_bytes=64)
-        rel_words = loads.tile([P, T], I32, name="rel_words", offset=SLOT + J, align_bytes=64)
+        ent_words = arena.tile([P, T], I32, name="ent_words", offset=ENT_WORDS_AT, align_bytes=64)
+        rel_words = arena.tile([P, T], I32, name="rel_words", offset=REL_WORDS_AT, align_bytes=64)
         passes = {
-            "a": wer, "b": wei,
-            "c0": wrr[:K_PASS, :], "c1": wrr[K_PASS:, :], "d0": wri[:K_PASS, :], "d1": wri[K_PASS:, :],
+            "er": wer, "ei": wei,
+            "rr0": wrr[:K_PASS, :], "rr1": wrr[K_PASS:, :], "ri0": wri[:K_PASS, :], "ri1": wri[K_PASS:, :],
         }
         raw = {}
-        slot = {"a": 0, "b": 3 * SLOT + J, "c0": 4 * SLOT + J, "c1": 5 * SLOT + J, "d0": MID - SLOT, "d1": MID + GAP}
 
-        def load_weight(name, parts=1, only=None):
-            rows = passes[name].rearrange("(p e) r -> p e r", e=PACK)
-            width = R // parts
-            raw.setdefault(name, [])
-            for part in range(parts) if only is None else [only]:
-                piece = loads.tile(
-                    [P, PACK, width], F32, name="raw_%s_%d" % (name, part), align_bytes=64,
-                    offset=slot[name] + part * SLOT // parts,
-                )
-                nc.sync.dma_start(piece[:], rows[:, :, part * width : (part + 1) * width])
-                raw[name].append(piece)
+        def load_weight(name):
+            raw[name] = arena.tile([P, PACK, R], F32, name="raw_" + name, offset=RAW_AT[name], align_bytes=64)
+            nc.sync.dma_start(raw[name][:], passes[name].rearrange("(p e) r -> p e r", e=PACK))
 
-        late = 11 * SLOT
         ent_codes = [
             keep.tile([P, HALF], U32, name="ent_codes0", align_bytes=64),
-            loads.tile([P, HALF], U32, name="ent_codes1", offset=slot["b"] + 3 * SLOT // 4, align_bytes=64),
+            arena.tile([P, HALF], U32, name="ent_codes1", offset=RAW_AT["ei"] + 3 * QUARTER, align_bytes=64),
         ]
-        rel_pairs = [
-            keep.tile([P, HALF], U32, name="rel_pairs0", align_bytes=64),
-            keep.tile([P, HALF], U32, name="rel_pairs1", align_bytes=64),
-        ]
+        rel_pairs = [keep.tile([P, HALF], U32, name="rel_pairs%d" % e, align_bytes=64) for e in range(2)]
         rel_codes = [
             keep.tile([P, 2, 2 * HALF], U8, name="rel_codes0", align_bytes=64),
-            loads.tile([P, 2, 2 * HALF], U8, name="rel_codes1", offset=slot["c1"] + SLOT // 2, align_bytes=64),
+            arena.tile([P, 2, 2 * HALF], U8, name="rel_codes1", offset=RAW_AT["rr1"] + HALF_SLOT, align_bytes=64),
         ]
 
         def gather_entities(e):
@@ -114,202 +121,191 @@ def tile_list_ckg_sig_kernel(
                 rel_codes[e][:].bitcast(U16), rel_pairs[e][:].bitcast(U16).rearrange("p (j a) -> p a j", a=2)
             )
 
-        ent_sc = keep.tile([P, J], U8, name="ent_sc", align_bytes=64)
+        ent_scales = keep.tile([P, J], U8, name="ent_scales", align_bytes=64)
         w_codes = {name: keep.tile([P, R], U32, name="codes_" + name, align_bytes=64) for name in passes}
         w_scales = {name: keep.tile([P, R], U8, name="scales_" + name, align_bytes=64) for name in passes}
 
-        def on_gpsimd(dst, src):
-            for e in range(PACK):
-                nc.gpsimd.tensor_scalar(dst[:, :, e, :], src[:, :, e, :], 1.0, 0.0, MULT, ADD)
-
-        on_scalar, on_vector = nc.scalar.copy, nc.vector.tensor_copy
-
-        placed = {"a": late - SLOT // 2, "b": late + SLOT, "c0": late - SLOT // 2, "d1": late, "c1": late + 3 * SLOT // 2}
-
-        def interleave(name, engines, first=P // 2):
-            if name in placed:
-                grouped = loads.tile([P, PACK * R], BF16, name="grouped_" + name, offset=placed[name], align_bytes=64)
+        def quantize_weight(name):
+            if name in GROUPED_AT:
+                grouped = arena.tile([P, PACK * R], BF16, name="grouped_" + name, offset=GROUPED_AT[name], align_bytes=64)
             else:
-                grouped = ring.tile([P, PACK * R], BF16, name="grouped", align_bytes=64, bufs=1)
+                grouped = ring.tile([P, PACK * R], BF16, name="grouped", align_bytes=64)
             dst = grouped[:].rearrange("p (t m e) -> p m e t", t=PACK, e=PACK)
-            src = raw[name][0][:].rearrange("p e (m t) -> p m e t", t=PACK)
-            shares = [slice(0, P)] if len(engines) == 1 else [slice(0, first), slice(first, P)]
-            for share, copy in zip(shares, engines):
-                copy(dst[:, share], src[:, share])
-            return grouped
-
-        def quantize(name, grouped):
+            src = raw[name][:].rearrange("p e (m t) -> p m e t", t=PACK)
+            share = SCALAR_SHARE[name]
+            nc.scalar.copy(dst[:, :share], src[:, :share])
+            if share < P:
+                nc.vector.tensor_copy(dst[:, share:], src[:, share:])
             nc.vector.quantize_mx(out=w_codes[name][:].bitcast(FP8X4), scales=w_scales[name][:], in_=grouped[:])
-
-        def quantize_weight(name, engines):
-            quantize(name, interleave(name, engines))
 
         nc.sync.dma_start(ent_list[:], offs)
         nc.sync.dma_start(rel_list[:], offs2)
         for q in range(QUADS):
-            nc.sync.dma_start(ent_scales[32 * q + 8 : 32 * q + 12, :], tab_scales[0, 4 * q : 4 * q + 4, :].bitcast(I32))
-        load_weight("a")
+            rows = slice(32 * q + ENT_ROW, 32 * q + ENT_ROW + 4)
+            nc.sync.dma_start(ent_window[rows, :], tab_scales[0, 4 * q : 4 * q + 4, :].bitcast(I32))
+        load_weight("er")
         for q in range(QUADS):
-            nc.sync.dma_start(rel_held[32 * q : 32 * q + 4, LIP : LIP + T // 4], tab2_scales[0, 4 * q : 4 * q + 4, :].bitcast(I32))
-        nc.sync.dma_start(rel_held[4:P:8, LIP : LIP + T // 4], tab2_scales[1].bitcast(I32))
+            nc.sync.dma_start(rel_held[32 * q : 32 * q + 4, window_words], tab2_scales[0, 4 * q : 4 * q + 4, :].bitcast(I32))
+        nc.sync.dma_start(rel_held[4:P:8, window_words], tab2_scales[1].bitcast(I32))
         nc.sync.dma_start(ent_words[:], tab_words[0].rearrange("p t i -> p (t i)").bitcast(I32))
-        load_weight("b")
+        load_weight("ei")
         nc.sync.dma_start(rel_words[:], tab2_words[0].rearrange("p t i -> p (t i)").bitcast(I32))
-        load_weight("c0")
-        load_weight("c1")
-        nc.vector.tensor_copy(ent_sc[:], ent_scales[:].bitcast(U8).indirect(ent_list[:]))
-        rel_sc0 = keep.tile([P, J // 4], I32, name="rel_sc0", align_bytes=64)
-        rel_sc1 = loads.tile([P, J // 4], I32, name="rel_sc1", offset=SLOT, align_bytes=64)
-        rel_sc = [rel_sc0, rel_sc1]
-        nc.vector.tensor_copy(rel_sc0[:].bitcast(U8), rel_scales.bitcast(U8).indirect(rel_list[:]))
-        quantize_weight("a", [on_scalar])
+        load_weight("rr0")
+        load_weight("rr1")
+        nc.vector.tensor_copy(ent_scales[:], ent_window[:].bitcast(U8).indirect(ent_list[:]))
+        rel_scales = [
+            keep.tile([P, J // 4], I32, name="rel_scales0", align_bytes=64),
+            arena.tile([P, J // 4], I32, name="rel_scales1", offset=MOVED_AT, align_bytes=64),
+        ]
+        nc.vector.tensor_copy(rel_scales[0][:].bitcast(U8), rel_held[:, window_words].bitcast(U8).indirect(rel_list[:]))
+        quantize_weight("er")
         gather_entities(0)
-        for q in range(QUADS):
-            nc.sync.dma_start(rel_sc1[q:P:32, :], rel_sc0[8 * q + 4 : P : 32, :])
-        load_weight("d0", 1)
-        load_weight("d1")
-        cand_sc = loads.tile([P, 2, N // 4], I32, name="cand_sc", offset=MID + T, align_bytes=64)
-        cand = loads.tile([P, 2, N // 2], I32, name="cand", offset=MID + T + 2 * N, align_bytes=64)
-        for s, (cand_words, cand_scales) in enumerate(((nr_words, nr_scales), (ni_words, ni_scales))):
-            nc.sync.dma_start(cand[:, s, :], cand_words[0].bitcast(I32))
+        for c in range(4):
+            nc.sync.dma_start(rel_scales[1][c:P:32, :], rel_scales[0][8 * c + 4 : P : 32, :])
+        load_weight("ri0")
+        load_weight("ri1")
+        cand_scales = arena.tile([P, 2, N // 4], I32, name="cand_scales", offset=WINDOW_AT + T, align_bytes=64)
+        cand = arena.tile([P, 2, N // 2], I32, name="cand", offset=WINDOW_AT + T + 2 * N, align_bytes=64)
+        for s, (words, scales) in enumerate(((nr_words, nr_scales), (ni_words, ni_scales))):
+            nc.sync.dma_start(cand[:, s, :], words[0].bitcast(I32))
             for q in range(QUADS):
-                nc.sync.dma_start(cand_sc[32 * q : 32 * q + 4, s, :], cand_scales[0, 4 * q : 4 * q + 4, :].bitcast(I32))
+                nc.sync.dma_start(cand_scales[32 * q : 32 * q + 4, s, :], scales[0, 4 * q : 4 * q + 4, :].bitcast(I32))
 
-        def project(tag, names, moving, bank, turned=False):
+        def project(tag, names, table, bank, turned):
+            last = len(names) - 1
             if turned:
                 wide = psum.tile([P, R], F32, name=tag, offset=bank * BANK_BYTES)
                 for g, name in enumerate(names):
-                    table_codes, table_scales = moving[g]
+                    table_codes, table_scales = table[g]
                     nc.tensor.matmul_mx(
                         out=wide[:], lhsT=table_codes, lhsT_scale=table_scales,
                         rhs=w_codes[name][:].bitcast(FP8X4), rhs_scale=w_scales[name][:],
-                        start=(g == 0), stop=(g == len(names) - 1),
+                        start=(g == 0), stop=(g == last),
                     )
                 return wide[:].rearrange("p (n t) -> p n t", t=PACK)
             acc = psum.tile([P, PACK, CHUNK], F32, name=tag, offset=bank * BANK_BYTES)
             for g, name in enumerate(names):
-                table_codes, table_scales = moving[g]
+                table_codes, table_scales = table[g]
                 for t in range(PACK):
                     m = slice(t * P, (t + 1) * P)
                     nc.tensor.matmul_mx(
                         out=acc[:, t, :], lhsT=w_codes[name][:, m].bitcast(FP8X4), lhsT_scale=w_scales[name][:, m],
                         rhs=table_codes, rhs_scale=table_scales,
-                        start=(g == 0 and t == 0), stop=(g == len(names) - 1 and t == PACK - 1),
+                        start=(g == 0 and t == 0), stop=(g == last and t == PACK - 1),
                     )
             return acc[:].rearrange("p t n -> p n t")
 
-        half = SLOT // 2
-        quarter = SLOT // 4
-        under = slot["d1"] - 4 * LIP
-        ent_at = {(i, s): slot[("b", "a")[s]] + i * quarter for i in range(EARLY - 1) for s in range(2)}
-        ent_at.update({(3, 0): slot["c0"], (3, 1): slot["c1"]})
-        ent_at.update({(4, 1): under, (4, 0): under + quarter, (5, 0): under + half, (5, 1): under + half + quarter})
-        ent_at.update({(6, 0): 9 * SLOT + half, (6, 1): 9 * SLOT + half + quarter})
-        ent_sb = {
-            (i, s): loads.tile([P, CHUNK, PACK], F32, name="ent%d_%d" % (i, s), offset=ent_at[i, s])
+        under = RAW_AT["ri1"] - LIP
+        ent_at = {(i, s): RAW_AT[("ei", "er")[s]] + i * QUARTER for i in range(3) for s in range(2)}
+        ent_at.update({(3, 0): RAW_AT["rr0"], (3, 1): RAW_AT["rr1"]})
+        ent_at.update({(4, 1): under, (4, 0): under + QUARTER, (5, 0): under + 2 * QUARTER, (5, 1): under + 3 * QUARTER})
+        ent_at.update({(6, 0): SIXTH_AT, (6, 1): SIXTH_AT + QUARTER})
+        entity = {
+            (i, s): arena.tile([P, CHUNK, PACK], F32, name="ent%d_%d" % (i, s), offset=ent_at[i, s])
             if (i, s) in ent_at else keep.tile([P, CHUNK, PACK], F32, name="ent%d_%d" % (i, s))
-            for i in range(8) for s in range(2)
+            for i in range(CHUNKS) for s in range(2)
         }
 
-        def entity(i, s):
-            return ent_sb[i, s][:]
-
-        held = {4: ent_at[3, 1], 5: under - quarter, 6: ent_at[5, 1] + J, 7: ent_at[6, 1] + R}
-        held[3] = late
+        arr_at = {
+            ON_GPSIMD: GROUPED_AT["ri1"], 4: ent_at[3, 1], 5: ent_at[4, 1] - QUARTER,
+            6: ent_at[5, 1] + 2 * HALF, 7: ent_at[6, 1] + 4 * CHUNK,
+        }
         with_arr = {
-            i: loads.tile([P, 2, CHUNK, PACK], F32, name="with_arr%d" % i, offset=held[i])
-            if i in held else keep.tile([P, 2, CHUNK, PACK], F32, name="with_arr%d" % i)
-            for i in range(8) if i != 1
+            i: arena.tile([P, 2, CHUNK, PACK], F32, name="with_arr%d" % i, offset=arr_at[i])
+            if i in arr_at else keep.tile([P, 2, CHUNK, PACK], F32, name="with_arr%d" % i)
+            for i in range(CHUNKS) if i != STRADDLING
         }
         straddling = [
             keep.tile([P, CHUNK, PACK], F32, name="straddling0"),
-            loads.tile([P, CHUNK, PACK], F32, name="straddling1", offset=under + SLOT),
+            arena.tile([P, CHUNK, PACK], F32, name="straddling1", offset=under + SLOT),
         ]
+        with_ari = {}
+        arr, ari = {}, {}
 
         def arr_term(i, s):
-            return straddling[s][:] if i == 1 else with_arr[i][:, s]
-
-        terms = {}
+            return straddling[s][:] if i == STRADDLING else with_arr[i][:, s]
 
         def entity_sum(i, s, bank):
             cols = slice(i * CHUNK, (i + 1) * CHUNK)
             within = slice(i % HALF_CHUNKS * CHUNK, (i % HALF_CHUNKS + 1) * CHUNK)
-            ent = [(ent_codes[i // HALF_CHUNKS][:, within].bitcast(FP8X4), ent_sc[8:, cols])]
-            nc.scalar.copy(entity(i, s), project("ent%d_%d" % (i, s), ("ab"[s],), ent, bank, i in TURNED))
+            table = [(ent_codes[i // HALF_CHUNKS][:, within].bitcast(FP8X4), ent_scales[ENT_ROW:, cols])]
+            nc.scalar.copy(entity[i, s][:], project("ent%d_%d" % (i, s), (("er", "ei")[s],), table, bank, i in TURNED))
+
+        def both_entity_sums(i):
+            for s in range(2):
+                entity_sum(i, s, 2 * (i % 2) + s)
 
         def relation(i):
             cols = slice(i * CHUNK, (i + 1) * CHUNK)
             within = slice(i % HALF_CHUNKS * 2 * CHUNK, (i % HALF_CHUNKS + 1) * 2 * CHUNK)
             return [
-                (rel_codes[i // HALF_CHUNKS][:, a, within].bitcast(FP4X4), rel_sc[a][:].bitcast(U8)[:, cols])
+                (rel_codes[i // HALF_CHUNKS][:, a, within].bitcast(FP4X4), rel_scales[a][:].bitcast(U8)[:, cols])
                 for a in range(2)
             ]
 
-        sums = {}
-
         def arr_sum(i):
-            sums["arr", i] = project("arr%d" % i, ("c0", "c1"), relation(i), (4, 4, 5, 6, 5, 4, 5, 4)[i], i in TURNED)
+            bank = ARI_BANK if i == ON_GPSIMD else ARR_BANK + ARR_ORDER.index(i) % 2
+            arr[i] = project("arr%d" % i, ("rr0", "rr1"), relation(i), bank, i in TURNED)
 
         def ari_sum(i):
-            sums["ari", i] = project("ari%d" % i, ("d0", "d1"), relation(i), 6 + i % 2, i in TURNED)
+            ari[i] = project("ari%d" % i, ("ri0", "ri1"), relation(i), ARI_BANK + i % 2, i in TURNED)
 
-        def arr_terms(i, parts=(0, 1)):
+        def arr_products(i, parts=(0, 1)):
             for s in parts:
-                nc.vector.tensor_tensor(arr_term(i, s), sums["arr", i], entity(i, s), MULT)
+                nc.vector.tensor_tensor(arr_term(i, s), arr[i], entity[i, s][:], MULT)
 
-        def ari_terms(i):
-            if i == 7:
-                with_ari = loads.tile([P, 2, CHUNK, PACK], F32, name="with_ari7", offset=slot["c0"] + half)
-            else:
-                with_ari = ring.tile([P, 2, CHUNK, PACK], F32, name="with_ari", bufs=5)
-            ari = sums["ari", i]
-            nc.vector.scalar_tensor_tensor(with_ari[:, 0], ari, -1.0, entity(i, 1), MULT, MULT)
-            nc.vector.tensor_tensor(with_ari[:, 1], ari, entity(i, 0), MULT)
-            if i in TURNED:
-                terms[i] = [[x.rearrange("p n t -> p (n t)") for x in (arr_term(i, s), with_ari[:, s])] for s in range(2)]
-            else:
-                terms[i] = [x[:].rearrange("p s n t -> p s (n t)") for x in (with_arr[i], with_ari)]
+        four_at = RAW_AT["rr0"] + HALF_SLOT
 
-        quantize("b", interleave("b", [on_scalar, on_vector], 3 * P // 8))
+        def ari_products(i):
+            if i == CHUNKS - 1:
+                with_ari[i] = arena.tile([P, 2, CHUNK, PACK], F32, name="with_ari_last", offset=four_at)
+            else:
+                with_ari[i] = ring.tile([P, 2, CHUNK, PACK], F32, name="with_ari", bufs=5)
+            nc.vector.scalar_tensor_tensor(with_ari[i][:, 0], ari[i], -1.0, entity[i, 1][:], MULT, MULT)
+            nc.vector.tensor_tensor(with_ari[i][:, 1], ari[i], entity[i, 0][:], MULT)
+            if i + 2 < CHUNKS:
+                ari_sum(i + 2)
+
+        quantize_weight("ei")
         gather_entities(1)
         for s in range(2):
-            for i in range(EARLY - 1):
-                entity_sum(i, s, (s * (EARLY - 1) + i) % 4)
+            for i in range(3):
+                entity_sum(i, s, (3 * s + i) % 4)
         gather_relations(0)
         gather_relations(1)
         part_relations(0)
-        quantize("c0", interleave("c0", [on_scalar, on_vector], 3 * P // 4))
-        entity_sum(EARLY - 1, 0, 2)
-        quantize("c1", interleave("c1", [on_scalar, on_vector], 3 * P // 8))
-        entity_sum(EARLY - 1, 1, 3)
+        quantize_weight("rr0")
+        entity_sum(3, 0, 2)
+        quantize_weight("rr1")
+        entity_sum(3, 1, 3)
         part_relations(1)
         arr_sum(0)
         arr_sum(2)
-        arr_sum(3)
-        arr_terms(0)
-        arr_sum(1)
-        arr_terms(2)
+        arr_sum(ON_GPSIMD)
+        arr_products(0)
+        arr_sum(STRADDLING)
+        arr_products(2)
         arr_sum(4)
-        arr_terms(1, (0,))
-        quantize_weight("d0", [on_scalar])
-        arr_sb = loads.tile([P, CHUNK, PACK], F32, name="arr_sb", offset=slot["d0"] - quarter + 4 * LIP)
-        nc.scalar.copy(arr_sb[:], sums["arr", 3])
-        quantize("d1", interleave("d1", [on_scalar, on_vector], 5 * P // 8))
+        arr_products(STRADDLING, (0,))
+        quantize_weight("ri0")
+        arr_copy = arena.tile([P, CHUNK, PACK], F32, name="arr_copy", offset=RAW_AT["ri0"] - QUARTER + LIP)
+        nc.scalar.copy(arr_copy[:], arr[ON_GPSIMD])
+        quantize_weight("ri1")
         for s in range(2):
-            nc.gpsimd.tensor_tensor(arr_term(3, s), arr_sb[:], entity(3, s), MULT)
+            nc.gpsimd.tensor_tensor(arr_term(ON_GPSIMD, s), arr_copy[:], entity[ON_GPSIMD, s][:], MULT)
 
-        def quantize_h(h, columns, name, offset=None):
+        def quantize_h(h, columns, name, scales_at=None):
             h_codes = keep.tile([P, columns], U32, name="codes_" + name, align_bytes=64)
-            if offset is None:
+            if scales_at is None:
                 h_scales = keep.tile([P, columns], U8, name="scales_" + name, align_bytes=64)
             else:
-                h_scales = loads.tile([P, columns], U8, name="scales_" + name, offset=offset, align_bytes=64)
+                h_scales = arena.tile([P, columns], U8, name="scales_" + name, offset=scales_at, align_bytes=64)
             nc.vector.quantize_mx(out=h_codes[:].bitcast(FP8X4), scales=h_scales[:], in_=h)
             return h_codes, h_scales
 
-        def hr_hi(quantized, first, tokens):
+        def hr_hi(quantized, tokens):
             h_codes, h_scales = quantized
-            spans = [slice(first + s * tokens, first + (s + 1) * tokens) for s in range(2)]
+            spans = [slice(s * tokens, (s + 1) * tokens) for s in range(2)]
             return [(h_codes[:, span], h_scales[:, span]) for span in spans]
 
         def score_pass(y, u, s, operand, start, stop):
@@ -317,103 +313,109 @@ def tile_list_ckg_sig_kernel(
             nc.tensor.matmul_mx(
                 out=y,
                 lhsT=cand[:, s, :].bitcast(U8)[:, 2 * u * P : 2 * (u + 1) * P].bitcast(FP4X4),
-                lhsT_scale=cand_sc[:, s, :].bitcast(U8)[:, u * P : (u + 1) * P],
+                lhsT_scale=cand_scales[:, s, :].bitcast(U8)[:, u * P : (u + 1) * P],
                 rhs=h_codes.bitcast(FP8X4), rhs_scale=h_scales, start=start, stop=stop,
             )
 
-        def score(y, u, operands):
-            for s in range(2):
-                score_pass(y, u, s, operands[s], s == 0, s == 1)
+        def new_result(shape):
+            return ring.tile(shape, F32, name="result", bufs=8)
 
         def score_chunk(i, operands, bank):
             y = psum.tile([P, N // P, CHUNK], F32, name="y%d" % i, offset=bank * BANK_BYTES)
             for s in range(2):
                 for u in range(N // P):
                     score_pass(y[:, u, :], u, s, operands[s], s == 0 and u == 0, s == 1 and u == N // P - 1)
-            result = ring.tile([P, N // P, CHUNK], F32, name="result", tag="result", bufs=8)
+            result = new_result([P, N // P, CHUNK])
             nc.scalar.activation(result[:], y[:], SIGMOID)
             nc.sync.dma_start(out[:, i * CHUNK : (i + 1) * CHUNK].rearrange("(u p) j -> p u j", p=P), result[:])
 
-        def add_turned(i, banks):
-            totals = []
+        def score_half(u, operands):
+            y = psum.tile([P, HALF], F32, name="y_half%d" % u, offset=u % 3 * BANK_BYTES)
             for s in range(2):
-                total = psum.tile([P, PACK, CHUNK], F32, name="sum%d_%d" % (i, s), offset=banks[s] * BANK_BYTES)
-                for t in range(PACK):
-                    for g in range(2):
-                        nc.tensor.matmul(
-                            total[:, t, :], terms[i][s][g][:, t * P : (t + 1) * P], identity[:],
-                            start=(g == 0), stop=(g == 1), is_transpose=True,
-                        )
-                totals.append(total)
-            return totals
+                score_pass(y[:], u, s, operands[s], s == 0, s == 1)
+            result = new_result([P, HALF])
+            nc.scalar.activation(result[:], y[:], SIGMOID)
+            nc.sync.dma_start(out[u * P : (u + 1) * P, :HALF], result[:])
 
-        def round_sums(h, totals):
+        def new_totals(i, banks):
+            return [
+                psum.tile([P, PACK, CHUNK], F32, name="total%d_%d" % (i, s), offset=banks[s] * BANK_BYTES) for s in range(2)
+            ]
+
+        def turn(total, source, t, start, stop):
+            columns = source.rearrange("p n t -> p (n t)")[:, t * P : (t + 1) * P]
+            nc.tensor.matmul(total[:, t, :], columns, identity[:], start=start, stop=stop, is_transpose=True)
+
+        def round_totals(h, totals):
             for s, total in enumerate(totals):
                 nc.scalar.copy(h[:, s].rearrange("p (n t) -> p n t", t=PACK), total[:].rearrange("p t n -> p n t"))
 
-        def both_sums(i):
+        def add_turned(h, i, banks):
+            totals = new_totals(i, banks)
             for s in range(2):
-                entity_sum(i, s, 2 * (i % 2) + s)
+                for t in range(PACK):
+                    turn(totals[s], arr_term(i, s), t, True, False)
+                    turn(totals[s], with_ari[i][:, s], t, False, True)
+            round_totals(h, totals)
 
-        h_half = loads.tile([P, 2, HALF_CHUNKS, WIDE], BF16, name="h_half", offset=slot["d0"], align_bytes=64)
-        ari_sum(0)
-        ari_sum(1)
-        arr_terms(1, (1,))
-        arr_sum(5)
-        both_sums(4)
-        both_sums(5)
-
-        def with_arr_part(i):
-            arr_terms(i)
-            if i + 2 < 8:
-                arr_sum(i + 2)
-
-        def with_ari_part(i):
-            ari_terms(i)
-            if i + 2 < 8:
-                ari_sum(i + 2)
+        def flat(products):
+            return products[:].rearrange("p s n t -> p s (n t)")
 
         def add_on_gpsimd(h, i):
-            nc.gpsimd.tensor_tensor(h, terms[i][0], terms[i][1], ADD)
+            nc.gpsimd.tensor_tensor(h, flat(with_arr[i]), flat(with_ari[i]), ADD)
 
-        with_ari_part(0)
+        h_half = arena.tile([P, 2, HALF_CHUNKS, WIDE], BF16, name="h_half", offset=RAW_AT["ri0"], align_bytes=64)
+        ari_sum(0)
+        ari_sum(1)
+        arr_products(STRADDLING, (1,))
+        arr_sum(5)
+        both_entity_sums(4)
+        both_entity_sums(5)
+        ari_products(0)
         add_on_gpsimd(h_half[:, :, 0, :], 0)
-        both_sums(6)
-        with_ari_part(1)
-        both_sums(7)
-        round_sums(h_half[:, :, 1, :], add_turned(1, (0, 1)))
-        with_ari_part(2)
+        both_entity_sums(6)
+        ari_products(1)
+        both_entity_sums(7)
+        add_turned(h_half[:, :, 1, :], 1, (0, 1))
+        ari_products(2)
         add_on_gpsimd(h_half[:, :, 2, :], 2)
-        with_ari_part(3)
-        round_sums(h_half[:, :, 3, :], add_turned(3, (2, 3)))
-        with_arr_part(4)
-        with_ari_part(4)
-        h_four = loads.tile([P, 2, WIDE], BF16, name="h_four", offset=slot["c0"] + half, align_bytes=64)
+        ari_products(3)
+        add_turned(h_half[:, :, 3, :], 3, (2, 3))
+
+        arr_products(4)
+        arr_sum(6)
+        ari_products(4)
+        h_four = arena.tile([P, 2, WIDE], BF16, name="h_four", offset=four_at, align_bytes=64)
         add_on_gpsimd(h_four[:], 4)
-        with_arr_part(5)
-        with_ari_part(5)
-        operands = hr_hi(quantize_h(h_half[:].rearrange("p s i w -> p (s i w)"), 2 * HALF, "half", ent_at[5, 1]), 0, HALF)
-        h_five = loads.tile([P, 2, WIDE], BF16, name="h_five", offset=slot["d0"], align_bytes=64)
+        arr_products(5)
+        arr_sum(7)
+        ari_products(5)
+        arr_products(6)
+        totals = new_totals(6, (3, ARR_BANK + 1))
+        for s in range(2):
+            for t in range(PACK):
+                turn(totals[s], arr_term(6, s), t, t == 0, False)
+        half_operands = hr_hi(quantize_h(h_half[:].rearrange("p s i w -> p (s i w)"), 2 * HALF, "half", ent_at[5, 1]), HALF)
+        h_five = arena.tile([P, 2, WIDE], BF16, name="h_five", offset=RAW_AT["ri0"], align_bytes=64)
         add_on_gpsimd(h_five[:], 5)
-        for u in range(N // P):
-            y_half = psum.tile([P, HALF], F32, name="y_half%d" % u, offset=u * BANK_BYTES)
-            score(y_half[:], u, operands)
-            result_half = ring.tile([P, HALF], F32, name="result_half", tag="result", bufs=8)
-            nc.scalar.activation(result_half[:], y_half[:], SIGMOID)
-            nc.sync.dma_start(out[u * P : (u + 1) * P, :HALF], result_half[:])
-        with_arr_part(6)
-        with_ari_part(6)
+        for u in range(N // P - 1):
+            score_half(u, half_operands)
+        ari_products(6)
         h_six = keep.tile([P, 2, WIDE], BF16, name="h_six", align_bytes=64)
-        round_sums(h_six[:], add_turned(6, (5, 6)))
-        with_arr_part(7)
-        for i, h in ((4, h_four), (5, h_five)):
-            single = quantize_h(h[:].rearrange("p s w -> p (s w)"), 2 * CHUNK, "single%d" % i, ent_at[6, 1] + (i - 4) * 2 * CHUNK)
-            score_chunk(i, hr_hi(single, 0, CHUNK), i - 4)
-        with_ari_part(7)
+        for s in range(2):
+            for t in range(PACK):
+                turn(totals[s], with_ari[6][:, s], t, False, t == PACK - 1)
+        round_totals(h_six[:], totals)
+        score_half(N // P - 1, half_operands)
+        arr_products(7)
+
+        for e, h in enumerate((h_four, h_five)):
+            quantized = quantize_h(h[:].rearrange("p s w -> p (s w)"), 2 * CHUNK, "chunk%d" % (4 + e), ent_at[6, 1] + e * 2 * CHUNK)
+            score_chunk(4 + e, hr_hi(quantized, CHUNK), 1 + e)
+        ari_products(7)
         h_last = keep.tile([P, 2, WIDE], BF16, name="h_last", align_bytes=64)
-        nc.vector.tensor_tensor(h_last[:, 0], terms[7][0][:, 0], terms[7][1][:, 0], ADD)
-        single = quantize_h(h_six[:].rearrange("p s w -> p (s w)"), 2 * CHUNK, "six")
-        score_chunk(6, hr_hi(single, 0, CHUNK), 2)
-        nc.vector.tensor_tensor(h_last[:, 1], terms[7][0][:, 1], terms[7][1][:, 1], ADD)
-        apart = [quantize_h(h_last[:, s], CHUNK, "seven%d" % s) for s in range(2)]
-        score_chunk(7, [(h_codes[:], h_scales[:]) for h_codes, h_scales in apart], 3)
+        score_chunk(6, hr_hi(quantize_h(h_six[:].rearrange("p s w -> p (s w)"), 2 * CHUNK, "chunk6"), CHUNK), ARR_BANK)
+        for s in range(2):
+            nc.vector.tensor_tensor(h_last[:, s], flat(with_arr[7])[:, s], flat(with_ari[7])[:, s], ADD)
+        apart = [quantize_h(h_last[:, s], CHUNK, "last%d" % s) for s in range(2)]
+        score_chunk(7, [(h_codes[:], h_scales[:]) for h_codes, h_scales in apart], ARI_BANK)

@@ -30,13 +30,14 @@ HALF_CHUNKS = HALF // CHUNK
 BANK_BYTES = 2048
 ENT_ROW = 8
 
-TURNED = (1, 3, 6)
+TURNED = (1, 4)
 STRADDLING = 1
-ON_GPSIMD = 3
-ARR_ORDER = (0, 2, STRADDLING, 4, 5, 6, 7)
+ON_GPSIMD = 4
+ARR_ORDER = (0, 2, 3, STRADDLING, 5, 6, 7)
+ARI_ORDER = (0, 2, 3, 1, 4, 5, 6, 7)
 ARR_BANK, ARI_BANK = 4, 6
 
-SCALAR_SHARE = {"er": P, "ei": 3 * P // 8, "rr0": 3 * P // 4, "rr1": 3 * P // 8, "ri0": P, "ri1": 5 * P // 8}
+SCALAR_SHARE = {"er": P, "ei": 3 * P // 8, "rr0": 3 * P // 4, "rr1": 3 * P // 8, "ri1": P}
 
 SLOT = 4 * T
 HALF_SLOT = SLOT // 2
@@ -50,10 +51,9 @@ RAW_AT = {
     "er": 0, "ei": ENT_WORDS_AT + SLOT, "rr0": ENT_WORDS_AT + 2 * SLOT, "rr1": ENT_WORDS_AT + 3 * SLOT,
     "ri0": WINDOW_AT - SLOT, "ri1": WINDOW_AT + SLOT,
 }
-SIXTH_AT = 9 * SLOT + HALF_SLOT
 GROUPED_AT = {
     "er": 10 * SLOT + HALF_SLOT, "rr0": 10 * SLOT + HALF_SLOT, "ri1": 11 * SLOT, "ei": 12 * SLOT,
-    "rr1": 12 * SLOT + HALF_SLOT,
+    "rr1": 12 * SLOT + HALF_SLOT, "ri0": 13 * SLOT,
 }
 
 
@@ -102,7 +102,10 @@ def tile_list_ckg_sig_kernel(
             keep.tile([P, HALF], U32, name="ent_codes0", align_bytes=64),
             arena.tile([P, HALF], U32, name="ent_codes1", offset=RAW_AT["ei"] + 3 * QUARTER, align_bytes=64),
         ]
-        rel_pairs = [keep.tile([P, HALF], U32, name="rel_pairs%d" % e, align_bytes=64) for e in range(2)]
+        rel_pairs = [
+            keep.tile([P, HALF], U32, name="rel_pairs0", align_bytes=64),
+            arena.tile([P, HALF], U32, name="rel_pairs1", offset=GROUPED_AT["ri0"], align_bytes=64),
+        ]
         rel_codes = [
             keep.tile([P, 2, 2 * HALF], U8, name="rel_codes0", align_bytes=64),
             arena.tile([P, 2, 2 * HALF], U8, name="rel_codes1", offset=RAW_AT["rr1"] + HALF_SLOT, align_bytes=64),
@@ -126,16 +129,18 @@ def tile_list_ckg_sig_kernel(
         w_scales = {name: keep.tile([P, R], U8, name="scales_" + name, align_bytes=64) for name in passes}
 
         def quantize_weight(name):
-            if name in GROUPED_AT:
-                grouped = arena.tile([P, PACK * R], BF16, name="grouped_" + name, offset=GROUPED_AT[name], align_bytes=64)
+            grouped = arena.tile([P, PACK * R], BF16, name="grouped_" + name, offset=GROUPED_AT[name], align_bytes=64)
+            if name in SCALAR_SHARE:
+                dst = grouped[:].rearrange("p (t m e) -> p m e t", t=PACK, e=PACK)
+                src = raw[name][:].rearrange("p e (m t) -> p m e t", t=PACK)
+                share = SCALAR_SHARE[name]
+                nc.scalar.copy(dst[:, :share], src[:, :share])
+                if share < P:
+                    nc.vector.tensor_copy(dst[:, share:], src[:, share:])
             else:
-                grouped = ring.tile([P, PACK * R], BF16, name="grouped", align_bytes=64)
-            dst = grouped[:].rearrange("p (t m e) -> p m e t", t=PACK, e=PACK)
-            src = raw[name][:].rearrange("p e (m t) -> p m e t", t=PACK)
-            share = SCALAR_SHARE[name]
-            nc.scalar.copy(dst[:, :share], src[:, :share])
-            if share < P:
-                nc.vector.tensor_copy(dst[:, share:], src[:, share:])
+                dst = grouped[:].rearrange("p (t m e) -> p m t e", t=PACK, e=PACK)
+                src = raw[name][:].rearrange("p e (m t) -> p m t e", t=PACK)
+                nc.gpsimd.tensor_scalar(dst, src, 1.0, 0.0, MULT, ADD)
             nc.vector.quantize_mx(out=w_codes[name][:].bitcast(FP8X4), scales=w_scales[name][:], in_=grouped[:])
 
         nc.sync.dma_start(ent_list[:], offs)
@@ -195,11 +200,12 @@ def tile_list_ckg_sig_kernel(
                     )
             return acc[:].rearrange("p t n -> p n t")
 
-        under = RAW_AT["ri1"] - LIP
         ent_at = {(i, s): RAW_AT[("ei", "er")[s]] + i * QUARTER for i in range(3) for s in range(2)}
-        ent_at.update({(3, 0): RAW_AT["rr0"], (3, 1): RAW_AT["rr1"]})
-        ent_at.update({(4, 1): under, (4, 0): under + QUARTER, (5, 0): under + 2 * QUARTER, (5, 1): under + 3 * QUARTER})
-        ent_at.update({(6, 0): SIXTH_AT, (6, 1): SIXTH_AT + QUARTER})
+        ent_at.update({(4, 0): RAW_AT["rr0"], (4, 1): RAW_AT["rr1"]})
+        ent_at.update({(3, 0): RAW_AT["rr1"] + QUARTER, (3, 1): GROUPED_AT["rr1"]})
+        under = RAW_AT["ri1"] - LIP
+        ent_at.update({(6, 0): under + QUARTER, (5, 0): under + 2 * QUARTER, (5, 1): under + 3 * QUARTER})
+        ent_at[6, 1] = GROUPED_AT["ri1"] + LIP
         entity = {
             (i, s): arena.tile([P, CHUNK, PACK], F32, name="ent%d_%d" % (i, s), offset=ent_at[i, s])
             if (i, s) in ent_at else keep.tile([P, CHUNK, PACK], F32, name="ent%d_%d" % (i, s))
@@ -207,23 +213,27 @@ def tile_list_ckg_sig_kernel(
         }
 
         arr_at = {
-            ON_GPSIMD: GROUPED_AT["ri1"], 4: ent_at[3, 1], 5: ent_at[4, 1] - QUARTER,
-            6: ent_at[5, 1] + 2 * HALF, 7: ent_at[6, 1] + 4 * CHUNK,
+            6: ent_at[5, 1] + QUARTER - LIP, 7: ent_at[6, 1],
         }
         with_arr = {
             i: arena.tile([P, 2, CHUNK, PACK], F32, name="with_arr%d" % i, offset=arr_at[i])
             if i in arr_at else keep.tile([P, 2, CHUNK, PACK], F32, name="with_arr%d" % i)
-            for i in range(CHUNKS) if i != STRADDLING
+            for i in range(CHUNKS) if i not in TURNED
         }
-        straddling = [
-            keep.tile([P, CHUNK, PACK], F32, name="straddling0"),
-            arena.tile([P, CHUNK, PACK], F32, name="straddling1", offset=under + SLOT),
-        ]
+        apart_at = {
+            (STRADDLING, 1): under + SLOT,
+            (ON_GPSIMD, 0): GROUPED_AT["ri0"], (ON_GPSIMD, 1): GROUPED_AT["ri1"] + LIP - QUARTER,
+        }
+        apart = {
+            (i, s): arena.tile([P, CHUNK, PACK], F32, name="apart%d_%d" % (i, s), offset=apart_at[i, s])
+            if (i, s) in apart_at else keep.tile([P, CHUNK, PACK], F32, name="apart%d_%d" % (i, s))
+            for i in TURNED for s in range(2)
+        }
         with_ari = {}
         arr, ari = {}, {}
 
         def arr_term(i, s):
-            return straddling[s][:] if i == STRADDLING else with_arr[i][:, s]
+            return apart[i, s][:] if i in TURNED else with_arr[i][:, s]
 
         def entity_sum(i, s, bank):
             cols = slice(i * CHUNK, (i + 1) * CHUNK)
@@ -231,9 +241,9 @@ def tile_list_ckg_sig_kernel(
             table = [(ent_codes[i // HALF_CHUNKS][:, within].bitcast(FP8X4), ent_scales[ENT_ROW:, cols])]
             nc.scalar.copy(entity[i, s][:], project("ent%d_%d" % (i, s), (("er", "ei")[s],), table, bank, i in TURNED))
 
-        def both_entity_sums(i):
+        def both_entity_sums(i, bank):
             for s in range(2):
-                entity_sum(i, s, 2 * (i % 2) + s)
+                entity_sum(i, s, bank + s)
 
         def relation(i):
             cols = slice(i * CHUNK, (i + 1) * CHUNK)
@@ -248,23 +258,20 @@ def tile_list_ckg_sig_kernel(
             arr[i] = project("arr%d" % i, ("rr0", "rr1"), relation(i), bank, i in TURNED)
 
         def ari_sum(i):
-            ari[i] = project("ari%d" % i, ("ri0", "ri1"), relation(i), ARI_BANK + i % 2, i in TURNED)
+            ari[i] = project("ari%d" % i, ("ri0", "ri1"), relation(i), ARI_BANK + ARI_ORDER.index(i) % 2, i in TURNED)
 
         def arr_products(i, parts=(0, 1)):
             for s in parts:
                 nc.vector.tensor_tensor(arr_term(i, s), arr[i], entity[i, s][:], MULT)
 
-        four_at = RAW_AT["rr0"] + HALF_SLOT
-
-        def ari_products(i):
-            if i == CHUNKS - 1:
-                with_ari[i] = arena.tile([P, 2, CHUNK, PACK], F32, name="with_ari_last", offset=four_at)
-            else:
+        def ari_products(i, parts=(0, 1)):
+            if 0 in parts:
                 with_ari[i] = ring.tile([P, 2, CHUNK, PACK], F32, name="with_ari", bufs=5)
-            nc.vector.scalar_tensor_tensor(with_ari[i][:, 0], ari[i], -1.0, entity[i, 1][:], MULT, MULT)
-            nc.vector.tensor_tensor(with_ari[i][:, 1], ari[i], entity[i, 0][:], MULT)
-            if i + 2 < CHUNKS:
-                ari_sum(i + 2)
+                nc.vector.scalar_tensor_tensor(with_ari[i][:, 0], ari[i], -1.0, entity[i, 1][:], MULT, MULT)
+            if 1 in parts:
+                nc.vector.tensor_tensor(with_ari[i][:, 1], ari[i], entity[i, 0][:], MULT)
+                if ARI_ORDER.index(i) + 2 < CHUNKS:
+                    ari_sum(ARI_ORDER[ARI_ORDER.index(i) + 2])
 
         quantize_weight("ei")
         gather_entities(1)
@@ -275,38 +282,53 @@ def tile_list_ckg_sig_kernel(
         gather_relations(1)
         part_relations(0)
         quantize_weight("rr0")
-        entity_sum(3, 0, 2)
+        entity_sum(4, 0, 2)
         quantize_weight("rr1")
-        entity_sum(3, 1, 3)
+        entity_sum(4, 1, 3)
         part_relations(1)
         arr_sum(0)
         arr_sum(2)
         arr_sum(ON_GPSIMD)
         arr_products(0)
-        arr_sum(STRADDLING)
+        arr_sum(3)
+        both_entity_sums(3, 0)
         arr_products(2)
-        arr_sum(4)
-        arr_products(STRADDLING, (0,))
+        arr_sum(STRADDLING)
+        def copy_arr(i, at):
+            arr_copy[i] = arena.tile([P, CHUNK, PACK], F32, name="arr_copy%d" % i, offset=at)
+            nc.scalar.copy(arr_copy[i][:], arr[i])
+
+        def arr_product_on_gpsimd(i, s):
+            nc.gpsimd.tensor_tensor(arr_term(i, s), arr_copy[i][:], entity[i, s][:], MULT)
+
+        arr_copy = {}
+        copy_arr(ON_GPSIMD, RAW_AT["rr1"] + 3 * QUARTER)
         quantize_weight("ri0")
-        arr_copy = arena.tile([P, CHUNK, PACK], F32, name="arr_copy", offset=RAW_AT["ri0"] - QUARTER + LIP)
-        nc.scalar.copy(arr_copy[:], arr[ON_GPSIMD])
+        arr_products(3, (0,))
+        arr_product_on_gpsimd(ON_GPSIMD, 0)
+        arr_products(3, (1,))
+        arr_sum(5)
+        arr_products(STRADDLING, (0,))
         quantize_weight("ri1")
-        for s in range(2):
-            nc.gpsimd.tensor_tensor(arr_term(ON_GPSIMD, s), arr_copy[:], entity[ON_GPSIMD, s][:], MULT)
+        arr_products(STRADDLING, (1,))
+        arr_product_on_gpsimd(ON_GPSIMD, 1)
 
-        def quantize_h(h, columns, name, scales_at=None):
-            h_codes = keep.tile([P, columns], U32, name="codes_" + name, align_bytes=64)
+        h_at = {i: RAW_AT["ri0"] + i * QUARTER for i in range(HALF_CHUNKS)}
+        h_at.update({4: GROUPED_AT["ei"], 5: h_at[3], 6: RAW_AT["rr0"] + HALF_SLOT, 7: RAW_AT["rr0"] + 3 * QUARTER})
+        h = {i: arena.tile([P, 2, WIDE], BF16, name="h%d" % i, offset=at, align_bytes=64)[:] for i, at in h_at.items()}
+
+        def quantize_h(chunks, scales_at=None):
+            shape = [P, 2, len(chunks) * CHUNK]
+            h_codes = keep.tile(shape, U32, name="codes_h%d" % chunks[0], align_bytes=64)
             if scales_at is None:
-                h_scales = keep.tile([P, columns], U8, name="scales_" + name, align_bytes=64)
+                h_scales = keep.tile(shape, U8, name="scales_h%d" % chunks[0], align_bytes=64)
             else:
-                h_scales = arena.tile([P, columns], U8, name="scales_" + name, offset=scales_at, align_bytes=64)
-            nc.vector.quantize_mx(out=h_codes[:].bitcast(FP8X4), scales=h_scales[:], in_=h)
-            return h_codes, h_scales
-
-        def hr_hi(quantized, tokens):
-            h_codes, h_scales = quantized
-            spans = [slice(s * tokens, (s + 1) * tokens) for s in range(2)]
-            return [(h_codes[:, span], h_scales[:, span]) for span in spans]
+                h_scales = arena.tile(shape, U8, name="scales_h%d" % chunks[0], offset=scales_at, align_bytes=64)
+            for e, i in enumerate(chunks):
+                cols = slice(e * CHUNK, (e + 1) * CHUNK)
+                for s in range(2):
+                    nc.vector.quantize_mx(out=h_codes[:, s, cols].bitcast(FP8X4), scales=h_scales[:, s, cols], in_=h[i][:, s])
+            return [(h_codes[:, s], h_scales[:, s]) for s in range(2)]
 
         def score_pass(y, u, s, operand, start, stop):
             h_codes, h_scales = operand
@@ -317,25 +339,18 @@ def tile_list_ckg_sig_kernel(
                 rhs=h_codes.bitcast(FP8X4), rhs_scale=h_scales, start=start, stop=stop,
             )
 
-        def new_result(shape):
-            return ring.tile(shape, F32, name="result", bufs=8)
-
-        def score_chunk(i, operands, bank):
-            y = psum.tile([P, N // P, CHUNK], F32, name="y%d" % i, offset=bank * BANK_BYTES)
-            for s in range(2):
-                for u in range(N // P):
-                    score_pass(y[:, u, :], u, s, operands[s], s == 0 and u == 0, s == 1 and u == N // P - 1)
-            result = new_result([P, N // P, CHUNK])
-            nc.scalar.activation(result[:], y[:], SIGMOID)
-            nc.sync.dma_start(out[:, i * CHUNK : (i + 1) * CHUNK].rearrange("(u p) j -> p u j", p=P), result[:])
-
-        def score_half(u, operands):
-            y = psum.tile([P, HALF], F32, name="y_half%d" % u, offset=u % 3 * BANK_BYTES)
-            for s in range(2):
-                score_pass(y[:], u, s, operands[s], s == 0, s == 1)
-            result = new_result([P, HALF])
-            nc.scalar.activation(result[:], y[:], SIGMOID)
-            nc.sync.dma_start(out[u * P : (u + 1) * P, :HALF], result[:])
+        def score(first, tokens, operands, banks):
+            blocks = N // P // len(banks)
+            for b, bank in enumerate(banks):
+                y = psum.tile([P, blocks, tokens], F32, name="y%d_%d" % (first, b), offset=bank * BANK_BYTES)
+                for s in range(2):
+                    for u in range(blocks):
+                        score_pass(y[:, u, :], b * blocks + u, s, operands[s], s == 0 and u == 0, s == 1 and u == blocks - 1)
+                result = keep.tile([P, blocks, tokens], F32, name="result%d_%d" % (first, b))
+                nc.scalar.activation(result[:], y[:], SIGMOID)
+                rows = slice(b * blocks * P, (b + 1) * blocks * P)
+                cols = slice(first * CHUNK, first * CHUNK + tokens)
+                nc.sync.dma_start(out[rows, cols].rearrange("(u p) j -> p u j", p=P), result[:])
 
         def new_totals(i, banks):
             return [
@@ -346,76 +361,65 @@ def tile_list_ckg_sig_kernel(
             columns = source.rearrange("p n t -> p (n t)")[:, t * P : (t + 1) * P]
             nc.tensor.matmul(total[:, t, :], columns, identity[:], start=start, stop=stop, is_transpose=True)
 
-        def round_totals(h, totals):
-            for s, total in enumerate(totals):
-                nc.scalar.copy(h[:, s].rearrange("p (n t) -> p n t", t=PACK), total[:].rearrange("p t n -> p n t"))
+        totals = {}
 
-        def add_turned(h, i, banks):
-            totals = new_totals(i, banks)
+        def turn_arr_terms(i, banks):
+            totals[i] = new_totals(i, banks)
             for s in range(2):
                 for t in range(PACK):
-                    turn(totals[s], arr_term(i, s), t, True, False)
-                    turn(totals[s], with_ari[i][:, s], t, False, True)
-            round_totals(h, totals)
+                    turn(totals[i][s], arr_term(i, s), t, t == 0, False)
+
+        def add_turned(i):
+            for s in range(2):
+                for t in range(PACK):
+                    turn(totals[i][s], with_ari[i][:, s], t, False, t == PACK - 1)
+            for s, total in enumerate(totals[i]):
+                nc.scalar.copy(h[i][:, s].rearrange("p (n t) -> p n t", t=PACK), total[:].rearrange("p t n -> p n t"))
 
         def flat(products):
             return products[:].rearrange("p s n t -> p s (n t)")
 
-        def add_on_gpsimd(h, i):
-            nc.gpsimd.tensor_tensor(h, flat(with_arr[i]), flat(with_ari[i]), ADD)
+        def add_on_gpsimd(i):
+            nc.gpsimd.tensor_tensor(h[i], flat(with_arr[i]), flat(with_ari[i]), ADD)
 
-        h_half = arena.tile([P, 2, HALF_CHUNKS, WIDE], BF16, name="h_half", offset=RAW_AT["ri0"], align_bytes=64)
+        def add_on_vector(i):
+            for s in range(2):
+                nc.vector.tensor_tensor(h[i][:, s], flat(with_arr[i])[:, s], flat(with_ari[i])[:, s], ADD)
+
         ari_sum(0)
-        ari_sum(1)
-        arr_products(STRADDLING, (1,))
-        arr_sum(5)
-        both_entity_sums(4)
-        both_entity_sums(5)
+        ari_sum(2)
+        entity_sum(5, 0, 2)
+        copy_arr(5, under)
+        arr_product_on_gpsimd(5, 0)
+        entity_sum(5, 1, 3)
         ari_products(0)
-        add_on_gpsimd(h_half[:, :, 0, :], 0)
-        both_entity_sums(6)
-        ari_products(1)
-        both_entity_sums(7)
-        add_turned(h_half[:, :, 1, :], 1, (0, 1))
+        add_on_gpsimd(0)
+        both_entity_sums(6, 0)
         ari_products(2)
-        add_on_gpsimd(h_half[:, :, 2, :], 2)
-        ari_products(3)
-        add_turned(h_half[:, :, 3, :], 3, (2, 3))
-
-        arr_products(4)
+        add_on_gpsimd(2)
+        both_entity_sums(7, 2)
         arr_sum(6)
+        ari_products(3)
+        add_on_gpsimd(3)
+        ari_products(1)
+        turn_arr_terms(1, (0, 1))
         ari_products(4)
-        h_four = arena.tile([P, 2, WIDE], BF16, name="h_four", offset=four_at, align_bytes=64)
-        add_on_gpsimd(h_four[:], 4)
-        arr_products(5)
+        add_turned(1)
+        turn_arr_terms(4, (2, 3))
+        arr_products(5, (1,))
         arr_sum(7)
         ari_products(5)
+        add_turned(4)
         arr_products(6)
-        totals = new_totals(6, (3, ARR_BANK + 1))
-        for s in range(2):
-            for t in range(PACK):
-                turn(totals[s], arr_term(6, s), t, t == 0, False)
-        half_operands = hr_hi(quantize_h(h_half[:].rearrange("p s i w -> p (s i w)"), 2 * HALF, "half", ent_at[5, 1]), HALF)
-        h_five = arena.tile([P, 2, WIDE], BF16, name="h_five", offset=RAW_AT["ri0"], align_bytes=64)
-        add_on_gpsimd(h_five[:], 5)
-        for u in range(N // P - 1):
-            score_half(u, half_operands)
+        operands = quantize_h((0, 1, 2, 3), ent_at[5, 0])
+        add_on_gpsimd(5)
+        score(0, HALF, operands, (0, 1, 2, 3))
         ari_products(6)
-        h_six = keep.tile([P, 2, WIDE], BF16, name="h_six", align_bytes=64)
-        for s in range(2):
-            for t in range(PACK):
-                turn(totals[s], with_ari[6][:, s], t, False, t == PACK - 1)
-        round_totals(h_six[:], totals)
-        score_half(N // P - 1, half_operands)
         arr_products(7)
-
-        for e, h in enumerate((h_four, h_five)):
-            quantized = quantize_h(h[:].rearrange("p s w -> p (s w)"), 2 * CHUNK, "chunk%d" % (4 + e), ent_at[6, 1] + e * 2 * CHUNK)
-            score_chunk(4 + e, hr_hi(quantized, CHUNK), 1 + e)
         ari_products(7)
-        h_last = keep.tile([P, 2, WIDE], BF16, name="h_last", align_bytes=64)
-        score_chunk(6, hr_hi(quantize_h(h_six[:].rearrange("p s w -> p (s w)"), 2 * CHUNK, "chunk6"), CHUNK), ARR_BANK)
-        for s in range(2):
-            nc.vector.tensor_tensor(h_last[:, s], flat(with_arr[7])[:, s], flat(with_ari[7])[:, s], ADD)
-        apart = [quantize_h(h_last[:, s], CHUNK, "last%d" % s) for s in range(2)]
-        score_chunk(7, [(h_codes[:], h_scales[:]) for h_codes, h_scales in apart], ARI_BANK)
+        score(4, 2 * CHUNK, quantize_h((4, 5), ent_at[6, 0]), (ARR_BANK, ARR_BANK + 1))
+        add_on_vector(6)
+        nc.vector.tensor_tensor(h[7][:, 0], flat(with_arr[7])[:, 0], flat(with_ari[7])[:, 0], ADD)
+        score(6, CHUNK, quantize_h((6,)), (ARI_BANK,))
+        nc.vector.tensor_tensor(h[7][:, 1], flat(with_arr[7])[:, 1], flat(with_ari[7])[:, 1], ADD)
+        score(7, CHUNK, quantize_h((7,)), (ARI_BANK + 1,))

@@ -36,8 +36,9 @@ ON_GPSIMD = 4
 ARR_ORDER = (0, 2, 3, STRADDLING, 5, 6, 7)
 ARI_ORDER = (0, 2, 3, 1, 4, 5, 6, 7)
 ARR_BANK, ARI_BANK = 4, 6
+ARI_BANKS = (6, 7, 5)
 
-SCALAR_SHARE = {"er": P, "ei": 3 * P // 8, "rr0": 3 * P // 4, "rr1": 3 * P // 8, "ri1": P}
+SCALAR_SHARE = {"er": P, "ei": 3 * P // 8, "rr0": 3 * P // 4, "rr1": 3 * P // 8, "ri0": P // 4, "ri1": P}
 
 SLOT = 4 * T
 HALF_SLOT = SLOT // 2
@@ -130,17 +131,15 @@ def tile_list_ckg_sig_kernel(
 
         def quantize_weight(name):
             grouped = arena.tile([P, PACK * R], BF16, name="grouped_" + name, offset=GROUPED_AT[name], align_bytes=64)
-            if name in SCALAR_SHARE:
-                dst = grouped[:].rearrange("p (t m e) -> p m e t", t=PACK, e=PACK)
-                src = raw[name][:].rearrange("p e (m t) -> p m e t", t=PACK)
-                share = SCALAR_SHARE[name]
-                nc.scalar.copy(dst[:, :share], src[:, :share])
-                if share < P:
-                    nc.vector.tensor_copy(dst[:, share:], src[:, share:])
-            else:
-                dst = grouped[:].rearrange("p (t m e) -> p m t e", t=PACK, e=PACK)
-                src = raw[name][:].rearrange("p e (m t) -> p m t e", t=PACK)
+            dst = grouped[:].rearrange("p (t m e) -> p m e t", t=PACK, e=PACK)
+            src = raw[name][:].rearrange("p e (m t) -> p m e t", t=PACK)
+            share = SCALAR_SHARE[name]
+            nc.scalar.copy(dst[:, :share], src[:, :share])
+            if name == "ri0":
+                dst, src = (side[:, share:].rearrange("p m e t -> p m t e") for side in (dst, src))
                 nc.gpsimd.tensor_scalar(dst, src, 1.0, 0.0, MULT, ADD)
+            elif share < P:
+                nc.vector.tensor_copy(dst[:, share:], src[:, share:])
             nc.vector.quantize_mx(out=w_codes[name][:].bitcast(FP8X4), scales=w_scales[name][:], in_=grouped[:])
 
         nc.sync.dma_start(ent_list[:], offs)
@@ -205,6 +204,7 @@ def tile_list_ckg_sig_kernel(
         ent_at.update({(3, 0): RAW_AT["rr1"] + QUARTER, (3, 1): GROUPED_AT["rr1"]})
         under = RAW_AT["ri1"] - LIP
         ent_at.update({(6, 0): under + QUARTER, (5, 0): under + 2 * QUARTER, (5, 1): under + 3 * QUARTER})
+        ent_at[7, 1] = RAW_AT["rr0"] + QUARTER
         ent_at[6, 1] = GROUPED_AT["ri1"] + LIP
         entity = {
             (i, s): arena.tile([P, CHUNK, PACK], F32, name="ent%d_%d" % (i, s), offset=ent_at[i, s])
@@ -218,7 +218,7 @@ def tile_list_ckg_sig_kernel(
         with_arr = {
             i: arena.tile([P, 2, CHUNK, PACK], F32, name="with_arr%d" % i, offset=arr_at[i])
             if i in arr_at else keep.tile([P, 2, CHUNK, PACK], F32, name="with_arr%d" % i)
-            for i in range(CHUNKS) if i not in TURNED
+            for i in range(CHUNKS) if i not in (STRADDLING, ON_GPSIMD)
         }
         apart_at = {
             (STRADDLING, 1): under + SLOT,
@@ -227,13 +227,13 @@ def tile_list_ckg_sig_kernel(
         apart = {
             (i, s): arena.tile([P, CHUNK, PACK], F32, name="apart%d_%d" % (i, s), offset=apart_at[i, s])
             if (i, s) in apart_at else keep.tile([P, CHUNK, PACK], F32, name="apart%d_%d" % (i, s))
-            for i in TURNED for s in range(2)
+            for i in (STRADDLING, ON_GPSIMD) for s in range(2)
         }
         with_ari = {}
         arr, ari = {}, {}
 
         def arr_term(i, s):
-            return apart[i, s][:] if i in TURNED else with_arr[i][:, s]
+            return apart[i, s][:] if (i, s) in apart else with_arr[i][:, s]
 
         def entity_sum(i, s, bank):
             cols = slice(i * CHUNK, (i + 1) * CHUNK)
@@ -254,11 +254,11 @@ def tile_list_ckg_sig_kernel(
             ]
 
         def arr_sum(i):
-            bank = ARI_BANK if i == ON_GPSIMD else ARR_BANK + ARR_ORDER.index(i) % 2
+            bank = ARI_BANK if i == ON_GPSIMD else ARR_BANK + (ARR_ORDER.index(i) % 2 if i < 5 else i == 7)
             arr[i] = project("arr%d" % i, ("rr0", "rr1"), relation(i), bank, i in TURNED)
 
         def ari_sum(i):
-            ari[i] = project("ari%d" % i, ("ri0", "ri1"), relation(i), ARI_BANK + ARI_ORDER.index(i) % 2, i in TURNED)
+            ari[i] = project("ari%d" % i, ("ri0", "ri1"), relation(i), ARI_BANKS[ARI_ORDER.index(i) % 3], i in TURNED)
 
         def arr_products(i, parts=(0, 1)):
             for s in parts:
@@ -270,8 +270,7 @@ def tile_list_ckg_sig_kernel(
                 nc.vector.scalar_tensor_tensor(with_ari[i][:, 0], ari[i], -1.0, entity[i, 1][:], MULT, MULT)
             if 1 in parts:
                 nc.vector.tensor_tensor(with_ari[i][:, 1], ari[i], entity[i, 0][:], MULT)
-                if ARI_ORDER.index(i) + 2 < CHUNKS:
-                    ari_sum(ARI_ORDER[ARI_ORDER.index(i) + 2])
+
 
         quantize_weight("ei")
         gather_entities(1)
@@ -292,8 +291,7 @@ def tile_list_ckg_sig_kernel(
         arr_products(0)
         arr_sum(3)
         both_entity_sums(3, 0)
-        arr_products(2)
-        arr_sum(STRADDLING)
+
         def copy_arr(i, at):
             arr_copy[i] = arena.tile([P, CHUNK, PACK], F32, name="arr_copy%d" % i, offset=at)
             nc.scalar.copy(arr_copy[i][:], arr[i])
@@ -302,11 +300,12 @@ def tile_list_ckg_sig_kernel(
             nc.gpsimd.tensor_tensor(arr_term(i, s), arr_copy[i][:], entity[i, s][:], MULT)
 
         arr_copy = {}
-        copy_arr(ON_GPSIMD, RAW_AT["rr1"] + 3 * QUARTER)
+        arr_products(2)
+        arr_sum(STRADDLING)
         quantize_weight("ri0")
-        arr_products(3, (0,))
+        copy_arr(ON_GPSIMD, RAW_AT["rr1"] + 3 * QUARTER)
         arr_product_on_gpsimd(ON_GPSIMD, 0)
-        arr_products(3, (1,))
+        arr_products(3)
         arr_sum(5)
         arr_products(STRADDLING, (0,))
         quantize_weight("ri1")
@@ -314,18 +313,19 @@ def tile_list_ckg_sig_kernel(
         arr_product_on_gpsimd(ON_GPSIMD, 1)
 
         h_at = {i: RAW_AT["ri0"] + i * QUARTER for i in range(HALF_CHUNKS)}
-        h_at.update({4: GROUPED_AT["ei"], 5: h_at[3], 6: RAW_AT["rr0"] + HALF_SLOT, 7: RAW_AT["rr0"] + 3 * QUARTER})
+        h_at.update({4: GROUPED_AT["ei"], 5: h_at[1], 6: RAW_AT["rr0"] + HALF_SLOT, 7: RAW_AT["rr0"] + 3 * QUARTER})
         h = {i: arena.tile([P, 2, WIDE], BF16, name="h%d" % i, offset=at, align_bytes=64)[:] for i, at in h_at.items()}
 
         def quantize_h(chunks, scales_at=None):
             shape = [P, 2, len(chunks) * CHUNK]
+            first = min(chunks)
             h_codes = keep.tile(shape, U32, name="codes_h%d" % chunks[0], align_bytes=64)
             if scales_at is None:
                 h_scales = keep.tile(shape, U8, name="scales_h%d" % chunks[0], align_bytes=64)
             else:
                 h_scales = arena.tile(shape, U8, name="scales_h%d" % chunks[0], offset=scales_at, align_bytes=64)
-            for e, i in enumerate(chunks):
-                cols = slice(e * CHUNK, (e + 1) * CHUNK)
+            for i in chunks:
+                cols = slice((i - first) * CHUNK, (i - first + 1) * CHUNK)
                 for s in range(2):
                     nc.vector.quantize_mx(out=h_codes[:, s, cols].bitcast(FP8X4), scales=h_scales[:, s, cols], in_=h[i][:, s])
             return [(h_codes[:, s], h_scales[:, s]) for s in range(2)]
@@ -339,9 +339,10 @@ def tile_list_ckg_sig_kernel(
                 rhs=h_codes.bitcast(FP8X4), rhs_scale=h_scales, start=start, stop=stop,
             )
 
-        def score(first, tokens, operands, banks):
+        def score(first, tokens, operands, banks, parts=None):
             blocks = N // P // len(banks)
-            for b, bank in enumerate(banks):
+            for b in parts or range(len(banks)):
+                bank = banks[b]
                 y = psum.tile([P, blocks, tokens], F32, name="y%d_%d" % (first, b), offset=bank * BANK_BYTES)
                 for s in range(2):
                     for u in range(blocks):
@@ -382,44 +383,53 @@ def tile_list_ckg_sig_kernel(
         def add_on_gpsimd(i):
             nc.gpsimd.tensor_tensor(h[i], flat(with_arr[i]), flat(with_ari[i]), ADD)
 
-        def add_on_vector(i):
-            for s in range(2):
+        with_six = ent_at[5, 0]
+
+        def add_on_vector(i, parts=(0, 1)):
+            for s in parts:
                 nc.vector.tensor_tensor(h[i][:, s], flat(with_arr[i])[:, s], flat(with_ari[i])[:, s], ADD)
 
         ari_sum(0)
         ari_sum(2)
+        ari_sum(3)
         entity_sum(5, 0, 2)
         copy_arr(5, under)
         arr_product_on_gpsimd(5, 0)
         entity_sum(5, 1, 3)
+        both_entity_sums(6, 0)
+        both_entity_sums(7, 2)
         ari_products(0)
         add_on_gpsimd(0)
-        both_entity_sums(6, 0)
+        ari_sum(1)
         ari_products(2)
         add_on_gpsimd(2)
-        both_entity_sums(7, 2)
-        arr_sum(6)
+        turn_arr_terms(1, (0, 1))
+        ari_sum(4)
         ari_products(3)
         add_on_gpsimd(3)
+        turn_arr_terms(4, (2, 3))
+        ari_sum(5)
+        arr_products(5, (1,))
+        arr_sum(6)
         ari_products(1)
-        turn_arr_terms(1, (0, 1))
+        ari_sum(6)
         ari_products(4)
         add_turned(1)
-        turn_arr_terms(4, (2, 3))
-        arr_products(5, (1,))
-        arr_sum(7)
-        ari_products(5)
         add_turned(4)
+        ari_products(5)
+        arr_sum(7)
+        ari_sum(7)
         arr_products(6)
-        operands = quantize_h((0, 1, 2, 3), ent_at[5, 0])
+        ari_products(6, (0,))
+        operands = quantize_h((0, 2, 3, 1), with_six)
         add_on_gpsimd(5)
         score(0, HALF, operands, (0, 1, 2, 3))
-        ari_products(6)
+        ari_products(6, (1,))
         arr_products(7)
-        ari_products(7)
+        ari_products(7, (0,))
         score(4, 2 * CHUNK, quantize_h((4, 5), ent_at[6, 0]), (ARR_BANK, ARR_BANK + 1))
         add_on_vector(6)
-        nc.vector.tensor_tensor(h[7][:, 0], flat(with_arr[7])[:, 0], flat(with_ari[7])[:, 0], ADD)
+        ari_products(7, (1,))
         score(6, CHUNK, quantize_h((6,)), (ARI_BANK,))
-        nc.vector.tensor_tensor(h[7][:, 1], flat(with_arr[7])[:, 1], flat(with_ari[7])[:, 1], ADD)
-        score(7, CHUNK, quantize_h((7,)), (ARI_BANK + 1,))
+        add_on_vector(7)
+        score(7, CHUNK, quantize_h((7,)), (ARI_BANK + 1, 0))

@@ -30,7 +30,7 @@ HALF_CHUNKS = HALF // CHUNK
 BANK_BYTES = 2048
 ENT_ROW = 8
 
-TURNED = (1, 4)
+TURNED = (1, 4, 6)
 STRADDLING = 1
 ON_GPSIMD = 4
 ARR_ORDER = (0, 2, 3, STRADDLING, 5, 6, 7)
@@ -38,7 +38,7 @@ ARI_ORDER = (0, 2, 3, 1, 4, 5, 6, 7)
 ARR_BANK, ARI_BANK = 4, 6
 ARI_BANKS = (6, 7, 5)
 
-SCALAR_SHARE = {"er": P, "ei": 3 * P // 8, "rr0": 3 * P // 4, "rr1": 3 * P // 8, "ri0": P // 4, "ri1": P}
+SCALAR_SHARE = {"er": P, "ei": 3 * P // 8, "rr0": 3 * P // 4, "rr1": 3 * P // 8, "ri0": 3 * P // 8, "ri1": P}
 
 SLOT = 4 * T
 HALF_SLOT = SLOT // 2
@@ -254,7 +254,7 @@ def tile_list_ckg_sig_kernel(
             ]
 
         def arr_sum(i):
-            bank = ARI_BANK if i == ON_GPSIMD else ARR_BANK + (ARR_ORDER.index(i) % 2 if i < 5 else i == 7)
+            bank = ARI_BANK if i == ON_GPSIMD else ARR_BANK + (ARR_ORDER.index(i) % 2 if i < 5 else 0)
             arr[i] = project("arr%d" % i, ("rr0", "rr1"), relation(i), bank, i in TURNED)
 
         def ari_sum(i):
@@ -312,22 +312,35 @@ def tile_list_ckg_sig_kernel(
         arr_products(STRADDLING, (1,))
         arr_product_on_gpsimd(ON_GPSIMD, 1)
 
-        h_at = {i: RAW_AT["ri0"] + i * QUARTER for i in range(HALF_CHUNKS)}
-        h_at.update({4: GROUPED_AT["ei"], 5: h_at[1], 6: RAW_AT["rr0"] + HALF_SLOT, 7: RAW_AT["rr0"] + 3 * QUARTER})
-        h = {i: arena.tile([P, 2, WIDE], BF16, name="h%d" % i, offset=at, align_bytes=64)[:] for i, at in h_at.items()}
+        groups = {(0, 1): RAW_AT["ri0"], (2, 3): RAW_AT["ri0"] + HALF_SLOT, (4,): GROUPED_AT["ei"], (5,): RAW_AT["ri0"] + HALF_SLOT,
+                  (6,): RAW_AT["rr0"] + HALF_SLOT, (7,): RAW_AT["rr0"] + HALF_SLOT}
+        held = {
+            group: arena.tile([P, 2, len(group), WIDE], BF16, name="h%d" % group[0], offset=at, align_bytes=64)
+            for group, at in groups.items()
+        }
+        h = {i: held[group][:, :, e, :] for group in groups for e, i in enumerate(group)}
 
-        def quantize_h(chunks, scales_at=None):
-            shape = [P, 2, len(chunks) * CHUNK]
-            first = min(chunks)
-            h_codes = keep.tile(shape, U32, name="codes_h%d" % chunks[0], align_bytes=64)
+        def quantize_h(parts, scales_at=None, joined=False):
+            first = min(parts)[0]
+            shape = [P, 2, sum(map(len, parts)) * CHUNK]
+            h_codes = keep.tile(shape, U32, name="codes_h%d" % first, align_bytes=64)
             if scales_at is None:
-                h_scales = keep.tile(shape, U8, name="scales_h%d" % chunks[0], align_bytes=64)
+                h_scales = keep.tile(shape, U8, name="scales_h%d" % first, align_bytes=64)
             else:
-                h_scales = arena.tile(shape, U8, name="scales_h%d" % chunks[0], offset=scales_at, align_bytes=64)
-            for i in chunks:
-                cols = slice((i - first) * CHUNK, (i - first + 1) * CHUNK)
-                for s in range(2):
-                    nc.vector.quantize_mx(out=h_codes[:, s, cols].bitcast(FP8X4), scales=h_scales[:, s, cols], in_=h[i][:, s])
+                h_scales = arena.tile(shape, U8, name="scales_h%d" % first, offset=scales_at, align_bytes=64)
+            if joined:
+                nc.vector.quantize_mx(
+                    out=h_codes[:].rearrange("p s j -> p (s j)").bitcast(FP8X4), scales=h_scales[:].rearrange("p s j -> p (s j)"),
+                    in_=held[parts[0]][:].rearrange("p s i w -> p (s i w)"),
+                )
+            else:
+                for group in parts:
+                    cols = slice((group[0] - first) * CHUNK, (group[-1] - first + 1) * CHUNK)
+                    for s in range(2):
+                        nc.vector.quantize_mx(
+                            out=h_codes[:, s, cols].bitcast(FP8X4), scales=h_scales[:, s, cols],
+                            in_=held[group][:, s].rearrange("p i w -> p (i w)"),
+                        )
             return [(h_codes[:, s], h_scales[:, s]) for s in range(2)]
 
         def score_pass(y, u, s, operand, start, stop):
@@ -416,20 +429,23 @@ def tile_list_ckg_sig_kernel(
         ari_products(4)
         add_turned(1)
         add_turned(4)
-        ari_products(5)
-        arr_sum(7)
         ari_sum(7)
+        ari_products(5)
         arr_products(6)
+        arr_sum(7)
+        turn_arr_terms(6, (3, ARR_BANK + 1))
         ari_products(6, (0,))
-        operands = quantize_h((0, 2, 3, 1), with_six)
+        operands = quantize_h(((0, 1), (2, 3)), ent_at[5, 0])
         add_on_gpsimd(5)
-        score(0, HALF, operands, (0, 1, 2, 3))
+        score(0, HALF, operands, (0, 1, 2, 0), (0, 1))
         ari_products(6, (1,))
+        add_turned(6)
+        score(0, HALF, operands, (0, 1, 2, 0), (2, 3))
         arr_products(7)
         ari_products(7, (0,))
-        score(4, 2 * CHUNK, quantize_h((4, 5), ent_at[6, 0]), (ARR_BANK, ARR_BANK + 1))
-        add_on_vector(6)
+        score(4, 2 * CHUNK, quantize_h(((4,), (5,)), ent_at[6, 0]), (1, 2))
+        operands = quantize_h(((6,),), joined=True)
         ari_products(7, (1,))
-        score(6, CHUNK, quantize_h((6,)), (ARI_BANK,))
+        score(6, CHUNK, operands, (ARR_BANK,))
         add_on_vector(7)
-        score(7, CHUNK, quantize_h((7,)), (ARI_BANK + 1, 0))
+        score(7, CHUNK, quantize_h(((7,),)), (ARI_BANK, 0))

@@ -25,6 +25,7 @@ GROUP = 16
 CHUNK = 128
 CHUNKS = J // CHUNK
 WIDE = CHUNK * PACK
+PAIR = 2 * CHUNK
 HALF = J // 2
 HALF_CHUNKS = HALF // CHUNK
 BANK_BYTES = 2048
@@ -33,12 +34,14 @@ ENT_ROW = 8
 TURNED = (1, 4, 6)
 STRADDLING = 1
 ON_GPSIMD = 4
-ARR_ORDER = (0, 2, 3, STRADDLING, 5, 6, 7)
-ARI_ORDER = (0, 2, 3, 1, 4, 5, 6, 7)
-ARR_BANK, ARI_BANK = 4, 6
-ARI_BANKS = (6, 7, 5)
+LAST = CHUNKS - 1
 
-SCALAR_SHARE = {"er": P, "ei": 3 * P // 8, "rr0": 3 * P // 4, "rr1": 3 * P // 8, "ri0": 3 * P // 8, "ri1": P}
+ARI_ORDER = (0, 2, 1, 3, 4, 5, 6, 7)
+ARI_BANKS = (6, 7, 5)
+EARLY_ARR_BANK = {0: 4, 2: 5, ON_GPSIMD: 2, STRADDLING: 5}
+LATE_ARR_BANK = 3
+
+SCALAR_SHARE = {"er": P, "ei": 3 * P // 8, "rr0": 3 * P // 4, "rr1": P // 2, "ri0": P // 4, "ri1": P}
 
 SLOT = 4 * T
 HALF_SLOT = SLOT // 2
@@ -199,22 +202,19 @@ def tile_list_ckg_sig_kernel(
                     )
             return acc[:].rearrange("p t n -> p n t")
 
-        ent_at = {(i, s): RAW_AT[("ei", "er")[s]] + i * QUARTER for i in range(3) for s in range(2)}
-        ent_at.update({(4, 0): RAW_AT["rr0"], (4, 1): RAW_AT["rr1"]})
-        ent_at.update({(3, 0): RAW_AT["rr1"] + QUARTER, (3, 1): GROUPED_AT["rr1"]})
         under = RAW_AT["ri1"] - LIP
+        ent_at = {(i, s): RAW_AT[("ei", "er")[s]] + i * QUARTER for i in range(3) for s in range(2)}
+        ent_at.update({(4, 0): RAW_AT["rr1"] + QUARTER, (4, 1): RAW_AT["rr1"]})
+        ent_at.update({(3, 0): GROUPED_AT["rr1"] + QUARTER, (3, 1): GROUPED_AT["rr1"]})
         ent_at.update({(6, 0): under + QUARTER, (5, 0): under + 2 * QUARTER, (5, 1): under + 3 * QUARTER})
-        ent_at[7, 1] = RAW_AT["rr0"] + QUARTER
-        ent_at[6, 1] = GROUPED_AT["ri1"] + LIP
+        ent_at.update({(6, 1): GROUPED_AT["ri1"] + LIP, (7, 1): RAW_AT["rr0"] + QUARTER})
         entity = {
             (i, s): arena.tile([P, CHUNK, PACK], F32, name="ent%d_%d" % (i, s), offset=ent_at[i, s])
             if (i, s) in ent_at else keep.tile([P, CHUNK, PACK], F32, name="ent%d_%d" % (i, s))
             for i in range(CHUNKS) for s in range(2)
         }
 
-        arr_at = {
-            6: ent_at[5, 1] + QUARTER - LIP, 7: ent_at[6, 1],
-        }
+        arr_at = {6: ent_at[5, 1] + QUARTER - LIP, 7: ent_at[6, 1]}
         with_arr = {
             i: arena.tile([P, 2, CHUNK, PACK], F32, name="with_arr%d" % i, offset=arr_at[i])
             if i in arr_at else keep.tile([P, 2, CHUNK, PACK], F32, name="with_arr%d" % i)
@@ -254,11 +254,12 @@ def tile_list_ckg_sig_kernel(
             ]
 
         def arr_sum(i):
-            bank = ARI_BANK if i == ON_GPSIMD else ARR_BANK + (ARR_ORDER.index(i) % 2 if i < 5 else 0)
+            bank = EARLY_ARR_BANK.get(i, LATE_ARR_BANK)
             arr[i] = project("arr%d" % i, ("rr0", "rr1"), relation(i), bank, i in TURNED)
 
         def ari_sum(i):
-            ari[i] = project("ari%d" % i, ("ri0", "ri1"), relation(i), ARI_BANKS[ARI_ORDER.index(i) % 3], i in TURNED)
+            bank = ARI_BANKS[ARI_ORDER.index(i) % len(ARI_BANKS)]
+            ari[i] = project("ari%d" % i, ("ri0", "ri1"), relation(i), bank, i in TURNED)
 
         def arr_products(i, parts=(0, 1)):
             for s in parts:
@@ -271,7 +272,6 @@ def tile_list_ckg_sig_kernel(
             if 1 in parts:
                 nc.vector.tensor_tensor(with_ari[i][:, 1], ari[i], entity[i, 0][:], MULT)
 
-
         quantize_weight("ei")
         gather_entities(1)
         for s in range(2):
@@ -281,39 +281,32 @@ def tile_list_ckg_sig_kernel(
         gather_relations(1)
         part_relations(0)
         quantize_weight("rr0")
-        entity_sum(4, 0, 2)
         quantize_weight("rr1")
-        entity_sum(4, 1, 3)
+        both_entity_sums(4, 2)
         part_relations(1)
         arr_sum(0)
         arr_sum(2)
         arr_sum(ON_GPSIMD)
-        arr_products(0)
         arr_sum(3)
+        arr_products(0)
         both_entity_sums(3, 0)
-
-        def copy_arr(i, at):
-            arr_copy[i] = arena.tile([P, CHUNK, PACK], F32, name="arr_copy%d" % i, offset=at)
-            nc.scalar.copy(arr_copy[i][:], arr[i])
-
-        def arr_product_on_gpsimd(i, s):
-            nc.gpsimd.tensor_tensor(arr_term(i, s), arr_copy[i][:], entity[i, s][:], MULT)
-
-        arr_copy = {}
         arr_products(2)
         arr_sum(STRADDLING)
         quantize_weight("ri0")
-        copy_arr(ON_GPSIMD, RAW_AT["rr1"] + 3 * QUARTER)
-        arr_product_on_gpsimd(ON_GPSIMD, 0)
+        arr_copy = arena.tile([P, CHUNK, PACK], F32, name="arr_copy", offset=RAW_AT["rr1"] + 3 * QUARTER)
+        nc.scalar.copy(arr_copy[:], arr[ON_GPSIMD])
+        nc.gpsimd.tensor_tensor(arr_term(ON_GPSIMD, 0), arr_copy[:], entity[ON_GPSIMD, 0][:], MULT)
         arr_products(3)
         arr_sum(5)
         arr_products(STRADDLING, (0,))
         quantize_weight("ri1")
         arr_products(STRADDLING, (1,))
-        arr_product_on_gpsimd(ON_GPSIMD, 1)
+        nc.gpsimd.tensor_tensor(arr_term(ON_GPSIMD, 1), arr_copy[:], entity[ON_GPSIMD, 1][:], MULT)
 
-        groups = {(0, 1): RAW_AT["ri0"], (2, 3): RAW_AT["ri0"] + HALF_SLOT, (4,): GROUPED_AT["ei"], (5,): RAW_AT["ri0"] + HALF_SLOT,
-                  (6,): RAW_AT["rr0"] + HALF_SLOT, (7,): RAW_AT["rr0"] + HALF_SLOT}
+        groups = {
+            (0, 1): RAW_AT["ri0"], (2,): RAW_AT["ri0"] + HALF_SLOT, (3,): RAW_AT["ri0"], (4,): GROUPED_AT["ei"],
+            (5,): RAW_AT["ri0"], (6,): RAW_AT["rr0"] + HALF_SLOT, (7,): RAW_AT["rr0"] + HALF_SLOT,
+        }
         held = {
             group: arena.tile([P, 2, len(group), WIDE], BF16, name="h%d" % group[0], offset=at, align_bytes=64)
             for group, at in groups.items()
@@ -352,10 +345,9 @@ def tile_list_ckg_sig_kernel(
                 rhs=h_codes.bitcast(FP8X4), rhs_scale=h_scales, start=start, stop=stop,
             )
 
-        def score(first, tokens, operands, banks, parts=None):
+        def score(first, tokens, operands, banks):
             blocks = N // P // len(banks)
-            for b in parts or range(len(banks)):
-                bank = banks[b]
+            for b, bank in enumerate(banks):
                 y = psum.tile([P, blocks, tokens], F32, name="y%d_%d" % (first, b), offset=bank * BANK_BYTES)
                 for s in range(2):
                     for u in range(blocks):
@@ -366,11 +358,6 @@ def tile_list_ckg_sig_kernel(
                 cols = slice(first * CHUNK, first * CHUNK + tokens)
                 nc.sync.dma_start(out[rows, cols].rearrange("(u p) j -> p u j", p=P), result[:])
 
-        def new_totals(i, banks):
-            return [
-                psum.tile([P, PACK, CHUNK], F32, name="total%d_%d" % (i, s), offset=banks[s] * BANK_BYTES) for s in range(2)
-            ]
-
         def turn(total, source, t, start, stop):
             columns = source.rearrange("p n t -> p (n t)")[:, t * P : (t + 1) * P]
             nc.tensor.matmul(total[:, t, :], columns, identity[:], start=start, stop=stop, is_transpose=True)
@@ -378,7 +365,9 @@ def tile_list_ckg_sig_kernel(
         totals = {}
 
         def turn_arr_terms(i, banks):
-            totals[i] = new_totals(i, banks)
+            totals[i] = [
+                psum.tile([P, PACK, CHUNK], F32, name="total%d_%d" % (i, s), offset=banks[s] * BANK_BYTES) for s in range(2)
+            ]
             for s in range(2):
                 for t in range(PACK):
                     turn(totals[i][s], arr_term(i, s), t, t == 0, False)
@@ -396,56 +385,53 @@ def tile_list_ckg_sig_kernel(
         def add_on_gpsimd(i):
             nc.gpsimd.tensor_tensor(h[i], flat(with_arr[i]), flat(with_ari[i]), ADD)
 
-        with_six = ent_at[5, 0]
-
-        def add_on_vector(i, parts=(0, 1)):
-            for s in parts:
-                nc.vector.tensor_tensor(h[i][:, s], flat(with_arr[i])[:, s], flat(with_ari[i])[:, s], ADD)
-
         ari_sum(0)
         ari_sum(2)
-        ari_sum(3)
+        ari_sum(1)
         entity_sum(5, 0, 2)
-        copy_arr(5, under)
-        arr_product_on_gpsimd(5, 0)
-        entity_sum(5, 1, 3)
+        arr_products(5, (0,))
+        entity_sum(5, 1, 4)
         both_entity_sums(6, 0)
-        both_entity_sums(7, 2)
+        both_entity_sums(7, 0)
         ari_products(0)
         add_on_gpsimd(0)
-        ari_sum(1)
+        ari_sum(3)
         ari_products(2)
         add_on_gpsimd(2)
-        turn_arr_terms(1, (0, 1))
+        turn_arr_terms(1, (4, 2))
         ari_sum(4)
-        ari_products(3)
-        add_on_gpsimd(3)
-        turn_arr_terms(4, (2, 3))
+        ari_products(1)
+        add_turned(1)
         ari_sum(5)
+        ari_products(3)
         arr_products(5, (1,))
         arr_sum(6)
-        ari_products(1)
         ari_sum(6)
+        turn_arr_terms(4, (0, 1))
         ari_products(4)
-        add_turned(1)
         add_turned(4)
+
+        first_pair = quantize_h(((0, 1),), ent_at[4, 1], joined=True)
+        add_on_gpsimd(3)
         ari_sum(7)
+        score(0, PAIR, first_pair, (4, 2))
         ari_products(5)
         arr_products(6)
         arr_sum(7)
-        turn_arr_terms(6, (3, ARR_BANK + 1))
+        turn_arr_terms(6, (0, 5))
         ari_products(6, (0,))
-        operands = quantize_h(((0, 1), (2, 3)), ent_at[5, 0])
+
+        single = quantize_h(((4,),), ent_at[5, 0], joined=True)
+        second_pair = quantize_h(((2,), (3,)), ent_at[5, 0] + 2 * PAIR)
         add_on_gpsimd(5)
-        score(0, HALF, operands, (0, 1, 2, 0), (0, 1))
         ari_products(6, (1,))
         add_turned(6)
-        score(0, HALF, operands, (0, 1, 2, 0), (2, 3))
-        arr_products(7)
-        ari_products(7, (0,))
-        score(4, 2 * CHUNK, quantize_h(((4,), (5,)), ent_at[6, 0]), (1, 2))
-        operands = quantize_h(((6,),), joined=True)
-        ari_products(7, (1,))
-        score(6, CHUNK, operands, (ARR_BANK,))
-        add_on_vector(7)
-        score(7, CHUNK, quantize_h(((7,),)), (ARI_BANK, 0))
+        score(2, PAIR, second_pair, (4, 2))
+        score(4, CHUNK, single, (1,))
+        arr_products(LAST)
+        ari_products(LAST)
+
+        score(5, PAIR, quantize_h(((6,), (5,)), ent_at[LAST, 1]), (4, 3))
+        for s in range(2):
+            nc.vector.tensor_tensor(h[LAST][:, s], flat(with_arr[LAST])[:, s], flat(with_ari[LAST])[:, s], ADD)
+        score(LAST, CHUNK, quantize_h(((LAST,),)), (6, 1))

@@ -32,16 +32,18 @@ BANK_BYTES = 2048
 ENT_ROW = 8
 
 TURNED = (1, 4, 6)
-STRADDLING = 1
+WAITING = 1
 ON_GPSIMD = 4
 LAST = CHUNKS - 1
+EARLY_CHUNKS = 3
 
 ARI_ORDER = (0, 2, 1, 3, 4, 5, 6, 7)
 ARI_BANKS = (6, 7, 5)
-EARLY_ARR_BANK = {0: 4, 2: 5, ON_GPSIMD: 2, STRADDLING: 5}
+EARLY_ARR_BANK = {0: 4, 2: 5, 3: 6, ON_GPSIMD: 2, WAITING: 5}
 LATE_ARR_BANK = 3
 
-SCALAR_SHARE = {"er": P, "ei": 3 * P // 8, "rr0": 3 * P // 4, "rr1": P // 2, "ri0": P // 4, "ri1": P}
+SCALAR_SHARE = {"er": P, "ei": 3 * P // 8, "rr0": 3 * P // 4, "rr1": P // 2, "ri0": P // 4, "ri1": 3 * P // 4}
+SHARED_WITH_GPSIMD = ("ri0", "ri1")
 
 SLOT = 4 * T
 HALF_SLOT = SLOT // 2
@@ -132,18 +134,28 @@ def tile_list_ckg_sig_kernel(
         w_codes = {name: keep.tile([P, R], U32, name="codes_" + name, align_bytes=64) for name in passes}
         w_scales = {name: keep.tile([P, R], U8, name="scales_" + name, align_bytes=64) for name in passes}
 
-        def quantize_weight(name):
-            grouped = arena.tile([P, PACK * R], BF16, name="grouped_" + name, offset=GROUPED_AT[name], align_bytes=64)
-            dst = grouped[:].rearrange("p (t m e) -> p m e t", t=PACK, e=PACK)
+        grouped = {}
+
+        def interleave(name):
+            grouped[name] = arena.tile(
+                [P, PACK * R], BF16, name="grouped_" + name, offset=GROUPED_AT[name], align_bytes=64
+            )
+            dst = grouped[name][:].rearrange("p (t m e) -> p m e t", t=PACK, e=PACK)
             src = raw[name][:].rearrange("p e (m t) -> p m e t", t=PACK)
             share = SCALAR_SHARE[name]
             nc.scalar.copy(dst[:, :share], src[:, :share])
-            if name == "ri0":
+            if name in SHARED_WITH_GPSIMD:
                 dst, src = (side[:, share:].rearrange("p m e t -> p m t e") for side in (dst, src))
                 nc.gpsimd.tensor_scalar(dst, src, 1.0, 0.0, MULT, ADD)
             elif share < P:
                 nc.vector.tensor_copy(dst[:, share:], src[:, share:])
-            nc.vector.quantize_mx(out=w_codes[name][:].bitcast(FP8X4), scales=w_scales[name][:], in_=grouped[:])
+
+        def quantize_grouped(name):
+            nc.vector.quantize_mx(out=w_codes[name][:].bitcast(FP8X4), scales=w_scales[name][:], in_=grouped[name][:])
+
+        def quantize_weight(name):
+            interleave(name)
+            quantize_grouped(name)
 
         nc.sync.dma_start(ent_list[:], offs)
         nc.sync.dma_start(rel_list[:], offs2)
@@ -203,7 +215,7 @@ def tile_list_ckg_sig_kernel(
             return acc[:].rearrange("p t n -> p n t")
 
         under = RAW_AT["ri1"] - LIP
-        ent_at = {(i, s): RAW_AT[("ei", "er")[s]] + i * QUARTER for i in range(3) for s in range(2)}
+        ent_at = {(i, s): RAW_AT[("ei", "er")[s]] + i * QUARTER for i in range(EARLY_CHUNKS) for s in range(2)}
         ent_at.update({(4, 0): RAW_AT["rr1"] + QUARTER, (4, 1): RAW_AT["rr1"]})
         ent_at.update({(3, 0): GROUPED_AT["rr1"] + QUARTER, (3, 1): GROUPED_AT["rr1"]})
         ent_at.update({(6, 0): under + QUARTER, (5, 0): under + 2 * QUARTER, (5, 1): under + 3 * QUARTER})
@@ -218,16 +230,16 @@ def tile_list_ckg_sig_kernel(
         with_arr = {
             i: arena.tile([P, 2, CHUNK, PACK], F32, name="with_arr%d" % i, offset=arr_at[i])
             if i in arr_at else keep.tile([P, 2, CHUNK, PACK], F32, name="with_arr%d" % i)
-            for i in range(CHUNKS) if i not in (STRADDLING, ON_GPSIMD)
+            for i in range(CHUNKS) if i not in (WAITING, ON_GPSIMD)
         }
         apart_at = {
-            (STRADDLING, 1): under + SLOT,
-            (ON_GPSIMD, 0): GROUPED_AT["ri0"], (ON_GPSIMD, 1): GROUPED_AT["ri1"] + LIP - QUARTER,
+            (WAITING, 1): under + SLOT,
+            (ON_GPSIMD, 0): GROUPED_AT["ri1"] + HALF_SLOT - LIP, (ON_GPSIMD, 1): GROUPED_AT["ri1"] + LIP - QUARTER,
         }
         apart = {
             (i, s): arena.tile([P, CHUNK, PACK], F32, name="apart%d_%d" % (i, s), offset=apart_at[i, s])
             if (i, s) in apart_at else keep.tile([P, CHUNK, PACK], F32, name="apart%d_%d" % (i, s))
-            for i in (STRADDLING, ON_GPSIMD) for s in range(2)
+            for i in (WAITING, ON_GPSIMD) for s in range(2)
         }
         with_ari = {}
         arr, ari = {}, {}
@@ -275,8 +287,8 @@ def tile_list_ckg_sig_kernel(
         quantize_weight("ei")
         gather_entities(1)
         for s in range(2):
-            for i in range(3):
-                entity_sum(i, s, (3 * s + i) % 4)
+            for i in range(EARLY_CHUNKS):
+                entity_sum(i, s, (EARLY_CHUNKS * s + i) % 4)
         gather_relations(0)
         gather_relations(1)
         part_relations(0)
@@ -286,22 +298,23 @@ def tile_list_ckg_sig_kernel(
         part_relations(1)
         arr_sum(0)
         arr_sum(2)
-        arr_sum(ON_GPSIMD)
         arr_sum(3)
+        arr_sum(ON_GPSIMD)
         arr_products(0)
         both_entity_sums(3, 0)
         arr_products(2)
-        arr_sum(STRADDLING)
-        quantize_weight("ri0")
+        arr_sum(WAITING)
+        interleave("ri0")
         arr_copy = arena.tile([P, CHUNK, PACK], F32, name="arr_copy", offset=RAW_AT["rr1"] + 3 * QUARTER)
         nc.scalar.copy(arr_copy[:], arr[ON_GPSIMD])
-        nc.gpsimd.tensor_tensor(arr_term(ON_GPSIMD, 0), arr_copy[:], entity[ON_GPSIMD, 0][:], MULT)
+        interleave("ri1")
         arr_products(3)
         arr_sum(5)
-        arr_products(STRADDLING, (0,))
-        quantize_weight("ri1")
-        arr_products(STRADDLING, (1,))
-        nc.gpsimd.tensor_tensor(arr_term(ON_GPSIMD, 1), arr_copy[:], entity[ON_GPSIMD, 1][:], MULT)
+        quantize_grouped("ri0")
+        quantize_grouped("ri1")
+        arr_products(WAITING)
+        for s in range(2):
+            nc.gpsimd.tensor_tensor(arr_term(ON_GPSIMD, s), arr_copy[:], entity[ON_GPSIMD, s][:], MULT)
 
         groups = {
             (0, 1): RAW_AT["ri0"], (2,): RAW_AT["ri0"] + HALF_SLOT, (3,): RAW_AT["ri0"], (4,): GROUPED_AT["ei"],
@@ -323,7 +336,8 @@ def tile_list_ckg_sig_kernel(
                 h_scales = arena.tile(shape, U8, name="scales_h%d" % first, offset=scales_at, align_bytes=64)
             if joined:
                 nc.vector.quantize_mx(
-                    out=h_codes[:].rearrange("p s j -> p (s j)").bitcast(FP8X4), scales=h_scales[:].rearrange("p s j -> p (s j)"),
+                    out=h_codes[:].rearrange("p s j -> p (s j)").bitcast(FP8X4),
+                    scales=h_scales[:].rearrange("p s j -> p (s j)"),
                     in_=held[parts[0]][:].rearrange("p s i w -> p (s i w)"),
                 )
             else:

@@ -29,6 +29,7 @@ PAIR = 2 * CHUNK
 HALF = J // 2
 HALF_CHUNKS = HALF // CHUNK
 BANK_BYTES = 2048
+REL_ROW = 96
 ENT_ROW = 8
 
 TURNED = (1, 4, 6)
@@ -49,14 +50,13 @@ SLOT = 4 * T
 HALF_SLOT = SLOT // 2
 QUARTER = SLOT // 4
 LIP = 64
-MOVED_AT = SLOT
-REL_WORDS_AT = MOVED_AT + J
-ENT_WORDS_AT = REL_WORDS_AT + SLOT
-WINDOW_AT = REL_WORDS_AT + 6 * SLOT
-RAW_AT = {
-    "er": 0, "ei": ENT_WORDS_AT + SLOT, "rr0": ENT_WORDS_AT + 2 * SLOT, "rr1": ENT_WORDS_AT + 3 * SLOT,
-    "ri0": WINDOW_AT - SLOT, "ri1": WINDOW_AT + SLOT,
-}
+ENT_WORDS_AT = SLOT
+REL_SCALES_AT = 3 * SLOT
+CAND_SCALES_AT = REL_SCALES_AT + 2 * J
+WINDOW_AT = CAND_SCALES_AT + 2 * N
+CAND_AT = WINDOW_AT + T
+REL_WORDS_AT = 4 * SLOT
+RAW_AT = {"er": 0, "ei": 2 * SLOT, "rr0": 5 * SLOT, "rr1": 6 * SLOT, "ri0": 7 * SLOT, "ri1": 8 * SLOT}
 GROUPED_AT = {
     "er": 10 * SLOT + HALF_SLOT, "rr0": 10 * SLOT + HALF_SLOT, "ri1": 11 * SLOT, "ei": 12 * SLOT,
     "rr1": 12 * SLOT + HALF_SLOT, "ri0": 13 * SLOT,
@@ -77,16 +77,15 @@ def tile_list_ckg_sig_kernel(
         ent_list = keep.tile([P, J // GROUP], U16, name="ent_list")
         rel_list = keep.tile([P, J // GROUP], U16, name="rel_list")
 
+        rel_held = arena.tile([P, (5 * SLOT + LIP) // 4], I32, name="rel_held", offset=WINDOW_AT, align_bytes=64)
+        nc.vector.memset(rel_held[:REL_ROW, : T // 4], 0)
         ent_window = keep.tile([P, T // 4], I32, name="ent_window", align_bytes=64)
         nc.vector.memset(ent_window[:], 0)
-        moved_zeros = arena.tile([P, (LIP + J) // 4], I32, name="moved_zeros", offset=MOVED_AT - LIP, align_bytes=64)
-        nc.vector.memset(moved_zeros[:, LIP // 4 :], 0)
-        rel_held = arena.tile([P, (SLOT + 2 * LIP) // 4], I32, name="rel_held", offset=WINDOW_AT - LIP, align_bytes=64)
-        window_words = slice(LIP // 4, (LIP + T) // 4)
-        nc.vector.memset(rel_held[:, LIP // 4 : (LIP + T + 2 * N) // 4], 0)
         identity = keep.tile([P, P], F32, name="identity")
-        ones = arena.tile([P, 5 * T], F32, name="ones", offset=REL_WORDS_AT, align_bytes=64)
-        nc.vector.memset(ones[:, :P], 1.0)
+        zeros = arena.tile([P, (WINDOW_AT - ENT_WORDS_AT) // 4], I32, name="zeros", offset=ENT_WORDS_AT, align_bytes=64)
+        nc.vector.memset(zeros[:, (REL_SCALES_AT - ENT_WORDS_AT) // 4 :], 0)
+        ones = keep.tile([P, P], F32, name="ones")
+        nc.vector.memset(ones[:], 1.0)
         nc.gpsimd.affine_select(
             out=identity[:], in_=ones[:, :P], pattern=[[-1, P]], compare_op=mybir.AluOpType.is_equal,
             fill=0.0, base=0, channel_multiplier=1,
@@ -157,34 +156,36 @@ def tile_list_ckg_sig_kernel(
             interleave(name)
             quantize_grouped(name)
 
-        nc.sync.dma_start(ent_list[:], offs)
         nc.sync.dma_start(rel_list[:], offs2)
+        nc.sync.dma_start(rel_held[REL_ROW:, : T // 4], tab2_scales.rearrange("a q t -> (a q) t").bitcast(I32))
+        load_weight("er")
+        nc.sync.dma_start(ent_list[:], offs)
         for q in range(QUADS):
             rows = slice(32 * q + ENT_ROW, 32 * q + ENT_ROW + 4)
             nc.sync.dma_start(ent_window[rows, :], tab_scales[0, 4 * q : 4 * q + 4, :].bitcast(I32))
-        load_weight("er")
-        for q in range(QUADS):
-            nc.sync.dma_start(rel_held[32 * q : 32 * q + 4, window_words], tab2_scales[0, 4 * q : 4 * q + 4, :].bitcast(I32))
-        nc.sync.dma_start(rel_held[4:P:8, window_words], tab2_scales[1].bitcast(I32))
         nc.sync.dma_start(ent_words[:], tab_words[0].rearrange("p t i -> p (t i)").bitcast(I32))
         load_weight("ei")
-        nc.sync.dma_start(rel_words[:], tab2_words[0].rearrange("p t i -> p (t i)").bitcast(I32))
-        load_weight("rr0")
-        load_weight("rr1")
+        rel_picked = keep.tile([P, J // 4], I32, name="rel_picked", align_bytes=64)
+        nc.vector.tensor_copy(rel_picked[:].bitcast(U8), rel_held[:, : T // 4].bitcast(U8).indirect(rel_list[:]))
         nc.vector.tensor_copy(ent_scales[:], ent_window[:].bitcast(U8).indirect(ent_list[:]))
-        rel_scales = [
-            keep.tile([P, J // 4], I32, name="rel_scales0", align_bytes=64),
-            arena.tile([P, J // 4], I32, name="rel_scales1", offset=MOVED_AT, align_bytes=64),
-        ]
-        nc.vector.tensor_copy(rel_scales[0][:].bitcast(U8), rel_held[:, window_words].bitcast(U8).indirect(rel_list[:]))
+        rel_planes = arena.tile([P, 2, J // 4], I32, name="rel_planes", offset=REL_SCALES_AT, align_bytes=64)
+        rel_scales = [rel_planes[:, a, :] for a in range(2)]
+
+        def move_scales(a):
+            for q in range(QUADS):
+                first = REL_ROW + 16 * a + 4 * q
+                nc.sync.dma_start(rel_planes[32 * q : 32 * q + 4, a, :], rel_picked[first : first + 4, :])
+
+        move_scales(0)
+        nc.sync.dma_start(rel_words[:], tab2_words[0].rearrange("p t i -> p (t i)").bitcast(I32))
+        move_scales(1)
+        for name in ("rr0", "rr1", "ri0", "ri1"):
+            load_weight(name)
         quantize_weight("er")
         gather_entities(0)
-        for c in range(4):
-            nc.sync.dma_start(rel_scales[1][c:P:32, :], rel_scales[0][8 * c + 4 : P : 32, :])
-        load_weight("ri0")
-        load_weight("ri1")
-        cand_scales = arena.tile([P, 2, N // 4], I32, name="cand_scales", offset=WINDOW_AT + T, align_bytes=64)
-        cand = arena.tile([P, 2, N // 2], I32, name="cand", offset=WINDOW_AT + T + 2 * N, align_bytes=64)
+        cand_held = arena.tile([P, (2 * N + LIP) // 4], I32, name="cand_held", offset=CAND_SCALES_AT, align_bytes=64)
+        cand_scales = cand_held[:, : 2 * N // 4].rearrange("p (s n) -> p s n", s=2)
+        cand = arena.tile([P, 2, N // 2], I32, name="cand", offset=CAND_AT, align_bytes=64)
         for s, (words, scales) in enumerate(((nr_words, nr_scales), (ni_words, ni_scales))):
             nc.sync.dma_start(cand[:, s, :], words[0].bitcast(I32))
             for q in range(QUADS):
@@ -261,7 +262,7 @@ def tile_list_ckg_sig_kernel(
             cols = slice(i * CHUNK, (i + 1) * CHUNK)
             within = slice(i % HALF_CHUNKS * 2 * CHUNK, (i % HALF_CHUNKS + 1) * 2 * CHUNK)
             return [
-                (rel_codes[i // HALF_CHUNKS][:, a, within].bitcast(FP4X4), rel_scales[a][:].bitcast(U8)[:, cols])
+                (rel_codes[i // HALF_CHUNKS][:, a, within].bitcast(FP4X4), rel_scales[a].bitcast(U8)[:, cols])
                 for a in range(2)
             ]
 

from contextlib import ExitStack

import concourse.mybir as mybir

K, L, R, N, T, J = 512, 1024, 512, 512, 2048, 1024
FLOPS = 2 * J * (2 * K * R + 2 * L * R + 2 * R * N)

F32 = mybir.dt.float32
BF16 = mybir.dt.bfloat16
I32 = mybir.dt.int32
U32 = mybir.dt.uint32
U16 = mybir.dt.uint16
U8 = mybir.dt.uint8
FP8X4 = mybir.dt.float8_e4m3fn_x4
FP4X4 = mybir.dt.float4_e2m1fn_x4
MULT = mybir.AluOpType.mult
ADD = mybir.AluOpType.add
SIGMOID = mybir.ActivationFunctionType.Sigmoid

P = 128
PACK = 4
K_PASS = P * PACK
QUADS = 4
GROUP = 16
CHUNK = 128
CHUNKS = J // CHUNK
WIDE = CHUNK * PACK
PAIR = 2 * CHUNK
HALF = J // 2
HALF_CHUNKS = HALF // CHUNK
BANK_BYTES = 2048
REL_ROW = 96
ENT_ROW = 8

TURNED = (1, 4, 6)
WAITING = 1
ON_GPSIMD = 4
LAST = CHUNKS - 1
EARLY_CHUNKS = 3

ARI_ORDER = (0, 2, 1, 3, 4, 5, 6, 7)
ARI_BANKS = (6, 7, 5)
EARLY_ARR_BANK = {0: 4, 2: 5, 3: 6, ON_GPSIMD: 2, WAITING: 5}
LATE_ARR_BANK = 3

SCALAR_SHARE = {"er": P, "ei": 3 * P // 8, "rr0": 3 * P // 4, "rr1": P // 2, "ri0": P // 4, "ri1": 3 * P // 4}
SHARED_WITH_GPSIMD = ("ri0", "ri1")

SLOT = 4 * T
HALF_SLOT = SLOT // 2
QUARTER = SLOT // 4
LIP = 64
ENT_WORDS_AT = SLOT
REL_SCALES_AT = 3 * SLOT
CAND_SCALES_AT = REL_SCALES_AT + 2 * J
WINDOW_AT = CAND_SCALES_AT + 2 * N
CAND_AT = WINDOW_AT + T
REL_WORDS_AT = 4 * SLOT
RAW_AT = {"er": 0, "ei": 2 * SLOT, "rr0": 5 * SLOT, "rr1": 6 * SLOT, "ri0": 7 * SLOT, "ri1": 8 * SLOT}
GROUPED_AT = {
    "er": 10 * SLOT + HALF_SLOT, "rr0": 10 * SLOT + HALF_SLOT, "ri1": 11 * SLOT, "ei": 12 * SLOT,
    "rr1": 12 * SLOT + HALF_SLOT, "ri0": 13 * SLOT,
}


def tile_list_ckg_sig_kernel(
    tc, tab_words, tab_scales, tab2_words, tab2_scales, wer, wei, wrr, wri,
    nr_words, nr_scales, ni_words, ni_scales, offs, offs2, out
):
    nc = tc.nc
    with ExitStack() as ctx:
        keep = ctx.enter_context(tc.tile_pool(name="keep", bufs=1))
        arena = ctx.enter_context(tc.tile_pool(name="arena", bufs=1))
        ring = ctx.enter_context(tc.tile_pool(name="ring", bufs=1))
        psum = ctx.enter_context(tc.psum_pool(name="psum", bufs=1))

        ent_list = keep.tile([P, J // GROUP], U16, name="ent_list")
        rel_list = keep.tile([P, J // GROUP], U16, name="rel_list")

        rel_held = arena.tile([P, (5 * SLOT + LIP) // 4], I32, name="rel_held", offset=WINDOW_AT, align_bytes=64)
        nc.vector.memset(rel_held[:REL_ROW, : T // 4], 0)
        ent_window = keep.tile([P, T // 4], I32, name="ent_window", align_bytes=64)
        nc.vector.memset(ent_window[:], 0)
        identity = keep.tile([P, P], F32, name="identity")
        zeros = arena.tile([P, (WINDOW_AT - ENT_WORDS_AT) // 4], I32, name="zeros", offset=ENT_WORDS_AT, align_bytes=64)
        nc.vector.memset(zeros[:, (REL_SCALES_AT - ENT_WORDS_AT) // 4 :], 0)
        ones = keep.tile([P, P], F32, name="ones")
        nc.vector.memset(ones[:], 1.0)
        nc.gpsimd.affine_select(
            out=identity[:], in_=ones[:, :P], pattern=[[-1, P]], compare_op=mybir.AluOpType.is_equal,
            fill=0.0, base=0, channel_multiplier=1,
        )

        ent_words = arena.tile([P, T], I32, name="ent_words", offset=ENT_WORDS_AT, align_bytes=64)
        rel_words = arena.tile([P, T], I32, name="rel_words", offset=REL_WORDS_AT, align_bytes=64)
        passes = {
            "er": wer, "ei": wei,
            "rr0": wrr[:K_PASS, :], "rr1": wrr[K_PASS:, :], "ri0": wri[:K_PASS, :], "ri1": wri[K_PASS:, :],
        }
        raw = {}

        def load_weight(name):
            raw[name] = arena.tile([P, PACK, R], F32, name="raw_" + name, offset=RAW_AT[name], align_bytes=64)
            nc.sync.dma_start(raw[name][:], passes[name].rearrange("(p e) r -> p e r", e=PACK))

        ent_codes = [
            keep.tile([P, HALF], U32, name="ent_codes0", align_bytes=64),
            arena.tile([P, HALF], U32, name="ent_codes1", offset=RAW_AT["ei"] + 3 * QUARTER, align_bytes=64),
        ]
        rel_pairs = [
            keep.tile([P, HALF], U32, name="rel_pairs0", align_bytes=64),
            arena.tile([P, HALF], U32, name="rel_pairs1", offset=GROUPED_AT["ri0"], align_bytes=64),
        ]
        rel_codes = [
            keep.tile([P, 2, 2 * HALF], U8, name="rel_codes0", align_bytes=64),
            arena.tile([P, 2, 2 * HALF], U8, name="rel_codes1", offset=RAW_AT["rr1"] + HALF_SLOT, align_bytes=64),
        ]

        def gather_entities(e):
            entries = ent_list[:, e * HALF // GROUP : (e + 1) * HALF // GROUP]
            nc.vector.tensor_copy(ent_codes[e][:], ent_words[:].bitcast(U32).indirect(entries))

        def gather_relations(e):
            entries = rel_list[:, e * HALF // GROUP : (e + 1) * HALF // GROUP]
            nc.vector.tensor_copy(rel_pairs[e][:], rel_words[:].bitcast(U32).indirect(entries))

        def part_relations(e):
            nc.vector.tensor_copy(
                rel_codes[e][:].bitcast(U16), rel_pairs[e][:].bitcast(U16).rearrange("p (j a) -> p a j", a=2)
            )

        ent_scales = keep.tile([P, J], U8, name="ent_scales", align_bytes=64)
        w_codes = {name: keep.tile([P, R], U32, name="codes_" + name, align_bytes=64) for name in passes}
        w_scales = {name: keep.tile([P, R], U8, name="scales_" + name, align_bytes=64) for name in passes}

        grouped = {}

        def interleave(name):
            grouped[name] = arena.tile(
                [P, PACK * R], BF16, name="grouped_" + name, offset=GROUPED_AT[name], align_bytes=64
            )
            dst = grouped[name][:].rearrange("p (t m e) -> p m e t", t=PACK, e=PACK)
            src = raw[name][:].rearrange("p e (m t) -> p m e t", t=PACK)
            share = SCALAR_SHARE[name]
            nc.scalar.copy(dst[:, :share], src[:, :share])
            if name in SHARED_WITH_GPSIMD:
                dst, src = (side[:, share:].rearrange("p m e t -> p m t e") for side in (dst, src))
                nc.gpsimd.tensor_scalar(dst, src, 1.0, 0.0, MULT, ADD)
            elif share < P:
                nc.vector.tensor_copy(dst[:, share:], src[:, share:])

        def quantize_grouped(name):
            nc.vector.quantize_mx(out=w_codes[name][:].bitcast(FP8X4), scales=w_scales[name][:], in_=grouped[name][:])

        def quantize_weight(name):
            interleave(name)
            quantize_grouped(name)

        nc.sync.dma_start(rel_list[:], offs2)
        nc.sync.dma_start(rel_held[REL_ROW:, : T // 4], tab2_scales.rearrange("a q t -> (a q) t").bitcast(I32))
        load_weight("er")
        nc.sync.dma_start(ent_list[:], offs)
        for q in range(QUADS):
            rows = slice(32 * q + ENT_ROW, 32 * q + ENT_ROW + 4)
            nc.sync.dma_start(ent_window[rows, :], tab_scales[0, 4 * q : 4 * q + 4, :].bitcast(I32))
        nc.sync.dma_start(ent_words[:], tab_words[0].rearrange("p t i -> p (t i)").bitcast(I32))
        load_weight("ei")
        rel_picked = keep.tile([P, J // 4], I32, name="rel_picked", align_bytes=64)
        nc.vector.tensor_copy(rel_picked[:].bitcast(U8), rel_held[:, : T // 4].bitcast(U8).indirect(rel_list[:]))
        nc.vector.tensor_copy(ent_scales[:], ent_window[:].bitcast(U8).indirect(ent_list[:]))
        rel_planes = arena.tile([P, 2, J // 4], I32, name="rel_planes", offset=REL_SCALES_AT, align_bytes=64)
        rel_scales = [rel_planes[:, a, :] for a in range(2)]

        def move_scales(a):
            for q in range(QUADS):
                first = REL_ROW + 16 * a + 4 * q
                nc.sync.dma_start(rel_planes[32 * q : 32 * q + 4, a, :], rel_picked[first : first + 4, :])

        move_scales(0)
        nc.sync.dma_start(rel_words[:], tab2_words[0].rearrange("p t i -> p (t i)").bitcast(I32))
        move_scales(1)
        for name in ("rr0", "rr1", "ri0", "ri1"):
            load_weight(name)
        quantize_weight("er")
        gather_entities(0)
        cand_held = arena.tile([P, (2 * N + LIP) // 4], I32, name="cand_held", offset=CAND_SCALES_AT, align_bytes=64)
        cand_scales = cand_held[:, : 2 * N // 4].rearrange("p (s n) -> p s n", s=2)
        cand = arena.tile([P, 2, N // 2], I32, name="cand", offset=CAND_AT, align_bytes=64)
        for s, (words, scales) in enumerate(((nr_words, nr_scales), (ni_words, ni_scales))):
            nc.sync.dma_start(cand[:, s, :], words[0].bitcast(I32))
            for q in range(QUADS):
                nc.sync.dma_start(cand_scales[32 * q : 32 * q + 4, s, :], scales[0, 4 * q : 4 * q + 4, :].bitcast(I32))

        def project(tag, names, table, bank, turned):
            last = len(names) - 1
            if turned:
                wide = psum.tile([P, R], F32, name=tag, offset=bank * BANK_BYTES)
                for g, name in enumerate(names):
                    table_codes, table_scales = table[g]
                    nc.tensor.matmul_mx(
                        out=wide[:], lhsT=table_codes, lhsT_scale=table_scales,
                        rhs=w_codes[name][:].bitcast(FP8X4), rhs_scale=w_scales[name][:],
                        start=(g == 0), stop=(g == last),
                    )
                return wide[:].rearrange("p (n t) -> p n t", t=PACK)
            acc = psum.tile([P, PACK, CHUNK], F32, name=tag, offset=bank * BANK_BYTES)
            for g, name in enumerate(names):
                table_codes, table_scales = table[g]
                for t in range(PACK):
                    m = slice(t * P, (t + 1) * P)
                    nc.tensor.matmul_mx(
                        out=acc[:, t, :], lhsT=w_codes[name][:, m].bitcast(FP8X4), lhsT_scale=w_scales[name][:, m],
                        rhs=table_codes, rhs_scale=table_scales,
                        start=(g == 0 and t == 0), stop=(g == last and t == PACK - 1),
                    )
            return acc[:].rearrange("p t n -> p n t")

        under = RAW_AT["ri1"] - LIP
        ent_at = {(i, s): RAW_AT[("ei", "er")[s]] + i * QUARTER for i in range(EARLY_CHUNKS) for s in range(2)}
        ent_at.update({(4, 0): RAW_AT["rr1"] + QUARTER, (4, 1): RAW_AT["rr1"]})
        ent_at.update({(3, 0): GROUPED_AT["rr1"] + QUARTER, (3, 1): GROUPED_AT["rr1"]})
        ent_at.update({(6, 0): under + QUARTER, (5, 0): under + 2 * QUARTER, (5, 1): under + 3 * QUARTER})
        ent_at.update({(6, 1): GROUPED_AT["ri1"] + LIP, (7, 1): RAW_AT["rr0"] + QUARTER})
        entity = {
            (i, s): arena.tile([P, CHUNK, PACK], F32, name="ent%d_%d" % (i, s), offset=ent_at[i, s])
            if (i, s) in ent_at else keep.tile([P, CHUNK, PACK], F32, name="ent%d_%d" % (i, s))
            for i in range(CHUNKS) for s in range(2)
        }

        arr_at = {6: ent_at[5, 1] + QUARTER - LIP, 7: ent_at[6, 1]}
        with_arr = {
            i: arena.tile([P, 2, CHUNK, PACK], F32, name="with_arr%d" % i, offset=arr_at[i])
            if i in arr_at else keep.tile([P, 2, CHUNK, PACK], F32, name="with_arr%d" % i)
            for i in range(CHUNKS) if i not in (WAITING, ON_GPSIMD)
        }
        apart_at = {
            (WAITING, 1): under + SLOT,
            (ON_GPSIMD, 0): GROUPED_AT["ri1"] + HALF_SLOT - LIP, (ON_GPSIMD, 1): GROUPED_AT["ri1"] + LIP - QUARTER,
        }
        apart = {
            (i, s): arena.tile([P, CHUNK, PACK], F32, name="apart%d_%d" % (i, s), offset=apart_at[i, s])
            if (i, s) in apart_at else keep.tile([P, CHUNK, PACK], F32, name="apart%d_%d" % (i, s))
            for i in (WAITING, ON_GPSIMD) for s in range(2)
        }
        with_ari = {}
        arr, ari = {}, {}

        def arr_term(i, s):
            return apart[i, s][:] if (i, s) in apart else with_arr[i][:, s]

        def entity_sum(i, s, bank):
            cols = slice(i * CHUNK, (i + 1) * CHUNK)
            within = slice(i % HALF_CHUNKS * CHUNK, (i % HALF_CHUNKS + 1) * CHUNK)
            table = [(ent_codes[i // HALF_CHUNKS][:, within].bitcast(FP8X4), ent_scales[ENT_ROW:, cols])]
            nc.scalar.copy(entity[i, s][:], project("ent%d_%d" % (i, s), (("er", "ei")[s],), table, bank, i in TURNED))

        def both_entity_sums(i, bank):
            for s in range(2):
                entity_sum(i, s, bank + s)

        def relation(i):
            cols = slice(i * CHUNK, (i + 1) * CHUNK)
            within = slice(i % HALF_CHUNKS * 2 * CHUNK, (i % HALF_CHUNKS + 1) * 2 * CHUNK)
            return [
                (rel_codes[i // HALF_CHUNKS][:, a, within].bitcast(FP4X4), rel_scales[a].bitcast(U8)[:, cols])
                for a in range(2)
            ]

        def arr_sum(i):
            bank = EARLY_ARR_BANK.get(i, LATE_ARR_BANK)
            arr[i] = project("arr%d" % i, ("rr0", "rr1"), relation(i), bank, i in TURNED)

        def ari_sum(i):
            bank = ARI_BANKS[ARI_ORDER.index(i) % len(ARI_BANKS)]
            ari[i] = project("ari%d" % i, ("ri0", "ri1"), relation(i), bank, i in TURNED)

        def arr_products(i, parts=(0, 1)):
            for s in parts:
                nc.vector.tensor_tensor(arr_term(i, s), arr[i], entity[i, s][:], MULT)

        def ari_products(i, parts=(0, 1)):
            if 0 in parts:
                with_ari[i] = ring.tile([P, 2, CHUNK, PACK], F32, name="with_ari", bufs=5)
                nc.vector.scalar_tensor_tensor(with_ari[i][:, 0], ari[i], -1.0, entity[i, 1][:], MULT, MULT)
            if 1 in parts:
                nc.vector.tensor_tensor(with_ari[i][:, 1], ari[i], entity[i, 0][:], MULT)

        quantize_weight("ei")
        gather_entities(1)
        for s in range(2):
            for i in range(EARLY_CHUNKS):
                entity_sum(i, s, (EARLY_CHUNKS * s + i) % 4)
        gather_relations(0)
        gather_relations(1)
        part_relations(0)
        quantize_weight("rr0")
        quantize_weight("rr1")
        both_entity_sums(4, 2)
        part_relations(1)
        arr_sum(0)
        arr_sum(2)
        arr_sum(3)
        arr_sum(ON_GPSIMD)
        arr_products(0)
        both_entity_sums(3, 0)
        arr_products(2)
        arr_sum(WAITING)
        interleave("ri0")
        arr_copy = arena.tile([P, CHUNK, PACK], F32, name="arr_copy", offset=RAW_AT["rr1"] + 3 * QUARTER)
        nc.scalar.copy(arr_copy[:], arr[ON_GPSIMD])
        interleave("ri1")
        arr_products(3)
        arr_sum(5)
        quantize_grouped("ri0")
        quantize_grouped("ri1")
        arr_products(WAITING)
        for s in range(2):
            nc.gpsimd.tensor_tensor(arr_term(ON_GPSIMD, s), arr_copy[:], entity[ON_GPSIMD, s][:], MULT)

        groups = {
            (0, 1): RAW_AT["ri0"], (2,): RAW_AT["ri0"] + HALF_SLOT, (3,): RAW_AT["ri0"], (4,): GROUPED_AT["ei"],
            (5,): RAW_AT["ri0"], (6,): RAW_AT["rr0"] + HALF_SLOT, (7,): RAW_AT["rr0"] + HALF_SLOT,
        }
        held = {
            group: arena.tile([P, 2, len(group), WIDE], BF16, name="h%d" % group[0], offset=at, align_bytes=64)
            for group, at in groups.items()
        }
        h = {i: held[group][:, :, e, :] for group in groups for e, i in enumerate(group)}

        def quantize_h(parts, scales_at=None, joined=False):
            first = min(parts)[0]
            shape = [P, 2, sum(map(len, parts)) * CHUNK]
            h_codes = keep.tile(shape, U32, name="codes_h%d" % first, align_bytes=64)
            if scales_at is None:
                h_scales = keep.tile(shape, U8, name="scales_h%d" % first, align_bytes=64)
            else:
                h_scales = arena.tile(shape, U8, name="scales_h%d" % first, offset=scales_at, align_bytes=64)
            if joined:
                nc.vector.quantize_mx(
                    out=h_codes[:].rearrange("p s j -> p (s j)").bitcast(FP8X4),
                    scales=h_scales[:].rearrange("p s j -> p (s j)"),
                    in_=held[parts[0]][:].rearrange("p s i w -> p (s i w)"),
                )
            else:
                for group in parts:
                    cols = slice((group[0] - first) * CHUNK, (group[-1] - first + 1) * CHUNK)
                    for s in range(2):
                        nc.vector.quantize_mx(
                            out=h_codes[:, s, cols].bitcast(FP8X4), scales=h_scales[:, s, cols],
                            in_=held[group][:, s].rearrange("p i w -> p (i w)"),
                        )
            return [(h_codes[:, s], h_scales[:, s]) for s in range(2)]

        def score_pass(y, u, s, operand, start, stop):
            h_codes, h_scales = operand
            nc.tensor.matmul_mx(
                out=y,
                lhsT=cand[:, s, :].bitcast(U8)[:, 2 * u * P : 2 * (u + 1) * P].bitcast(FP4X4),
                lhsT_scale=cand_scales[:, s, :].bitcast(U8)[:, u * P : (u + 1) * P],
                rhs=h_codes.bitcast(FP8X4), rhs_scale=h_scales, start=start, stop=stop,
            )

        def score(first, tokens, operands, banks):
            blocks = N // P // len(banks)
            for b, bank in enumerate(banks):
                y = psum.tile([P, blocks, tokens], F32, name="y%d_%d" % (first, b), offset=bank * BANK_BYTES)
                for s in range(2):
                    for u in range(blocks):
                        score_pass(y[:, u, :], b * blocks + u, s, operands[s], s == 0 and u == 0, s == 1 and u == blocks - 1)
                result = keep.tile([P, blocks, tokens], F32, name="result%d_%d" % (first, b))
                nc.scalar.activation(result[:], y[:], SIGMOID)
                rows = slice(b * blocks * P, (b + 1) * blocks * P)
                cols = slice(first * CHUNK, first * CHUNK + tokens)
                nc.sync.dma_start(out[rows, cols].rearrange("(u p) j -> p u j", p=P), result[:])

        def turn(total, source, t, start, stop):
            columns = source.rearrange("p n t -> p (n t)")[:, t * P : (t + 1) * P]
            nc.tensor.matmul(total[:, t, :], columns, identity[:], start=start, stop=stop, is_transpose=True)

        totals = {}

        def turn_arr_terms(i, banks):
            totals[i] = [
                psum.tile([P, PACK, CHUNK], F32, name="total%d_%d" % (i, s), offset=banks[s] * BANK_BYTES) for s in range(2)
            ]
            for s in range(2):
                for t in range(PACK):
                    turn(totals[i][s], arr_term(i, s), t, t == 0, False)

        def add_turned(i):
            for s in range(2):
                for t in range(PACK):
                    turn(totals[i][s], with_ari[i][:, s], t, False, t == PACK - 1)
            for s, total in enumerate(totals[i]):
                nc.scalar.copy(h[i][:, s].rearrange("p (n t) -> p n t", t=PACK), total[:].rearrange("p t n -> p n t"))

        def flat(products):
            return products[:].rearrange("p s n t -> p s (n t)")

        def add_on_gpsimd(i):
            nc.gpsimd.tensor_tensor(h[i], flat(with_arr[i]), flat(with_ari[i]), ADD)

        ari_sum(0)
        ari_sum(2)
        ari_sum(1)
        entity_sum(5, 0, 2)
        arr_products(5, (0,))
        entity_sum(5, 1, 4)
        both_entity_sums(6, 0)
        both_entity_sums(7, 0)
        ari_products(0)
        add_on_gpsimd(0)
        ari_sum(3)
        ari_products(2)
        add_on_gpsimd(2)
        turn_arr_terms(1, (4, 2))
        ari_sum(4)
        ari_products(1)
        add_turned(1)
        ari_sum(5)
        ari_products(3)
        arr_products(5, (1,))
        arr_sum(6)
        ari_sum(6)
        turn_arr_terms(4, (0, 1))
        ari_products(4)
        add_turned(4)

        first_pair = quantize_h(((0, 1),), ent_at[4, 1], joined=True)
        add_on_gpsimd(3)
        ari_sum(7)
        score(0, PAIR, first_pair, (4, 2))
        ari_products(5)
        arr_products(6)
        arr_sum(7)
        turn_arr_terms(6, (0, 5))
        ari_products(6, (0,))

        single = quantize_h(((4,),), ent_at[5, 0], joined=True)
        second_pair = quantize_h(((2,), (3,)), ent_at[5, 0] + 2 * PAIR)
        add_on_gpsimd(5)
        ari_products(6, (1,))
        add_turned(6)
        score(2, PAIR, second_pair, (4, 2))
        score(4, CHUNK, single, (1,))
        arr_products(LAST)
        ari_products(LAST)

        score(5, PAIR, quantize_h(((6,), (5,)), ent_at[LAST, 1]), (4, 3))
        for s in range(2):
            nc.vector.tensor_tensor(h[LAST][:, s], flat(with_arr[LAST])[:, s], flat(with_ari[LAST])[:, s], ADD)
        score(LAST, CHUNK, quantize_h(((LAST,),)), (6, 1))
